import numpy as np
import ml_dtypes


def mxq(x, axis, fmt="e4m3"):
    dtype, down = {"e4m3": (ml_dtypes.float8_e4m3fn, 7), "e5m2": (ml_dtypes.float8_e5m2, 14)}[fmt]
    v = np.moveaxis(np.asarray(x, np.float32).astype(ml_dtypes.bfloat16).astype(np.float64), axis, -1)
    blocks = v.reshape(v.shape[:-1] + (-1, 32))
    amax = np.abs(blocks).max(-1, keepdims=True)
    byte = np.maximum(np.where(amax > 0, np.frexp(amax)[1] - 1 + 127, 0) - down, 1)
    scale = np.exp2(byte - 127.0)
    codes = (blocks / scale).astype(np.float32).astype(dtype).astype(np.float64)
    return np.moveaxis((codes * scale).reshape(v.shape), -1, axis)


WIDE = False


def mx_kscale(k):
    if not WIDE:
        return np.ones(k)
    levels = np.array([18, -18])
    if k % 512:
        return np.exp2(np.random.permutation(np.resize(levels, k // 32))).repeat(32)
    a = np.empty((k // 512, 16))
    for p in range(k // 512):
        a[p, :8] = np.random.permutation(np.resize(levels, 8))
        for g in range(8):
            far = levels[np.abs(levels - a[p, g]) >= 10]
            a[p, g + 8] = far[np.random.randint(len(far))]
    return np.exp2(a.ravel()).repeat(32)


def f64(x):
    return np.asarray(x).astype(np.float64)


def striped(idx):
    return np.tile(np.asarray(idx).reshape(-1, 16).T, (8, 1)).astype(np.uint16)


def unstriped(offs):
    return offs[:16].T.reshape(-1).astype(np.int64)


E2M1 = np.array([0.0, 0.5, 1.0, 1.5, 2.0, 3.0, 4.0, 6.0, -0.0, -0.5, -1.0, -1.5, -2.0, -3.0, -4.0, -6.0])


def pack_weight(w, fmt):
    k, n = w.shape
    w = f64(np.asarray(w, np.float32).astype(ml_dtypes.bfloat16)).reshape(k // 32, 32, n)
    amax = np.abs(w).max(1)
    if fmt == "e4m3":
        byte = np.frexp(amax)[1] - 1 + 127 - 7
    else:
        mant, ex = np.frexp(amax / 6.0)
        byte = np.where(mant > 0.5, ex, ex - 1) + 127
    byte = np.clip(np.where(amax > 0, byte, 1), 1, 254)
    scaled = (w * np.exp2(127.0 - byte)[:, None, :]).reshape(k, n).astype(np.float32)
    by_word = np.ascontiguousarray(scaled.reshape(k // 512, 128, 4, n).transpose(0, 1, 3, 2))
    if fmt == "e4m3":
        words = by_word.astype(ml_dtypes.float8_e4m3fn).view(np.uint8)
    else:
        c = by_word.astype(ml_dtypes.float4_e2m1fn).view(np.uint8) & 0xF
        words = (c[..., 0::2] | (c[..., 1::2] << 4)).reshape(k // 512, 128, 2 * n)
    return np.ascontiguousarray(words), np.ascontiguousarray(byte.astype(np.uint8).reshape(k // 512, 16, n))


def unpack_weight(words, scales, fmt):
    g, _, n = scales.shape
    words = np.ascontiguousarray(words).reshape(g, 128, n, -1)
    if fmt == "e4m3":
        vals = words.view(ml_dtypes.float8_e4m3fn).astype(np.float64)
    else:
        nib = np.empty((g, 128, n, 4), np.uint8)
        nib[..., 0::2] = words & 0xF
        nib[..., 1::2] = words >> 4
        vals = E2M1[nib]
    vals = vals * np.repeat(np.exp2(scales.astype(np.float64) - 127.0), 8, axis=1)[..., None]
    return vals.transpose(0, 1, 3, 2).reshape(g * 512, n)


B, N, T, D, DV, R = 2, 512, 2048, 512, 512, 512


def setup_inputs():
    n = np.random.standard_normal
    idx = np.random.permutation(T)[:B * N]
    s = mx_kscale(D)[:, None]
    z = mx_kscale(R)[:, None]
    v = mx_kscale(DV)[:, None]
    q = n((B, D, R))
    do = n((B, DV, R))
    kp = pack_weight(n((D, T)) * (1.00 / np.sqrt(D)) / s, "e4m3")
    vp = pack_weight(n((DV, T)) / np.sqrt(DV) / v, "e4m3")
    return {
        "qT": (q * s).astype(np.float32),
        "k_words": kp[0],
        "k_scales": kp[1],
        "v_words": vp[0],
        "v_scales": vp[1],
        "doT": (do * v).astype(np.float32),
        "rw": (np.random.uniform(0.5, 1.5, (B, R, 1)) * 1.0 / np.sqrt(R) * z).astype(np.float32),
        "qm": (q.transpose(0, 2, 1) / z).astype(np.float32),
        "offs": striped(idx),
    }


def reference(qT, k_words, k_scales, v_words, v_scales, doT, rw, qm, offs):
    idx = unstriped(offs)
    v = unpack_weight(v_words, v_scales, "e4m3")
    k = unpack_weight(k_words, k_scales, "e4m3")
    pick = lambda x: x[:, idx].reshape(x.shape[0], B, N).transpose(1, 0, 2)
    a = mxq(f64(qT), 1, "e4m3").transpose(0, 2, 1) @ pick(k)
    p = np.tanh(a)
    dp = mxq(f64(doT), 1, "e5m2").transpose(0, 2, 1) @ pick(v)
    ds = f64(rw) * dp * (1.0 - p * p)
    dk = mxq(f64(qm), 1, "e4m3").transpose(0, 2, 1) @ mxq(ds, 1, "e5m2")
    gk = np.zeros((D, T))
    gk[:, idx] = dk.transpose(1, 0, 2).reshape(D, B * N)
    return gk

@@ -1,0 +1,222 @@
+from contextlib import ExitStack
+
+import concourse.mybir as mybir
+
+B, N, T, D, R = 2, 512, 2048, 512, 512
+FLOPS = 3 * 2 * B * N * D * R
+
+F32 = mybir.dt.float32
+BF16 = mybir.dt.bfloat16
+I32 = mybir.dt.int32
+U32 = mybir.dt.uint32
+U16 = mybir.dt.uint16
+U8 = mybir.dt.uint8
+E4M3 = mybir.dt.float8_e4m3fn_x4
+E5M2 = mybir.dt.float8_e5m2_x4
+ACT = mybir.ActivationFunctionType
+ALU = mybir.AluOpType
+
+P = 128
+PACK = 4
+HALVES = 2
+HALF = N // HALVES
+LIST_COLS = N // 16
+
+
+def tile_attend_gat_tnh_k_kernel(
+    tc, qT, k_words, k_scales, v_words, v_scales, doT, rw, qm, offs, out
+):
+    nc = tc.nc
+    with ExitStack() as ctx:
+        keep = ctx.enter_context(tc.tile_pool(name="keep", bufs=1))
+        stage = ctx.enter_context(tc.tile_pool(name="stage", bufs=1))
+        work = ctx.enter_context(tc.tile_pool(name="work", bufs=2))
+        psum = ctx.enter_context(tc.psum_pool(name="psum", bufs=4))
+
+        offsets = keep.tile([P, B * LIST_COLS], U16, name="offsets")
+        nc.sync.dma_start(offsets[:], offs)
+
+        gate = keep.tile([P, B, PACK], F32, name="gate")
+        nc.sync.dma_start(gate[:], rw.rearrange("b (p t) o -> p b (t o)", t=PACK))
+        neg_gate = keep.tile([P, B, PACK], F32, name="neg_gate")
+        nc.scalar.activation(neg_gate[:], gate[:], ACT.Copy, scale=-1.0)
+
+        def load_rows(name, src, tag):
+            raw = stage.tile([P, PACK, src.shape[1]], F32, name=f"{name}_raw", tag=tag, align_bytes=64)
+            nc.sync.dma_start(raw[:], src.rearrange("(p j) w -> p j w", j=PACK))
+            return raw
+
+        def load_scales(name, src):
+            plane = stage.tile([P, T // 4], I32, name=f"{name}_pool_scales", tag=f"{name}_plane", align_bytes=64)
+            nc.vector.memset(plane[:], 0)
+            rows = src[0].bitcast(I32)
+            for f in range(4):
+                nc.sync.dma_start(plane[f:P:32, :], rows[f:16:4, :])
+            return plane
+
+        def load_words(name, src):
+            words = stage.tile([P, T], I32, name=f"{name}_pool_words", tag=f"{name}_pool", align_bytes=64)
+            nc.sync.dma_start(words[:], src[0].rearrange("p n j -> p (n j)").bitcast(I32))
+            return words
+
+        def zero_window(c, on_vector):
+            window = keep.tile([P, T], F32, name=f"window{c}")
+            if on_vector:
+                nc.vector.memset(window[:], 0.0)
+            else:
+                for x in range(0, T, 512):
+                    nc.gpsimd.memset(window[:, x : x + 512], 0.0)
+            return window
+
+        def quantize(name, grouped, fmt):
+            codes = work.tile([P, 512], U32, name=f"{name}_codes", align_bytes=64)
+            scales = work.tile([P, 512], U8, name=f"{name}_scales", align_bytes=64)
+            nc.vector.quantize_mx(out=codes[:].bitcast(fmt), scales=scales[:], in_=grouped[:])
+            return codes, scales
+
+        def listed(b):
+            return offsets[:, b * LIST_COLS : (b + 1) * LIST_COLS]
+
+        def gather_scales(name, plane, b, tag):
+            scales = stage.tile([P, N], U8, name=f"{name}_got_scales", tag=tag, align_bytes=64)
+            nc.vector.tensor_copy(scales[:], plane[:].bitcast(U8).indirect(listed(b)))
+            return scales
+
+        def gather_words(name, pool_words, b, tag):
+            words = stage.tile([P, N], U32, name=f"{name}_got_words", tag=tag, align_bytes=64)
+            nc.vector.tensor_copy(words[:], pool_words[:].bitcast(U32).indirect(listed(b)))
+            return words
+
+        def group_permuted(name, pieces, engine):
+            grouped = work.tile([P, PACK * 512], BF16, name=f"{name}_grouped", align_bytes=64)
+            dst = grouped[:].rearrange("p (t m j) -> p m j t", t=PACK, j=PACK)
+            step = P // len(pieces)
+            for x, piece in enumerate(pieces):
+                part = dst[:, x * step : (x + 1) * step]
+                src = piece.rearrange("p j (m t) -> p m j t", t=PACK)
+                if engine == "vector":
+                    nc.vector.tensor_copy(part, src)
+                elif engine == "scalar":
+                    nc.scalar.copy(part, src)
+                else:
+                    nc.gpsimd.tensor_scalar(
+                        part.rearrange("p m j t -> p m t j"), src.rearrange("p m j t -> p m t j"), 1.0, 0.0, ALU.mult, ALU.add
+                    )
+            return grouped
+
+        def group_plain(name, raw, engine):
+            grouped = work.tile([P, PACK * 512], BF16, name=f"{name}_grouped", align_bytes=64)
+            dst = grouped[:].rearrange("p (c i j) -> p c j i", i=4, j=PACK)
+            src = raw[:].rearrange("p j (c i) -> p c j i", i=4)
+            if engine == "vector":
+                nc.vector.tensor_copy(dst, src)
+            elif engine == "scalar":
+                nc.scalar.copy(dst, src)
+            else:
+                nc.gpsimd.tensor_scalar(
+                    grouped[:].rearrange("p (c j) -> p c j", j=PACK),
+                    raw[:].rearrange("p j c -> p c j"),
+                    1.0,
+                    0.0,
+                    ALU.mult,
+                    ALU.add,
+                )
+            return grouped
+
+        def product(bank, lhs, lhs_fmt, block, rhs, rhs_fmt):
+            cols = slice(block * P, (block + 1) * P)
+            nc.tensor.matmul_mx(
+                out=bank[:],
+                lhsT=lhs[0][:, cols].bitcast(lhs_fmt),
+                lhsT_scale=lhs[1][:, cols],
+                rhs=rhs[0][:].bitcast(rhs_fmt),
+                rhs_scale=rhs[1][:],
+                start=True,
+                stop=True,
+            )
+
+        def weights(b, q_mx, k_mx):
+            p = stage.tile([P, PACK, N], F32, name="p", tag=f"p{b}", align_bytes=64)
+            for t in range(PACK):
+                bank = psum.tile([P, N], F32, name="a_bank", tag="a", bufs=3)
+                product(bank, q_mx, E4M3, t, k_mx, E4M3)
+                nc.scalar.activation(p[:, t, :], bank[:], ACT.Tanh)
+            return p
+
+        def score_gradient(b, p, do_mx, v_mx):
+            dp_banks = []
+            for t in range(PACK):
+                bank = psum.tile([P, N], F32, name="dp_bank")
+                product(bank, do_mx, E5M2, t, v_mx, E4M3)
+                dp_banks.append(bank)
+            ds_codes = work.tile([P, N], U32, name="ds_codes", align_bytes=64)
+            ds_scales = work.tile([P, N], U8, name="ds_scales", align_bytes=64)
+            for h in range(HALVES):
+                cols = slice(h * HALF, (h + 1) * HALF)
+                nc.scalar.activation(p[:, :, cols], p[:, :, cols], ACT.Square)
+                dp = work.tile([P, PACK, HALF], F32, name=f"dp{h}")
+                for t in range(PACK):
+                    nc.scalar.activation(dp[:, t, :], dp_banks[t][:, cols], ACT.Copy, scale=neg_gate[:, b, t : t + 1])
+                ds = work.tile([P, HALF, PACK], BF16, name=f"ds{h}", align_bytes=64)
+                nc.vector.scalar_tensor_tensor(
+                    out=ds[:],
+                    in0=p[:, :, cols].rearrange("p t i -> p i t"),
+                    scalar=1.0,
+                    in1=dp[:].rearrange("p t i -> p i t"),
+                    op0=ALU.subtract,
+                    op1=ALU.mult,
+                )
+                nc.vector.quantize_mx(
+                    out=ds_codes[:, cols].bitcast(E5M2),
+                    scales=ds_scales[:, cols],
+                    in_=ds[:].rearrange("p i t -> p (i t)"),
+                )
+            return ds_codes, ds_scales
+
+        def key_gradient(b, c, qm_mx, ds_mx, staged=None):
+            bank = psum.tile([P, N], F32, name="dk_bank", tag="dk", bufs=1)
+            product(bank, qm_mx, E4M3, c, ds_mx, E5M2)
+            if staged is None:
+                staged = work.tile([P, N], F32, name=f"dk{c}")[:]
+            nc.scalar.copy(staged, bank[:])
+            nc.vector.tensor_copy(windows[c][:].indirect(listed(b)), staged)
+
+        q_raw = [load_rows("q", qT[0], "q0")[:]]
+        k_plane = load_scales("k", k_scales)
+        k_pool = load_words("k", k_words)
+        v_plane = load_scales("v", v_scales)
+        v_pool = load_words("v", v_words)
+        do_raw = load_rows("do", doT[0], "do")
+        qm_raw = load_rows("qm", qm[0], "qm")
+        windows = [zero_window(c, c < 4) for c in range(D // P)]
+
+        q_grouped = group_permuted("q", q_raw, "scalar")
+        k_got_scales = gather_scales("k", k_plane, 0, "s0")
+        q_mx = quantize("q", q_grouped, E4M3)
+        k_mx = gather_words("k", k_pool, 0, "w0"), k_got_scales
+        p = weights(0, q_mx, k_mx)
+        do_grouped = group_permuted("do", [do_raw[:]], "vector")
+        v_got_scales = gather_scales("v", v_plane, 0, "s1")
+        do_mx = quantize("do", do_grouped, E5M2)
+        v_mx = gather_words("v", v_pool, 0, "w1"), v_got_scales
+        ds_first = score_gradient(0, p, do_mx, v_mx)
+        qm_first = quantize("qm", group_plain("qm", qm_raw, "scalar"), E4M3)
+
+        k_mx = gather_words("k", k_pool, 1, "do"), gather_scales("k", k_plane, 1, "k_pool")
+        v_mx = gather_words("v", v_pool, 1, "qm"), gather_scales("v", v_plane, 1, "k_plane")
+        q_raw = load_rows("q", qT[1], "q1n")
+        do_raw = load_rows("do", doT[1], "do1n")
+        qm_raw = load_rows("qm", qm[1], "qm1n")
+
+        key_gradient(0, 0, qm_first, ds_first)
+        q_mx = quantize("q", group_permuted("q", [q_raw[:, :, :256], q_raw[:, :, 256:]], "scalar"), E4M3)
+        do_mx = quantize("do", group_permuted("do", [do_raw[:]], "scalar"), E5M2)
+        key_gradient(0, 1, qm_first, ds_first, staged=do_raw[:, 0, :])
+        p = weights(1, q_mx, k_mx)
+        key_gradient(0, 2, qm_first, ds_first, staged=do_raw[:, 1, :])
+        ds_second = score_gradient(1, p, do_mx, v_mx)
+        qm_second = quantize("qm", group_plain("qm", qm_raw, "scalar"), E4M3)
+        key_gradient(0, 3, qm_first, ds_first, staged=p[:, 0, :])
+        for c in range(D // P):
+            key_gradient(1, c, qm_second, ds_second)
+            nc.sync.dma_start(out[c * P : (c + 1) * P, :], windows[c][:])

@@ -36,10 +36,15 @@ def tile_attend_gat_tnh_k_kernel(
         offsets = keep.tile([P, B * LIST_COLS], U16, name="offsets")
         nc.sync.dma_start(offsets[:], offs)
 
-        gate = keep.tile([P, B, PACK], F32, name="gate")
-        nc.sync.dma_start(gate[:], rw.rearrange("b (p t) o -> p b (t o)", t=PACK))
-        neg_gate = keep.tile([P, B, PACK], F32, name="neg_gate")
-        nc.scalar.activation(neg_gate[:], gate[:], ACT.Copy, scale=-1.0)
+        neg_gates = []
+        for b in range(B):
+            gate = stage.tile([P, PACK], F32, name="gate", tag=f"g{b}", align_bytes=64)
+            nc.sync.dma_start(gate[:], rw[b].rearrange("(p t) o -> p (t o)", t=PACK))
+            neg_gate = stage.tile([P, PACK], F32, name="neg_gate", tag=f"ng{b}", align_bytes=64)
+            nc.scalar.activation(neg_gate[:], gate[:], ACT.Copy, scale=-1.0)
+            neg_gates.append(neg_gate)
+
+        tags = ["qg0","dog0","qmg0","qg1","ds0","qmg1"]
 
         def load_rows(name, src, tag):
             raw = stage.tile([P, PACK, src.shape[1]], F32, name=f"{name}_raw", tag=tag, align_bytes=64)
@@ -48,7 +53,7 @@ def tile_attend_gat_tnh_k_kernel(
 
         def load_scales(name, src):
             plane = stage.tile([P, T // 4], I32, name=f"{name}_pool_scales", tag=f"{name}_plane", align_bytes=64)
-            nc.vector.memset(plane[:], 0)
+            (nc.gpsimd if name in "-" else nc.vector).memset(plane[:], 0)
             rows = src[0].bitcast(I32)
             for f in range(4):
                 nc.sync.dma_start(plane[f:P:32, :], rows[f:16:4, :])
@@ -59,8 +64,8 @@ def tile_attend_gat_tnh_k_kernel(
             nc.sync.dma_start(words[:], src[0].rearrange("p n j -> p (n j)").bitcast(I32))
             return words
 
-        def zero_window(c, on_vector):
-            window = keep.tile([P, T], F32, name=f"window{c}")
+        def zero_window(c, on_vector, tag):
+            window = stage.tile([P, T], F32, name=f"window{c}", tag=tag, align_bytes=64)
             if on_vector:
                 nc.vector.memset(window[:], 0.0)
             else:
@@ -88,7 +93,7 @@ def tile_attend_gat_tnh_k_kernel(
             return words
 
         def group_permuted(name, pieces, engine):
-            grouped = work.tile([P, PACK * 512], BF16, name=f"{name}_grouped", align_bytes=64)
+            grouped = stage.tile([P, PACK * 512], BF16, name=f"{name}_grouped", tag=tags.pop(0), align_bytes=64)
             dst = grouped[:].rearrange("p (t m j) -> p m j t", t=PACK, j=PACK)
             step = P // len(pieces)
             for x, piece in enumerate(pieces):
@@ -105,7 +110,7 @@ def tile_attend_gat_tnh_k_kernel(
             return grouped
 
         def group_plain(name, raw, engine):
-            grouped = work.tile([P, PACK * 512], BF16, name=f"{name}_grouped", align_bytes=64)
+            grouped = stage.tile([P, PACK * 512], BF16, name=f"{name}_grouped", tag=tags.pop(0), align_bytes=64)
             dst = grouped[:].rearrange("p (c i j) -> p c j i", i=4, j=PACK)
             src = raw[:].rearrange("p j (c i) -> p c j i", i=4)
             if engine == "vector":
@@ -149,28 +154,26 @@ def tile_attend_gat_tnh_k_kernel(
                 bank = psum.tile([P, N], F32, name="dp_bank")
                 product(bank, do_mx, E5M2, t, v_mx, E4M3)
                 dp_banks.append(bank)
+            nc.scalar.activation(p[:], p[:], ACT.Square)
             ds_codes = work.tile([P, N], U32, name="ds_codes", align_bytes=64)
             ds_scales = work.tile([P, N], U8, name="ds_scales", align_bytes=64)
+            ds = stage.tile([P, N, PACK], BF16, name="ds", tag=f"ds{b}", align_bytes=64)
             for h in range(HALVES):
                 cols = slice(h * HALF, (h + 1) * HALF)
-                nc.scalar.activation(p[:, :, cols], p[:, :, cols], ACT.Square)
                 dp = work.tile([P, PACK, HALF], F32, name=f"dp{h}")
                 for t in range(PACK):
-                    nc.scalar.activation(dp[:, t, :], dp_banks[t][:, cols], ACT.Copy, scale=neg_gate[:, b, t : t + 1])
-                ds = work.tile([P, HALF, PACK], BF16, name=f"ds{h}", align_bytes=64)
+                    nc.scalar.activation(dp[:, t, :], dp_banks[t][:, cols], ACT.Copy, scale=neg_gates[b][:, t : t + 1])
                 nc.vector.scalar_tensor_tensor(
-                    out=ds[:],
+                    out=ds[:, cols, :],
                     in0=p[:, :, cols].rearrange("p t i -> p i t"),
                     scalar=1.0,
                     in1=dp[:].rearrange("p t i -> p i t"),
                     op0=ALU.subtract,
                     op1=ALU.mult,
                 )
-                nc.vector.quantize_mx(
-                    out=ds_codes[:, cols].bitcast(E5M2),
-                    scales=ds_scales[:, cols],
-                    in_=ds[:].rearrange("p i t -> p (i t)"),
-                )
+            nc.vector.quantize_mx(
+                out=ds_codes[:].bitcast(E5M2), scales=ds_scales[:], in_=ds[:].rearrange("p i t -> p (i t)")
+            )
             return ds_codes, ds_scales
 
         def key_gradient(b, c, qm_mx, ds_mx, staged=None):
@@ -181,16 +184,16 @@ def tile_attend_gat_tnh_k_kernel(
             nc.scalar.copy(staged, bank[:])
             nc.vector.tensor_copy(windows[c][:].indirect(listed(b)), staged)
 
-        q_raw = [load_rows("q", qT[0], "q0")[:]]
         k_plane = load_scales("k", k_scales)
-        k_pool = load_words("k", k_words)
+        q_raw = load_rows("q", qT[0], "q0")
         v_plane = load_scales("v", v_scales)
-        v_pool = load_words("v", v_words)
+        k_pool = load_words("k", k_words)
         do_raw = load_rows("do", doT[0], "do")
+        v_pool = load_words("v", v_words)
         qm_raw = load_rows("qm", qm[0], "qm")
-        windows = [zero_window(c, c < 4) for c in range(D // P)]
+        windows = [zero_window(c, True, f"win{c}") for c in range(2)]
 
-        q_grouped = group_permuted("q", q_raw, "scalar")
+        q_grouped = group_permuted("q", [q_raw[:]], "scalar")
         k_got_scales = gather_scales("k", k_plane, 0, "s0")
         q_mx = quantize("q", q_grouped, E4M3)
         k_mx = gather_words("k", k_pool, 0, "w0"), k_got_scales
@@ -199,18 +202,19 @@ def tile_attend_gat_tnh_k_kernel(
         v_got_scales = gather_scales("v", v_plane, 0, "s1")
         do_mx = quantize("do", do_grouped, E5M2)
         v_mx = gather_words("v", v_pool, 0, "w1"), v_got_scales
+        qm_first = quantize("qm", group_plain("qm", qm_raw, "vector"), E4M3)
         ds_first = score_gradient(0, p, do_mx, v_mx)
-        qm_first = quantize("qm", group_plain("qm", qm_raw, "scalar"), E4M3)
 
-        k_mx = gather_words("k", k_pool, 1, "do"), gather_scales("k", k_plane, 1, "k_pool")
-        v_mx = gather_words("v", v_pool, 1, "qm"), gather_scales("v", v_plane, 1, "k_plane")
+        k_mx = gather_words("k", k_pool, 1, "dog0"), gather_scales("k", k_plane, 1, "x2")
+        v_mx = gather_words("v", v_pool, 1, "p0"), gather_scales("v", v_plane, 1, "x4")
         q_raw = load_rows("q", qT[1], "q1n")
         do_raw = load_rows("do", doT[1], "do1n")
         qm_raw = load_rows("qm", qm[1], "qm1n")
 
         key_gradient(0, 0, qm_first, ds_first)
         q_mx = quantize("q", group_permuted("q", [q_raw[:, :, :256], q_raw[:, :, 256:]], "scalar"), E4M3)
-        do_mx = quantize("do", group_permuted("do", [do_raw[:]], "scalar"), E5M2)
+        do_mx = quantize("do", group_permuted("do", [do_raw[:, :, :256], do_raw[:, :, 256:]], "scalar"), E5M2)
+        windows += [zero_window(2, False, "qg1"), zero_window(3, False, "ds0")]
         key_gradient(0, 1, qm_first, ds_first, staged=do_raw[:, 0, :])
         p = weights(1, q_mx, k_mx)
         key_gradient(0, 2, qm_first, ds_first, staged=do_raw[:, 1, :])

@@ -41,10 +41,12 @@ def tile_attend_gat_tnh_k_kernel(
             gate = stage.tile([P, PACK], F32, name="gate", tag=f"g{b}", align_bytes=64)
             nc.sync.dma_start(gate[:], rw[b].rearrange("(p t) o -> p (t o)", t=PACK))
             neg_gate = stage.tile([P, PACK], F32, name="neg_gate", tag=f"ng{b}", align_bytes=64)
-            nc.scalar.activation(neg_gate[:], gate[:], ACT.Copy, scale=-1.0)
+            nc.scalar.activation(neg_gate[:], gate[:], ACT.Copy, scale=1.0 if b in [] else -1.0)
             neg_gates.append(neg_gate)
 
-        tags = ["qg0","dog0","qmg0","qg1","ds0","qmg1"]
+        tags = ["qg0","dog0","qmg0","qg1","qmg0","qmg1"]
+
+        code_tags = ["v_plane","k_pool","qmc0","dp01","doc1","qmc1"]
 
         def load_rows(name, src, tag):
             raw = stage.tile([P, PACK, src.shape[1]], F32, name=f"{name}_raw", tag=tag, align_bytes=64)
@@ -74,7 +76,7 @@ def tile_attend_gat_tnh_k_kernel(
             return window
 
         def quantize(name, grouped, fmt):
-            codes = work.tile([P, 512], U32, name=f"{name}_codes", align_bytes=64)
+            codes = stage.tile([P, 512], U32, name=f"{name}_codes", tag=code_tags.pop(0), align_bytes=64)
             scales = work.tile([P, 512], U8, name=f"{name}_scales", align_bytes=64)
             nc.vector.quantize_mx(out=codes[:].bitcast(fmt), scales=scales[:], in_=grouped[:])
             return codes, scales
@@ -105,7 +107,7 @@ def tile_attend_gat_tnh_k_kernel(
                     nc.scalar.copy(part, src)
                 else:
                     nc.gpsimd.tensor_scalar(
-                        part.rearrange("p m j t -> p m t j"), src.rearrange("p m j t -> p m t j"), 1.0, 0.0, ALU.mult, ALU.add
+                        part.rearrange("p m j t -> p t m j"), src.rearrange("p m j t -> p t m j"), 1.0, 0.0, ALU.mult, ALU.add
                     )
             return grouped
 
@@ -114,7 +116,7 @@ def tile_attend_gat_tnh_k_kernel(
             dst = grouped[:].rearrange("p (c i j) -> p c j i", i=4, j=PACK)
             src = raw[:].rearrange("p j (c i) -> p c j i", i=4)
             if engine == "vector":
-                nc.vector.tensor_copy(dst, src)
+                nc.vector.tensor_copy(grouped[:].rearrange("p (c j) -> p c j", j=PACK), raw[:].rearrange("p j c -> p c j"))
             elif engine == "scalar":
                 nc.scalar.copy(dst, src)
             else:
@@ -155,22 +157,32 @@ def tile_attend_gat_tnh_k_kernel(
                 product(bank, do_mx, E5M2, t, v_mx, E4M3)
                 dp_banks.append(bank)
             nc.scalar.activation(p[:], p[:], ACT.Square)
+            if b in []:
+                nc.scalar.activation(p[:], p[:], ACT.Copy, scale=-1.0, bias=1.0)
             ds_codes = work.tile([P, N], U32, name="ds_codes", align_bytes=64)
             ds_scales = work.tile([P, N], U8, name="ds_scales", align_bytes=64)
-            ds = stage.tile([P, N, PACK], BF16, name="ds", tag=f"ds{b}", align_bytes=64)
+            ds = stage.tile([P, N, PACK], BF16, name="ds", tag=("qm", "ds1")[b], align_bytes=64)
             for h in range(HALVES):
                 cols = slice(h * HALF, (h + 1) * HALF)
-                dp = work.tile([P, PACK, HALF], F32, name=f"dp{h}")
+                dp = stage.tile([P, PACK, HALF], F32, name=f"dp{h}", tag=f"dp{b}{h}", align_bytes=64)
                 for t in range(PACK):
                     nc.scalar.activation(dp[:, t, :], dp_banks[t][:, cols], ACT.Copy, scale=neg_gates[b][:, t : t + 1])
-                nc.vector.scalar_tensor_tensor(
-                    out=ds[:, cols, :],
-                    in0=p[:, :, cols].rearrange("p t i -> p i t"),
-                    scalar=1.0,
-                    in1=dp[:].rearrange("p t i -> p i t"),
-                    op0=ALU.subtract,
-                    op1=ALU.mult,
-                )
+                if b in []:
+                    nc.vector.tensor_tensor(
+                        ds[:, cols, :].rearrange("p (c i) t -> p c t i", i=4),
+                        p[:, :, cols].rearrange("p t (c i) -> p c t i", i=4),
+                        dp[:].rearrange("p t (c i) -> p c t i", i=4),
+                        ALU.mult,
+                    )
+                else:
+                    nc.vector.scalar_tensor_tensor(
+                        out=ds[:, cols, :],
+                        in0=p[:, :, cols].rearrange("p t i -> p i t"),
+                        scalar=1.0,
+                        in1=dp[:].rearrange("p t i -> p i t"),
+                        op0=ALU.subtract,
+                        op1=ALU.mult,
+                    )
             nc.vector.quantize_mx(
                 out=ds_codes[:].bitcast(E5M2), scales=ds_scales[:], in_=ds[:].rearrange("p i t -> p (i t)")
             )
@@ -187,8 +199,8 @@ def tile_attend_gat_tnh_k_kernel(
         k_plane = load_scales("k", k_scales)
         q_raw = load_rows("q", qT[0], "q0")
         v_plane = load_scales("v", v_scales)
-        k_pool = load_words("k", k_words)
         do_raw = load_rows("do", doT[0], "do")
+        k_pool = load_words("k", k_words)
         v_pool = load_words("v", v_words)
         qm_raw = load_rows("qm", qm[0], "qm")
         windows = [zero_window(c, True, f"win{c}") for c in range(2)]
@@ -198,14 +210,14 @@ def tile_attend_gat_tnh_k_kernel(
         q_mx = quantize("q", q_grouped, E4M3)
         k_mx = gather_words("k", k_pool, 0, "w0"), k_got_scales
         p = weights(0, q_mx, k_mx)
-        do_grouped = group_permuted("do", [do_raw[:]], "vector")
+        do_grouped = group_permuted("do", [do_raw[:]], "scalar")
         v_got_scales = gather_scales("v", v_plane, 0, "s1")
         do_mx = quantize("do", do_grouped, E5M2)
         v_mx = gather_words("v", v_pool, 0, "w1"), v_got_scales
         qm_first = quantize("qm", group_plain("qm", qm_raw, "vector"), E4M3)
         ds_first = score_gradient(0, p, do_mx, v_mx)
 
-        k_mx = gather_words("k", k_pool, 1, "dog0"), gather_scales("k", k_plane, 1, "x2")
+        k_mx = gather_words("k", k_pool, 1, "x1"), gather_scales("k", k_plane, 1, "x2")
         v_mx = gather_words("v", v_pool, 1, "p0"), gather_scales("v", v_plane, 1, "x4")
         q_raw = load_rows("q", qT[1], "q1n")
         do_raw = load_rows("do", doT[1], "do1n")
@@ -213,8 +225,8 @@ def tile_attend_gat_tnh_k_kernel(
 
         key_gradient(0, 0, qm_first, ds_first)
         q_mx = quantize("q", group_permuted("q", [q_raw[:, :, :256], q_raw[:, :, 256:]], "scalar"), E4M3)
-        do_mx = quantize("do", group_permuted("do", [do_raw[:, :, :256], do_raw[:, :, 256:]], "scalar"), E5M2)
-        windows += [zero_window(2, False, "qg1"), zero_window(3, False, "ds0")]
+        do_mx = quantize("do", group_permuted("do", [do_raw[:, :, x : x + 128] for x in range(0, 512, 128)], "scalar"), E5M2)
+        windows += [zero_window(2, False, "k_plane"), zero_window(3, False, "qg1")]
         key_gradient(0, 1, qm_first, ds_first, staged=do_raw[:, 0, :])
         p = weights(1, q_mx, k_mx)
         key_gradient(0, 2, qm_first, ds_first, staged=do_raw[:, 1, :])

@@ -18,8 +18,6 @@ ALU = mybir.AluOpType
 
 P = 128
 PACK = 4
-HALVES = 2
-HALF = N // HALVES
 LIST_COLS = N // 16
 
 
@@ -29,45 +27,32 @@ def tile_attend_gat_tnh_k_kernel(
     nc = tc.nc
     with ExitStack() as ctx:
         keep = ctx.enter_context(tc.tile_pool(name="keep", bufs=1))
-        stage = ctx.enter_context(tc.tile_pool(name="stage", bufs=1))
-        work = ctx.enter_context(tc.tile_pool(name="work", bufs=2))
-        psum = ctx.enter_context(tc.psum_pool(name="psum", bufs=4))
+        sb = ctx.enter_context(tc.tile_pool(name="sb", bufs=1))
+        psum = ctx.enter_context(tc.psum_pool(name="psum", bufs=1))
 
-        offsets = keep.tile([P, B * LIST_COLS], U16, name="offsets")
-        nc.sync.dma_start(offsets[:], offs)
+        def tile(shape, dtype, tag):
+            return sb.tile(shape, dtype, name=tag, tag=tag, align_bytes=64)
 
-        neg_gates = []
-        for b in range(B):
-            gate = stage.tile([P, PACK], F32, name="gate", tag=f"g{b}", align_bytes=64)
-            nc.sync.dma_start(gate[:], rw[b].rearrange("(p t) o -> p (t o)", t=PACK))
-            neg_gate = stage.tile([P, PACK], F32, name="neg_gate", tag=f"ng{b}", align_bytes=64)
-            nc.scalar.activation(neg_gate[:], gate[:], ACT.Copy, scale=1.0 if b in [] else -1.0)
-            neg_gates.append(neg_gate)
-
-        tags = ["qg0","dog0","qmg0","qg1","qmg0","qmg1"]
-
-        code_tags = ["v_plane","k_pool","qmc0","dp01","doc1","qmc1"]
-
-        def load_rows(name, src, tag):
-            raw = stage.tile([P, PACK, src.shape[1]], F32, name=f"{name}_raw", tag=tag, align_bytes=64)
+        def load_rows(src, tag):
+            raw = tile([P, PACK, src.shape[1]], F32, tag)
             nc.sync.dma_start(raw[:], src.rearrange("(p j) w -> p j w", j=PACK))
             return raw
 
-        def load_scales(name, src):
-            plane = stage.tile([P, T // 4], I32, name=f"{name}_pool_scales", tag=f"{name}_plane", align_bytes=64)
-            (nc.gpsimd if name in "-" else nc.vector).memset(plane[:], 0)
+        def load_scales(src, tag):
+            plane = tile([P, T // 4], I32, tag)
+            nc.vector.memset(plane[:], 0)
             rows = src[0].bitcast(I32)
             for f in range(4):
                 nc.sync.dma_start(plane[f:P:32, :], rows[f:16:4, :])
             return plane
 
-        def load_words(name, src):
-            words = stage.tile([P, T], I32, name=f"{name}_pool_words", tag=f"{name}_pool", align_bytes=64)
+        def load_words(src, tag):
+            words = tile([P, T], I32, tag)
             nc.sync.dma_start(words[:], src[0].rearrange("p n j -> p (n j)").bitcast(I32))
             return words
 
-        def zero_window(c, on_vector, tag):
-            window = stage.tile([P, T], F32, name=f"window{c}", tag=tag, align_bytes=64)
+        def zero_window(tag, on_vector):
+            window = tile([P, T], F32, tag)
             if on_vector:
                 nc.vector.memset(window[:], 0.0)
             else:
@@ -76,59 +61,33 @@ def tile_attend_gat_tnh_k_kernel(
             return window
 
         def quantize(name, grouped, fmt):
-            codes = stage.tile([P, 512], U32, name=f"{name}_codes", tag=code_tags.pop(0), align_bytes=64)
-            scales = work.tile([P, 512], U8, name=f"{name}_scales", align_bytes=64)
-            nc.vector.quantize_mx(out=codes[:].bitcast(fmt), scales=scales[:], in_=grouped[:])
+            words = grouped.shape[1] // PACK
+            codes = tile([P, words], U32, f"{name}_codes")
+            scales = tile([P, words], U8, f"{name}_scales")
+            nc.vector.quantize_mx(out=codes[:].bitcast(fmt), scales=scales[:], in_=grouped)
             return codes, scales
 
         def listed(b):
             return offsets[:, b * LIST_COLS : (b + 1) * LIST_COLS]
 
-        def gather_scales(name, plane, b, tag):
-            scales = stage.tile([P, N], U8, name=f"{name}_got_scales", tag=tag, align_bytes=64)
-            nc.vector.tensor_copy(scales[:], plane[:].bitcast(U8).indirect(listed(b)))
-            return scales
+        def gather(pool_tile, dtype, b, tag):
+            got = tile([P, N], dtype, tag)
+            nc.vector.tensor_copy(got[:], pool_tile[:].bitcast(dtype).indirect(listed(b)))
+            return got
 
-        def gather_words(name, pool_words, b, tag):
-            words = stage.tile([P, N], U32, name=f"{name}_got_words", tag=tag, align_bytes=64)
-            nc.vector.tensor_copy(words[:], pool_words[:].bitcast(U32).indirect(listed(b)))
-            return words
-
-        def group_permuted(name, pieces, engine):
-            grouped = stage.tile([P, PACK * 512], BF16, name=f"{name}_grouped", tag=tags.pop(0), align_bytes=64)
-            dst = grouped[:].rearrange("p (t m j) -> p m j t", t=PACK, j=PACK)
-            step = P // len(pieces)
-            for x, piece in enumerate(pieces):
-                part = dst[:, x * step : (x + 1) * step]
-                src = piece.rearrange("p j (m t) -> p m j t", t=PACK)
-                if engine == "vector":
-                    nc.vector.tensor_copy(part, src)
-                elif engine == "scalar":
-                    nc.scalar.copy(part, src)
-                else:
-                    nc.gpsimd.tensor_scalar(
-                        part.rearrange("p m j t -> p t m j"), src.rearrange("p m j t -> p t m j"), 1.0, 0.0, ALU.mult, ALU.add
-                    )
-            return grouped
-
-        def group_plain(name, raw, engine):
-            grouped = stage.tile([P, PACK * 512], BF16, name=f"{name}_grouped", tag=tags.pop(0), align_bytes=64)
-            dst = grouped[:].rearrange("p (c i j) -> p c j i", i=4, j=PACK)
-            src = raw[:].rearrange("p j (c i) -> p c j i", i=4)
+        def deal(grouped, piece, x0, engine):
+            width = piece.shape[2]
+            dst = grouped[:].rearrange("p (t m j) -> p m j t", t=PACK, j=PACK)[:, x0 // PACK : (x0 + width) // PACK]
+            src = piece.rearrange("p j (m t) -> p m j t", t=PACK)
             if engine == "vector":
-                nc.vector.tensor_copy(grouped[:].rearrange("p (c j) -> p c j", j=PACK), raw[:].rearrange("p j c -> p c j"))
-            elif engine == "scalar":
-                nc.scalar.copy(dst, src)
+                nc.vector.tensor_copy(dst, src)
             else:
-                nc.gpsimd.tensor_scalar(
-                    grouped[:].rearrange("p (c j) -> p c j", j=PACK),
-                    raw[:].rearrange("p j c -> p c j"),
-                    1.0,
-                    0.0,
-                    ALU.mult,
-                    ALU.add,
-                )
-            return grouped
+                nc.scalar.copy(dst, src)
+
+        def interleave(grouped, piece, x0):
+            width = piece.shape[2]
+            dst = grouped[:, PACK * x0 : PACK * (x0 + width)].rearrange("p (c i j) -> p c j i", i=4, j=PACK)
+            nc.scalar.copy(dst, piece.rearrange("p j (c i) -> p c j i", i=4))
 
         def product(bank, lhs, lhs_fmt, block, rhs, rhs_fmt):
             cols = slice(block * P, (block + 1) * P)
@@ -143,96 +102,114 @@ def tile_attend_gat_tnh_k_kernel(
             )
 
         def weights(b, q_mx, k_mx):
-            p = stage.tile([P, PACK, N], F32, name="p", tag=f"p{b}", align_bytes=64)
+            p = tile([P, PACK, N], F32, f"p{b}")
             for t in range(PACK):
-                bank = psum.tile([P, N], F32, name="a_bank", tag="a", bufs=3)
+                bank = psum.tile([P, N], F32, name="a_bank", tag="a", bufs=4)
                 product(bank, q_mx, E4M3, t, k_mx, E4M3)
                 nc.scalar.activation(p[:, t, :], bank[:], ACT.Tanh)
             return p
 
-        def score_gradient(b, p, do_mx, v_mx):
-            dp_banks = []
+        def value_products(do_mx, v_mx):
+            banks = []
             for t in range(PACK):
-                bank = psum.tile([P, N], F32, name="dp_bank")
+                bank = psum.tile([P, N], F32, name="dp_bank", tag="dp", bufs=4)
                 product(bank, do_mx, E5M2, t, v_mx, E4M3)
-                dp_banks.append(bank)
-            nc.scalar.activation(p[:], p[:], ACT.Square)
-            if b in []:
-                nc.scalar.activation(p[:], p[:], ACT.Copy, scale=-1.0, bias=1.0)
-            ds_codes = work.tile([P, N], U32, name="ds_codes", align_bytes=64)
-            ds_scales = work.tile([P, N], U8, name="ds_scales", align_bytes=64)
-            ds = stage.tile([P, N, PACK], BF16, name="ds", tag=("qm", "ds1")[b], align_bytes=64)
-            for h in range(HALVES):
-                cols = slice(h * HALF, (h + 1) * HALF)
-                dp = stage.tile([P, PACK, HALF], F32, name=f"dp{h}", tag=f"dp{b}{h}", align_bytes=64)
-                for t in range(PACK):
-                    nc.scalar.activation(dp[:, t, :], dp_banks[t][:, cols], ACT.Copy, scale=neg_gates[b][:, t : t + 1])
-                if b in []:
-                    nc.vector.tensor_tensor(
-                        ds[:, cols, :].rearrange("p (c i) t -> p c t i", i=4),
-                        p[:, :, cols].rearrange("p t (c i) -> p c t i", i=4),
-                        dp[:].rearrange("p t (c i) -> p c t i", i=4),
-                        ALU.mult,
-                    )
-                else:
-                    nc.vector.scalar_tensor_tensor(
-                        out=ds[:, cols, :],
-                        in0=p[:, :, cols].rearrange("p t i -> p i t"),
-                        scalar=1.0,
-                        in1=dp[:].rearrange("p t i -> p i t"),
-                        op0=ALU.subtract,
-                        op1=ALU.mult,
-                    )
-            nc.vector.quantize_mx(
-                out=ds_codes[:].bitcast(E5M2), scales=ds_scales[:], in_=ds[:].rearrange("p i t -> p (i t)")
+                banks.append(bank)
+            return banks
+
+        def gated(b, dp_banks, cols, tag):
+            width = cols.stop - cols.start
+            x = tile([P, PACK, width], F32, tag)
+            for t in range(PACK):
+                nc.scalar.activation(x[:, t, :], dp_banks[t][:, cols], ACT.Copy, scale=gates[:, b, t : t + 1])
+            return x
+
+        def minus_ds(ds, p, x, cols):
+            nc.vector.scalar_tensor_tensor(
+                out=ds[:, cols, :],
+                in0=p[:, :, cols].rearrange("p t i -> p i t"),
+                scalar=1.0,
+                in1=x[:].rearrange("p t i -> p i t"),
+                op0=ALU.subtract,
+                op1=ALU.mult,
             )
-            return ds_codes, ds_scales
 
-        def key_gradient(b, c, qm_mx, ds_mx, staged=None):
-            bank = psum.tile([P, N], F32, name="dk_bank", tag="dk", bufs=1)
-            product(bank, qm_mx, E4M3, c, ds_mx, E5M2)
-            if staged is None:
-                staged = work.tile([P, N], F32, name=f"dk{c}")[:]
-            nc.scalar.copy(staged, bank[:])
-            nc.vector.tensor_copy(windows[c][:].indirect(listed(b)), staged)
+        def key_gradient(b, c, qm_mx, block, ds_mx, tag=None):
+            bank = psum.tile([P, N], F32, name="dk_bank", tag="a", bufs=4)
+            product(bank, qm_mx, E4M3, block, ds_mx, E5M2)
+            staged = tile([P, N], F32, tag or f"dk{b}{c}")
+            nc.scalar.activation(staged[:], bank[:], ACT.Copy, scale=-1.0)
+            nc.vector.tensor_copy(windows[c][:].indirect(listed(b)), staged[:])
 
-        k_plane = load_scales("k", k_scales)
-        q_raw = load_rows("q", qT[0], "q0")
-        v_plane = load_scales("v", v_scales)
-        do_raw = load_rows("do", doT[0], "do")
-        k_pool = load_words("k", k_words)
-        v_pool = load_words("v", v_words)
-        qm_raw = load_rows("qm", qm[0], "qm")
-        windows = [zero_window(c, True, f"win{c}") for c in range(2)]
+        offsets = keep.tile([P, B * LIST_COLS], U16, name="offsets")
+        nc.sync.dma_start(offsets[:], offs)
 
-        q_grouped = group_permuted("q", [q_raw[:]], "scalar")
-        k_got_scales = gather_scales("k", k_plane, 0, "s0")
-        q_mx = quantize("q", q_grouped, E4M3)
-        k_mx = gather_words("k", k_pool, 0, "w0"), k_got_scales
-        p = weights(0, q_mx, k_mx)
-        do_grouped = group_permuted("do", [do_raw[:]], "scalar")
-        v_got_scales = gather_scales("v", v_plane, 0, "s1")
-        do_mx = quantize("do", do_grouped, E5M2)
-        v_mx = gather_words("v", v_pool, 0, "w1"), v_got_scales
-        qm_first = quantize("qm", group_plain("qm", qm_raw, "vector"), E4M3)
-        ds_first = score_gradient(0, p, do_mx, v_mx)
+        q_halves = [load_rows(qT[0][:, x : x + 256], f"q0_{x}") for x in (0, 256)]
+        k_plane = load_scales(k_scales, "k_plane")
+        k_pool = load_words(k_words, "k_pool")
+        gates = tile([P, B, PACK], F32, "gates")
+        nc.sync.dma_start(gates[:], rw.rearrange("b (p t) o -> p b (t o)", t=PACK))
+        v_plane = load_scales(v_scales, "v_plane")
+        do_halves = [load_rows(doT[0][:, x : x + 256], f"do0_{x}") for x in (0, 256)]
+        v_pool = load_words(v_words, "v_pool")
+        qm_raw = load_rows(qm[0], "qm0")
+        q1_raw = load_rows(qT[1], "q1")
+        do1_raw = load_rows(doT[1], "do1")
+        qm1_raw = load_rows(qm[1], "qm1")
+        windows = [zero_window(f"win{c}", True) for c in range(2)]
 
-        k_mx = gather_words("k", k_pool, 1, "x1"), gather_scales("k", k_plane, 1, "x2")
-        v_mx = gather_words("v", v_pool, 1, "p0"), gather_scales("v", v_plane, 1, "x4")
-        q_raw = load_rows("q", qT[1], "q1n")
-        do_raw = load_rows("do", doT[1], "do1n")
-        qm_raw = load_rows("qm", qm[1], "qm1n")
+        k0 = gather(k_pool, U32, 0, "kw0"), gather(k_plane, U8, 0, "ks0")
+        grouped = tile([P, PACK * 512], BF16, "q0g")
+        for h in range(2):
+            deal(grouped, q_halves[h][:], 256 * h, "scalar")
+        q_mx = quantize("q0", grouped[:], E4M3)
+        vs0 = gather(v_plane, U8, 0, "q0g")
+        grouped = tile([P, PACK * 512], BF16, "do0g")
+        deal(grouped, do_halves[0][:], 0, "vector")
+        deal(grouped, do_halves[1][:], 256, "vector")
+        p = weights(0, q_mx, k0)
+        do_mx = quantize("do0", grouped[:], E5M2)
+        v0 = gather(v_pool, U32, 0, "vw0"), vs0
+        dp_banks = value_products(do_mx, v0)
+        vw1 = gather(v_pool, U32, 1, "vw1")
+        k1 = gather(k_pool, U32, 1, "do0_codes"), gather(k_plane, U8, 1, "do0_scales")
+        for t in (0, 2):
+            nc.scalar.activation(p[:, t : t + 2, :], p[:, t : t + 2, :], ACT.Square)
+        ds = tile([P, N, PACK], BF16, "ds0")
+        for h in range(2):
+            cols = slice(256 * h, 256 * (h + 1))
+            minus_ds(ds, p, gated(0, dp_banks, cols, f"x0{h}"), cols)
+        qm_parts = []
+        grouped = tile([P, PACK * 512], BF16, "x00")
+        for x0, x1 in ((0, 128), (128, 256), (256, 512)):
+            interleave(grouped, qm_raw[:, :, x0:x1], x0)
+            qm_parts.append(quantize(f"qm0_{x0}", grouped[:, PACK * x0 : PACK * x1], E4M3))
+        ds_first = quantize("ds0", ds[:].rearrange("p i t -> p (i t)"), E5M2)
+        v1 = vw1, gather(v_plane, U8, 1, "ds0")
+        windows += [zero_window("k_pool", False), zero_window("v_pool", False)]
 
-        key_gradient(0, 0, qm_first, ds_first)
-        q_mx = quantize("q", group_permuted("q", [q_raw[:, :, :256], q_raw[:, :, 256:]], "scalar"), E4M3)
-        do_mx = quantize("do", group_permuted("do", [do_raw[:, :, x : x + 128] for x in range(0, 512, 128)], "scalar"), E5M2)
-        windows += [zero_window(2, False, "k_plane"), zero_window(3, False, "qg1")]
-        key_gradient(0, 1, qm_first, ds_first, staged=do_raw[:, 0, :])
-        p = weights(1, q_mx, k_mx)
-        key_gradient(0, 2, qm_first, ds_first, staged=do_raw[:, 1, :])
-        ds_second = score_gradient(1, p, do_mx, v_mx)
-        qm_second = quantize("qm", group_plain("qm", qm_raw, "scalar"), E4M3)
-        key_gradient(0, 3, qm_first, ds_first, staged=p[:, 0, :])
+        key_gradient(0, 0, qm_parts[0], 0, ds_first)
+        grouped = tile([P, PACK * 512], BF16, "qm0_0_codes")
+        deal(grouped, q1_raw[:], 0, "scalar")
+        q_mx = quantize("q1", grouped[:], E4M3)
+        key_gradient(0, 1, qm_parts[1], 0, ds_first)
+        grouped = tile([P, PACK * 512], BF16, "qm0_0_scales")
+        deal(grouped, do1_raw[:], 0, "scalar")
+        do_mx = quantize("do1", grouped[:], E5M2)
+        p = weights(1, q_mx, k1)
+        key_gradient(0, 2, qm_parts[2], 0, ds_first)
+        dp_banks = value_products(do_mx, v1)
+        for t in (0, 2):
+            nc.scalar.activation(p[:, t : t + 2, :], p[:, t : t + 2, :], ACT.Square)
+        ds = tile([P, N, PACK], BF16, "ds1")
+        for h in range(2):
+            cols = slice(256 * h, 256 * (h + 1))
+            minus_ds(ds, p, gated(1, dp_banks, cols, f"x1{h}"), cols)
+        grouped = tile([P, PACK * 512], BF16, "do1_codes")
+        interleave(grouped, qm1_raw[:], 0)
+        ds_second = quantize("ds1", ds[:].rearrange("p i t -> p (i t)"), E5M2)
+        qm_second = quantize("qm1", grouped[:], E4M3)
+        key_gradient(0, 3, qm_parts[2], 1, ds_first, "x10")
         for c in range(D // P):
-            key_gradient(1, c, qm_second, ds_second)
+            key_gradient(1, c, qm_second, c, ds_second)
             nc.sync.dma_start(out[c * P : (c + 1) * P, :], windows[c][:])

@@ -60,9 +60,9 @@ def tile_attend_gat_tnh_k_kernel(
                     nc.gpsimd.memset(window[:, x : x + 512], 0.0)
             return window
 
-        def quantize(name, grouped, fmt):
+        def quantize(name, grouped, fmt, tag=None):
             words = grouped.shape[1] // PACK
-            codes = tile([P, words], U32, f"{name}_codes")
+            codes = tile([P, words], U32, tag or f"{name}_codes")
             scales = tile([P, words], U8, f"{name}_scales")
             nc.vector.quantize_mx(out=codes[:].bitcast(fmt), scales=scales[:], in_=grouped)
             return codes, scales
@@ -79,15 +79,20 @@ def tile_attend_gat_tnh_k_kernel(
             width = piece.shape[2]
             dst = grouped[:].rearrange("p (t m j) -> p m j t", t=PACK, j=PACK)[:, x0 // PACK : (x0 + width) // PACK]
             src = piece.rearrange("p j (m t) -> p m j t", t=PACK)
+            nc.scalar.copy(dst, src)
+
+        def deal_vector(grouped, raw):
+            dst = grouped[:].rearrange("p (u v m j) -> p u m j v", u=2, v=2, j=PACK)
+            nc.vector.tensor_copy(dst, raw[:].rearrange("p j (m u v) -> p u m j v", u=2, v=2))
+
+        def interleave(grouped, piece, x0, engine="scalar"):
+            width = piece.shape[2]
+            dst = grouped[:, PACK * x0 : PACK * (x0 + width)].rearrange("p (c i j) -> p c j i", i=4, j=PACK)
+            src = piece.rearrange("p j (c i) -> p c j i", i=4)
             if engine == "vector":
                 nc.vector.tensor_copy(dst, src)
             else:
                 nc.scalar.copy(dst, src)
-
-        def interleave(grouped, piece, x0):
-            width = piece.shape[2]
-            dst = grouped[:, PACK * x0 : PACK * (x0 + width)].rearrange("p (c i j) -> p c j i", i=4, j=PACK)
-            nc.scalar.copy(dst, piece.rearrange("p j (c i) -> p c j i", i=4))
 
         def product(bank, lhs, lhs_fmt, block, rhs, rhs_fmt):
             cols = slice(block * P, (block + 1) * P)
@@ -101,115 +106,127 @@ def tile_attend_gat_tnh_k_kernel(
                 stop=True,
             )
 
+        def by_quarters(bank):
+            return bank[:].rearrange("p (i c) -> p c i", i=4)
+
         def weights(b, q_mx, k_mx):
-            p = tile([P, PACK, N], F32, f"p{b}")
+            p = tile([P, P, PACK, 4], F32, f"p{b}")
             for t in range(PACK):
                 bank = psum.tile([P, N], F32, name="a_bank", tag="a", bufs=4)
                 product(bank, q_mx, E4M3, t, k_mx, E4M3)
-                nc.scalar.activation(p[:, t, :], bank[:], ACT.Tanh)
+                nc.scalar.activation(p[:, :, t, :], by_quarters(bank), ACT.Tanh)
             return p
 
-        def value_products(do_mx, v_mx):
+        def value_products(do_blocks, v_mx):
             banks = []
             for t in range(PACK):
                 bank = psum.tile([P, N], F32, name="dp_bank", tag="dp", bufs=4)
-                product(bank, do_mx, E5M2, t, v_mx, E4M3)
+                product(bank, do_blocks[t][0], E5M2, do_blocks[t][1], v_mx, E4M3)
                 banks.append(bank)
             return banks
 
-        def gated(b, dp_banks, cols, tag):
-            width = cols.stop - cols.start
-            x = tile([P, PACK, width], F32, tag)
+        def gated(b, dp_banks, h, tag):
+            x = tile([P, P // 2, PACK, 4], F32, tag)
             for t in range(PACK):
-                nc.scalar.activation(x[:, t, :], dp_banks[t][:, cols], ACT.Copy, scale=gates[:, b, t : t + 1])
+                part = by_quarters(dp_banks[t])[:, 64 * h : 64 * (h + 1), :]
+                nc.scalar.activation(x[:, :, t, :], part, ACT.Copy, scale=gates[:, b, t : t + 1])
             return x
 
-        def minus_ds(ds, p, x, cols):
+        def minus_ds(ds, p, x, h):
             nc.vector.scalar_tensor_tensor(
-                out=ds[:, cols, :],
-                in0=p[:, :, cols].rearrange("p t i -> p i t"),
+                out=ds[:].rearrange("p (i y) -> p y i", i=4)[:, 256 * h : 256 * (h + 1), :],
+                in0=p[:, 64 * h : 64 * (h + 1)].rearrange("p c t i -> p (c t) i"),
                 scalar=1.0,
-                in1=x[:].rearrange("p t i -> p i t"),
+                in1=x[:].rearrange("p c t i -> p (c t) i"),
                 op0=ALU.subtract,
                 op1=ALU.mult,
             )
 
-        def key_gradient(b, c, qm_mx, block, ds_mx, tag=None):
+        def square(p):
+            for t in (0, 2):
+                nc.scalar.activation(p[:, :, t : t + 2, :], p[:, :, t : t + 2, :], ACT.Square)
+
+
+        def key_product(qm_mx, block, ds_mx):
             bank = psum.tile([P, N], F32, name="dk_bank", tag="a", bufs=4)
             product(bank, qm_mx, E4M3, block, ds_mx, E5M2)
+            return bank
+
+        def place(b, c, bank, tag=None):
             staged = tile([P, N], F32, tag or f"dk{b}{c}")
             nc.scalar.activation(staged[:], bank[:], ACT.Copy, scale=-1.0)
             nc.vector.tensor_copy(windows[c][:].indirect(listed(b)), staged[:])
 
+        def key_gradient(b, c, qm_mx, block, ds_mx, tag=None):
+            place(b, c, key_product(qm_mx, block, ds_mx), tag)
+
         offsets = keep.tile([P, B * LIST_COLS], U16, name="offsets")
         nc.sync.dma_start(offsets[:], offs)
 
-        q_halves = [load_rows(qT[0][:, x : x + 256], f"q0_{x}") for x in (0, 256)]
-        k_plane = load_scales(k_scales, "k_plane")
-        k_pool = load_words(k_words, "k_pool")
+        q_raw = load_rows(qT[0], "q0")
         gates = tile([P, B, PACK], F32, "gates")
         nc.sync.dma_start(gates[:], rw.rearrange("b (p t) o -> p b (t o)", t=PACK))
+        k_plane = load_scales(k_scales, "k_plane")
+        k_pool = load_words(k_words, "k_pool")
         v_plane = load_scales(v_scales, "v_plane")
-        do_halves = [load_rows(doT[0][:, x : x + 256], f"do0_{x}") for x in (0, 256)]
+        do_raw = load_rows(doT[0], "do0")
         v_pool = load_words(v_words, "v_pool")
         qm_raw = load_rows(qm[0], "qm0")
         q1_raw = load_rows(qT[1], "q1")
         do1_raw = load_rows(doT[1], "do1")
         qm1_raw = load_rows(qm[1], "qm1")
-        windows = [zero_window(f"win{c}", True) for c in range(2)]
+        windows = [zero_window(f"win{c}", True) for c in range(4)]
 
-        k0 = gather(k_pool, U32, 0, "kw0"), gather(k_plane, U8, 0, "ks0")
+        ks0 = gather(k_plane, U8, 0, "ks0")
         grouped = tile([P, PACK * 512], BF16, "q0g")
-        for h in range(2):
-            deal(grouped, q_halves[h][:], 256 * h, "scalar")
+        deal(grouped, q_raw[:], 0, "scalar")
         q_mx = quantize("q0", grouped[:], E4M3)
-        vs0 = gather(v_plane, U8, 0, "q0g")
-        grouped = tile([P, PACK * 512], BF16, "do0g")
-        deal(grouped, do_halves[0][:], 0, "vector")
-        deal(grouped, do_halves[1][:], 256, "vector")
+        k0 = gather(k_pool, U32, 0, "kw0"), ks0
         p = weights(0, q_mx, k0)
-        do_mx = quantize("do0", grouped[:], E5M2)
+        vs0 = gather(v_plane, U8, 0, "vs0")
+        grouped = tile([P, PACK * 512], BF16, "do0g")
+        deal_vector(grouped, do_raw)
+        parts = [
+            quantize(f"do0_{x0}", grouped[:, PACK * x0 : PACK * x1], E5M2) for x0, x1 in ((0, 128), (128, 256), (256, 512))
+        ]
         v0 = gather(v_pool, U32, 0, "vw0"), vs0
-        dp_banks = value_products(do_mx, v0)
+        dp_banks = value_products([(parts[0], 0), (parts[1], 0), (parts[2], 0), (parts[2], 1)], v0)
         vw1 = gather(v_pool, U32, 1, "vw1")
-        k1 = gather(k_pool, U32, 1, "do0_codes"), gather(k_plane, U8, 1, "do0_scales")
-        for t in (0, 2):
-            nc.scalar.activation(p[:, t : t + 2, :], p[:, t : t + 2, :], ACT.Square)
-        ds = tile([P, N, PACK], BF16, "ds0")
+        k1 = gather(k_pool, U32, 1, "do0_0_scales"), gather(k_plane, U8, 1, "do0_0_codes")
+        square(p)
+        qm_grouped = tile([P, PACK * 512], BF16, "qm0g")
+        interleave(qm_grouped, qm_raw[:, :, :256], 0)
+        qm_low = quantize("qm0_low", qm_grouped[:, : PACK * 256], E4M3)
+        ds = tile([P, N * PACK], BF16, "ds0")
         for h in range(2):
-            cols = slice(256 * h, 256 * (h + 1))
-            minus_ds(ds, p, gated(0, dp_banks, cols, f"x0{h}"), cols)
-        qm_parts = []
-        grouped = tile([P, PACK * 512], BF16, "x00")
-        for x0, x1 in ((0, 128), (128, 256), (256, 512)):
-            interleave(grouped, qm_raw[:, :, x0:x1], x0)
-            qm_parts.append(quantize(f"qm0_{x0}", grouped[:, PACK * x0 : PACK * x1], E4M3))
-        ds_first = quantize("ds0", ds[:].rearrange("p i t -> p (i t)"), E5M2)
+            minus_ds(ds, p, gated(0, dp_banks, h, f"x0{h}"), h)
+        ds_first = quantize("ds0", ds[:], E5M2)
         v1 = vw1, gather(v_plane, U8, 1, "ds0")
-        windows += [zero_window("k_pool", False), zero_window("v_pool", False)]
 
-        key_gradient(0, 0, qm_parts[0], 0, ds_first)
-        grouped = tile([P, PACK * 512], BF16, "qm0_0_codes")
+        grouped = tile([P, PACK * 512], BF16, "x00")
         deal(grouped, q1_raw[:], 0, "scalar")
         q_mx = quantize("q1", grouped[:], E4M3)
-        key_gradient(0, 1, qm_parts[1], 0, ds_first)
-        grouped = tile([P, PACK * 512], BF16, "qm0_0_scales")
+        key_gradient(0, 0, qm_low, 0, ds_first)
+        bank = key_product(qm_low, 1, ds_first)
+        qm_grouped = tile([P, PACK * 256], BF16, "qm0_low_scales")
+        interleave(qm_grouped, qm_raw[:, :, 256:], 0)
+        qm_high = quantize("qm0_high", qm_grouped[:], E4M3)
+        grouped = tile([P, PACK * 512], BF16, "x00")
         deal(grouped, do1_raw[:], 0, "scalar")
         do_mx = quantize("do1", grouped[:], E5M2)
+        place(0, 1, bank)
         p = weights(1, q_mx, k1)
-        key_gradient(0, 2, qm_parts[2], 0, ds_first)
-        dp_banks = value_products(do_mx, v1)
-        for t in (0, 2):
-            nc.scalar.activation(p[:, t : t + 2, :], p[:, t : t + 2, :], ACT.Square)
-        ds = tile([P, N, PACK], BF16, "ds1")
+        key_gradient(0, 2, qm_high, 0, ds_first)
+        dp_banks = value_products([(do_mx, t) for t in range(PACK)], v1)
+        square(p)
+        ds = tile([P, N * PACK], BF16, "ds1")
         for h in range(2):
-            cols = slice(256 * h, 256 * (h + 1))
-            minus_ds(ds, p, gated(1, dp_banks, cols, f"x1{h}"), cols)
+            minus_ds(ds, p, gated(1, dp_banks, h, f"x1{h}"), h)
         grouped = tile([P, PACK * 512], BF16, "do1_codes")
         interleave(grouped, qm1_raw[:], 0)
-        ds_second = quantize("ds1", ds[:].rearrange("p i t -> p (i t)"), E5M2)
+        ds_second = quantize("ds1", ds[:], E5M2)
         qm_second = quantize("qm1", grouped[:], E4M3)
-        key_gradient(0, 3, qm_parts[2], 1, ds_first, "x10")
+        key_gradient(0, 3, qm_high, 1, ds_first, "x11")
         for c in range(D // P):
             key_gradient(1, c, qm_second, c, ds_second)
             nc.sync.dma_start(out[c * P : (c + 1) * P, :], windows[c][:])

@@ -18,7 +18,28 @@ ALU = mybir.AluOpType
 
 P = 128
 PACK = 4
-LIST_COLS = N // 16
+LINE = 4
+GROUP = 16
+BANKS = 4
+HALF = N // 2
+RUN = HALF // LINE
+VECTOR_SHARE = 320
+
+KIB = 1024
+AT_GATED_LOW = 0
+AT_QM_FIRST_CODES = 0
+AT_QM_SECOND = 3 * KIB
+AT_DS_HIGH = 4 * KIB
+AT_QM_LAST = 3 * KIB
+AT_GATED_HIGH = 8 * KIB
+AT_Q_NEXT = 7 * KIB
+AT_FIRST_STAGE = 11 * KIB
+AT_THIRD_WINDOW = 3 * KIB
+AT_DO_RAW = 36 * KIB
+AT_V_SCALES_NEXT = 36 * KIB
+AT_TANH = 38 * KIB
+AT_DO_NEXT = 38 * KIB
+AT_FOURTH_WINDOW = 38 * KIB
 
 
 def tile_attend_gat_tnh_k_kernel(
@@ -28,205 +49,224 @@ def tile_attend_gat_tnh_k_kernel(
     with ExitStack() as ctx:
         keep = ctx.enter_context(tc.tile_pool(name="keep", bufs=1))
         sb = ctx.enter_context(tc.tile_pool(name="sb", bufs=1))
+        placed = ctx.enter_context(tc.tile_pool(name="placed", bufs=1))
         psum = ctx.enter_context(tc.psum_pool(name="psum", bufs=1))
 
-        def tile(shape, dtype, tag):
-            return sb.tile(shape, dtype, name=tag, tag=tag, align_bytes=64)
+        def tile(shape, dtype, tag, offset=None):
+            if offset is None:
+                return sb.tile(shape, dtype, name=tag, tag=tag, align_bytes=64)
+            return placed.tile(shape, dtype, name=tag, tag=tag, align_bytes=64, offset=offset)
 
-        def load_rows(src, tag):
-            raw = tile([P, PACK, src.shape[1]], F32, tag)
+        def load_rows(src, tag, offset=None):
+            raw = tile([P, PACK, src.shape[1]], F32, tag, offset)
             nc.sync.dma_start(raw[:], src.rearrange("(p j) w -> p j w", j=PACK))
             return raw
 
-        def load_scales(src, tag):
+        def zero_plane(tag):
             plane = tile([P, T // 4], I32, tag)
             nc.vector.memset(plane[:], 0)
+            return plane
+
+        def load_scales(plane, src):
             rows = src[0].bitcast(I32)
             for f in range(4):
                 nc.sync.dma_start(plane[f:P:32, :], rows[f:16:4, :])
-            return plane
 
-        def load_words(src, tag):
-            words = tile([P, T], I32, tag)
-            nc.sync.dma_start(words[:], src[0].rearrange("p n j -> p (n j)").bitcast(I32))
-            return words
+        def word_rows(src):
+            return src[0].rearrange("p n j -> p (n j)").bitcast(I32)
 
-        def zero_window(tag, on_vector):
-            window = tile([P, T], F32, tag)
-            if on_vector:
-                nc.vector.memset(window[:], 0.0)
-            else:
-                for x in range(0, T, 512):
-                    nc.gpsimd.memset(window[:, x : x + 512], 0.0)
+        def zero_window(engine, tag, offset=None):
+            window = tile([P, T], F32, tag, offset)
+            engine.memset(window[:], 0.0)
             return window
 
-        def quantize(name, grouped, fmt, tag=None):
-            words = grouped.shape[1] // PACK
-            codes = tile([P, words], U32, tag or f"{name}_codes")
-            scales = tile([P, words], U8, f"{name}_scales")
-            nc.vector.quantize_mx(out=codes[:].bitcast(fmt), scales=scales[:], in_=grouped)
-            return codes, scales
+        def mx_tiles(name, words):
+            return tile([P, words], U32, f"{name}_codes"), tile([P, words], U8, f"{name}_scales")
 
-        def listed(b):
-            return offsets[:, b * LIST_COLS : (b + 1) * LIST_COLS]
+        def quantize(mx, x0, grouped, fmt):
+            cols = slice(x0, x0 + grouped.shape[1] // PACK)
+            nc.vector.quantize_mx(out=mx[0][:, cols].bitcast(fmt), scales=mx[1][:, cols], in_=grouped)
 
-        def gather(pool_tile, dtype, b, tag):
-            got = tile([P, N], dtype, tag)
-            nc.vector.tensor_copy(got[:], pool_tile[:].bitcast(dtype).indirect(listed(b)))
+        def listed(first, count):
+            return offsets[:, first // GROUP : (first + count) // GROUP]
+
+        def gather(pool_tile, dtype, first, count, tag, offset=None):
+            got = tile([P, count], dtype, tag, offset)
+            nc.vector.tensor_copy(got[:], pool_tile[:].bitcast(dtype).indirect(listed(first, count)))
             return got
 
-        def deal(grouped, piece, x0, engine):
-            width = piece.shape[2]
-            dst = grouped[:].rearrange("p (t m j) -> p m j t", t=PACK, j=PACK)[:, x0 // PACK : (x0 + width) // PACK]
-            src = piece.rearrange("p j (m t) -> p m j t", t=PACK)
-            nc.scalar.copy(dst, src)
+        def deal(grouped, raw, x0, x1):
+            dst = grouped[:].rearrange("p (t m j) -> p m j t", t=PACK, j=PACK)[:, x0 // PACK : x1 // PACK]
+            nc.scalar.copy(dst, raw[:, :, x0:x1].rearrange("p j (m t) -> p m j t", t=PACK))
 
-        def deal_vector(grouped, raw):
-            dst = grouped[:].rearrange("p (u v m j) -> p u m j v", u=2, v=2, j=PACK)
-            nc.vector.tensor_copy(dst, raw[:].rearrange("p j (m u v) -> p u m j v", u=2, v=2))
+        def deal_vector(grouped, raw, x0, x1):
+            dst = grouped[:].rearrange("p (u v m j) -> p u m j v", u=2, v=2, j=PACK)[:, :, x0 // PACK : x1 // PACK]
+            nc.vector.tensor_copy(dst, raw[:, :, x0:x1].rearrange("p j (m u v) -> p u m j v", u=2, v=2))
 
-        def interleave(grouped, piece, x0, engine="scalar"):
-            width = piece.shape[2]
-            dst = grouped[:, PACK * x0 : PACK * (x0 + width)].rearrange("p (c i j) -> p c j i", i=4, j=PACK)
-            src = piece.rearrange("p j (c i) -> p c j i", i=4)
-            if engine == "vector":
-                nc.vector.tensor_copy(dst, src)
-            else:
-                nc.scalar.copy(dst, src)
+        def group(piece, tag, offset=None):
+            grouped = tile([P, PACK * piece.shape[2]], BF16, tag, offset)
+            dst = grouped[:].rearrange("p (c i j) -> p c j i", i=LINE, j=PACK)
+            nc.scalar.copy(dst, piece.rearrange("p j (c i) -> p c j i", i=LINE))
+            return grouped
 
-        def product(bank, lhs, lhs_fmt, block, rhs, rhs_fmt):
+        def group_gpsimd(piece, tag, offset=None):
+            grouped = tile([P, PACK * piece.shape[2]], BF16, tag, offset)
+            dst = grouped[:].rearrange("p (c j) -> p c j", j=PACK)
+            nc.gpsimd.tensor_scalar(dst, piece.rearrange("p j c -> p c j"), 1.0, 0.0, ALU.mult, ALU.add)
+            return grouped
+
+        def product(ring, lhs, lhs_fmt, block, rhs, rhs_fmt, x0=0):
+            bank = psum.tile([P, N], F32, name=f"{ring}_bank", tag=ring, bufs=BANKS)
             cols = slice(block * P, (block + 1) * P)
             nc.tensor.matmul_mx(
                 out=bank[:],
                 lhsT=lhs[0][:, cols].bitcast(lhs_fmt),
                 lhsT_scale=lhs[1][:, cols],
-                rhs=rhs[0][:].bitcast(rhs_fmt),
-                rhs_scale=rhs[1][:],
+                rhs=rhs[0][:, x0 : x0 + N].bitcast(rhs_fmt),
+                rhs_scale=rhs[1][:, x0 : x0 + N],
                 start=True,
                 stop=True,
             )
+            return bank
 
-        def by_quarters(bank):
-            return bank[:].rearrange("p (i c) -> p c i", i=4)
+        def by_lines(bank):
+            return bank[:].rearrange("p (h i c) -> p h c i", h=2, i=LINE)
 
-        def weights(b, q_mx, k_mx):
-            p = tile([P, P, PACK, 4], F32, f"p{b}")
+        def weights(tag, q_mx, k_mx, offset=None):
+            p = tile([P, 2, RUN, PACK, LINE], F32, tag, offset)
             for t in range(PACK):
-                bank = psum.tile([P, N], F32, name="a_bank", tag="a", bufs=4)
-                product(bank, q_mx, E4M3, t, k_mx, E4M3)
-                nc.scalar.activation(p[:, :, t, :], by_quarters(bank), ACT.Tanh)
+                bank = product("a", q_mx, E4M3, t, k_mx, E4M3)
+                nc.scalar.activation(p[:, :, :, t, :], by_lines(bank), ACT.Tanh)
             return p
 
-        def value_products(do_blocks, v_mx):
-            banks = []
-            for t in range(PACK):
-                bank = psum.tile([P, N], F32, name="dp_bank", tag="dp", bufs=4)
-                product(bank, do_blocks[t][0], E5M2, do_blocks[t][1], v_mx, E4M3)
-                banks.append(bank)
-            return banks
+        def square(p, h):
+            nc.scalar.activation(p[:, h], p[:, h], ACT.Square)
 
-        def gated(b, dp_banks, h, tag):
-            x = tile([P, P // 2, PACK, 4], F32, tag)
+        def gated(b, dp_banks, h, tag, offset=None):
+            x = tile([P, RUN, PACK, LINE], F32, tag, offset)
             for t in range(PACK):
-                part = by_quarters(dp_banks[t])[:, 64 * h : 64 * (h + 1), :]
-                nc.scalar.activation(x[:, :, t, :], part, ACT.Copy, scale=gates[:, b, t : t + 1])
+                nc.scalar.activation(x[:, :, t, :], by_lines(dp_banks[t])[:, h], ACT.Copy, scale=gates[:, b, t : t + 1])
             return x
 
-        def minus_ds(ds, p, x, h):
+        def minus_ds(p, x, h, ds):
             nc.vector.scalar_tensor_tensor(
-                out=ds[:].rearrange("p (i y) -> p y i", i=4)[:, 256 * h : 256 * (h + 1), :],
-                in0=p[:, 64 * h : 64 * (h + 1)].rearrange("p c t i -> p (c t) i"),
+                out=ds.rearrange("p (i y) -> p y i", i=LINE),
+                in0=p[:, h].rearrange("p c t i -> p (c t) i"),
                 scalar=1.0,
                 in1=x[:].rearrange("p c t i -> p (c t) i"),
                 op0=ALU.subtract,
                 op1=ALU.mult,
             )
 
-        def square(p):
-            for t in (0, 2):
-                nc.scalar.activation(p[:, :, t : t + 2, :], p[:, :, t : t + 2, :], ACT.Square)
+        def place(first, c, part, tag, offset=None):
+            count = part.shape[1]
+            staged = tile([P, count], F32, tag, offset)
+            nc.scalar.activation(staged[:], part, ACT.Copy, scale=-1.0)
+            nc.vector.tensor_copy(windows[c][:].indirect(listed(first, count)), staged[:])
 
-
-        def key_product(qm_mx, block, ds_mx):
-            bank = psum.tile([P, N], F32, name="dk_bank", tag="a", bufs=4)
-            product(bank, qm_mx, E4M3, block, ds_mx, E5M2)
-            return bank
-
-        def place(b, c, bank, tag=None):
-            staged = tile([P, N], F32, tag or f"dk{b}{c}")
-            nc.scalar.activation(staged[:], bank[:], ACT.Copy, scale=-1.0)
-            nc.vector.tensor_copy(windows[c][:].indirect(listed(b)), staged[:])
-
-        def key_gradient(b, c, qm_mx, block, ds_mx, tag=None):
-            place(b, c, key_product(qm_mx, block, ds_mx), tag)
-
-        offsets = keep.tile([P, B * LIST_COLS], U16, name="offsets")
+        offsets = keep.tile([P, B * N // GROUP], U16, name="offsets")
         nc.sync.dma_start(offsets[:], offs)
 
+        k_plane = zero_plane("k_plane")
+        v_plane = zero_plane("v_plane")
+        k_pool = tile([P, T], I32, "k_pool")
+        nc.sync.dma_start(k_pool[:, : T // 2], word_rows(k_words)[:, : T // 2])
+        load_scales(k_plane, k_scales)
         q_raw = load_rows(qT[0], "q0")
+        load_scales(v_plane, v_scales)
+        nc.sync.dma_start(k_pool[:, T // 2 :], word_rows(k_words)[:, T // 2 :])
+        do_raw = load_rows(doT[0], "do0", AT_DO_RAW)
+        v_pool = tile([P, T], I32, "v_pool")
+        nc.sync.dma_start(v_pool[:], word_rows(v_words))
+        qm_first_raw = load_rows(qm[0][:, :P], "qm0a")
         gates = tile([P, B, PACK], F32, "gates")
         nc.sync.dma_start(gates[:], rw.rearrange("b (p t) o -> p b (t o)", t=PACK))
-        k_plane = load_scales(k_scales, "k_plane")
-        k_pool = load_words(k_words, "k_pool")
-        v_plane = load_scales(v_scales, "v_plane")
-        do_raw = load_rows(doT[0], "do0")
-        v_pool = load_words(v_words, "v_pool")
-        qm_raw = load_rows(qm[0], "qm0")
-        q1_raw = load_rows(qT[1], "q1")
-        do1_raw = load_rows(doT[1], "do1")
-        qm1_raw = load_rows(qm[1], "qm1")
-        windows = [zero_window(f"win{c}", True) for c in range(4)]
+        qm_rest_raw = load_rows(qm[0][:, P:], "qm0b")
+        q_next_raw = load_rows(qT[1], "q1")
+        do_next_raw = load_rows(doT[1], "do1")
+        qm_next_raw = load_rows(qm[1], "qm1")
+        windows = [zero_window(nc.vector, f"win{c}") for c in range(2)]
 
-        ks0 = gather(k_plane, U8, 0, "ks0")
-        grouped = tile([P, PACK * 512], BF16, "q0g")
-        deal(grouped, q_raw[:], 0, "scalar")
-        q_mx = quantize("q0", grouped[:], E4M3)
-        k0 = gather(k_pool, U32, 0, "kw0"), ks0
-        p = weights(0, q_mx, k0)
-        vs0 = gather(v_plane, U8, 0, "vs0")
-        grouped = tile([P, PACK * 512], BF16, "do0g")
-        deal_vector(grouped, do_raw)
-        parts = [
-            quantize(f"do0_{x0}", grouped[:, PACK * x0 : PACK * x1], E5M2) for x0, x1 in ((0, 128), (128, 256), (256, 512))
-        ]
-        v0 = gather(v_pool, U32, 0, "vw0"), vs0
-        dp_banks = value_products([(parts[0], 0), (parts[1], 0), (parts[2], 0), (parts[2], 1)], v0)
-        vw1 = gather(v_pool, U32, 1, "vw1")
-        k1 = gather(k_pool, U32, 1, "do0_0_scales"), gather(k_plane, U8, 1, "do0_0_codes")
-        square(p)
-        qm_grouped = tile([P, PACK * 512], BF16, "qm0g")
-        interleave(qm_grouped, qm_raw[:, :, :256], 0)
-        qm_low = quantize("qm0_low", qm_grouped[:, : PACK * 256], E4M3)
-        ds = tile([P, N * PACK], BF16, "ds0")
+        k_bytes = gather(k_plane, U8, 0, B * N, "ks")
+        v_bytes = gather(v_plane, U8, 0, N, "vs0")
+        grouped = tile([P, PACK * R], BF16, "q0g")
+        deal(grouped, q_raw, 0, R)
+        keys = gather(k_pool, U32, 0, N, "kw0"), k_bytes[:, :N]
+        q_mx = mx_tiles("q0", R)
+        quantize(q_mx, 0, grouped[:], E4M3)
+        grouped = tile([P, PACK * R], BF16, "do0g")
+        deal(grouped, do_raw, VECTOR_SHARE, R)
+        deal_vector(grouped, do_raw, 0, VECTOR_SHARE)
+        v_bytes_next = gather(v_plane, U8, N, N, "vs1", AT_V_SCALES_NEXT)
+        p = weights("p0", q_mx, keys, AT_TANH)
+        ds_mx = mx_tiles("ds0", 3 * HALF)
+        do_parts = [mx_tiles("do0_0", P), mx_tiles("do0_1", P), ds_mx]
+        for part, (x0, x1) in zip(do_parts, ((0, P), (P, 2 * P), (2 * P, R))):
+            quantize(part, 0, grouped[:, PACK * x0 : PACK * x1], E5M2)
+        for part in do_parts[:2]:
+            product("dp", part, E5M2, 0, keys, E4M3)
+        values = gather(v_pool, U32, 0, N, "vw0"), v_bytes
+        do_blocks = [(do_parts[0], 0), (do_parts[1], 0), (ds_mx, 0), (ds_mx, 1)]
+        dp_banks = [product("dp", part, E5M2, block, values, E4M3) for part, block in do_blocks]
+        values_next = gather(v_pool, U32, N, N, "vw1"), v_bytes_next
+        qm_first_grouped = group_gpsimd(qm_first_raw[:], "qm0ag")
+        keys_next = gather(k_pool, U32, N, N, "do0_0_scales"), k_bytes[:, N:]
+
+        gated_halves = []
+        for h, offset in enumerate((AT_GATED_LOW, AT_GATED_HIGH)):
+            square(p, h)
+            gated_halves.append(gated(0, dp_banks, h, f"x0{h}", offset))
+        ds = tile([P, HALF * PACK], BF16, "ds00")
+        minus_ds(p, gated_halves[0], 0, ds[:])
+        qm_first = tile([P, P], U32, "qm0a_codes", AT_QM_FIRST_CODES), tile([P, P], U8, "qm0a_scales")
+        quantize(qm_first, 0, qm_first_grouped[:], E4M3)
+        quantize(ds_mx, HALF, ds[:], E5M2)
+        ds = tile([P, HALF * PACK], BF16, "ds01", AT_DS_HIGH)
+        minus_ds(p, gated_halves[1], 1, ds[:])
+        quantize(ds_mx, 2 * HALF, ds[:], E5M2)
+
+        grouped = group(qm_rest_raw[:, :, :P], "qm0bg", AT_QM_SECOND)
+        qm_second = mx_tiles("qm0b", P)
+        quantize(qm_second, 0, grouped[:], E4M3)
+        place(0, 0, product("a", qm_first, E4M3, 0, ds_mx, E5M2)[:, HALF:], "dk00a", AT_FIRST_STAGE)
+        qm_last_grouped = group_gpsimd(qm_rest_raw[:, :, P:], "qm0cg", AT_QM_LAST)
+        grouped = tile([P, PACK * R], BF16, "q1g", AT_Q_NEXT)
+        deal(grouped, q_next_raw, 0, R // 2)
+        place(HALF, 0, product("a", qm_first, E4M3, 0, ds_mx, E5M2, HALF)[:, HALF:], "dk00b")
+        deal(grouped, q_next_raw, R // 2, R)
+        qm_last = mx_tiles("qm0c", 2 * P)
+        quantize(qm_last, 0, qm_last_grouped[:], E4M3)
+        q_mx = mx_tiles("q1", R)
+        quantize(q_mx, 0, grouped[:], E4M3)
+        windows.append(zero_window(nc.gpsimd, "win2", AT_THIRD_WINDOW))
+        place(0, 1, product("a", qm_second, E4M3, 0, ds_mx, E5M2, HALF)[:], "dk01")
+        grouped = tile([P, PACK * R], BF16, "do1g", AT_DO_NEXT)
+        deal(grouped, do_next_raw, 0, R)
+        do_mx = mx_tiles("do1", R)
+        quantize(do_mx, 0, grouped[:], E5M2)
+        windows.append(zero_window(nc.gpsimd, "win3", AT_FOURTH_WINDOW))
+        place(0, 2, product("a", qm_last, E4M3, 0, ds_mx, E5M2, HALF)[:], "dk02")
+        p = weights("p1", q_mx, keys_next)
+        last_bank = product("a", qm_last, E4M3, 1, ds_mx, E5M2, HALF)
+        place(0, 3, last_bank[:, :HALF], "dk03a")
+
+        dp_banks = [product("dp", do_mx, E5M2, t, values_next, E4M3) for t in range(PACK)]
         for h in range(2):
-            minus_ds(ds, p, gated(0, dp_banks, h, f"x0{h}"), h)
-        ds_first = quantize("ds0", ds[:], E5M2)
-        v1 = vw1, gather(v_plane, U8, 1, "ds0")
-
-        grouped = tile([P, PACK * 512], BF16, "x00")
-        deal(grouped, q1_raw[:], 0, "scalar")
-        q_mx = quantize("q1", grouped[:], E4M3)
-        key_gradient(0, 0, qm_low, 0, ds_first)
-        bank = key_product(qm_low, 1, ds_first)
-        qm_grouped = tile([P, PACK * 256], BF16, "qm0_low_scales")
-        interleave(qm_grouped, qm_raw[:, :, 256:], 0)
-        qm_high = quantize("qm0_high", qm_grouped[:], E4M3)
-        grouped = tile([P, PACK * 512], BF16, "x00")
-        deal(grouped, do1_raw[:], 0, "scalar")
-        do_mx = quantize("do1", grouped[:], E5M2)
-        place(0, 1, bank)
-        p = weights(1, q_mx, k1)
-        key_gradient(0, 2, qm_high, 0, ds_first)
-        dp_banks = value_products([(do_mx, t) for t in range(PACK)], v1)
-        square(p)
+            square(p, h)
         ds = tile([P, N * PACK], BF16, "ds1")
         for h in range(2):
-            minus_ds(ds, p, gated(1, dp_banks, h, f"x1{h}"), h)
-        grouped = tile([P, PACK * 512], BF16, "do1_codes")
-        interleave(grouped, qm1_raw[:], 0)
-        ds_second = quantize("ds1", ds[:], E5M2)
-        qm_second = quantize("qm1", grouped[:], E4M3)
-        key_gradient(0, 3, qm_high, 1, ds_first, "x11")
-        for c in range(D // P):
-            key_gradient(1, c, qm_second, c, ds_second)
+            minus_ds(p, gated(1, dp_banks, h, f"x1{h}"), h, ds[:, h * HALF * PACK : (h + 1) * HALF * PACK])
+        ds_mx = mx_tiles("ds1", N)
+        quantize(ds_mx, 0, ds[:], E5M2)
+        qm_first_grouped = group(qm_next_raw[:, :, :P], "qm1a")
+        qm_first = mx_tiles("qm1a", P)
+        qm_rest_grouped = group(qm_next_raw[:, :, P:], "qm1b")
+        qm_rest = mx_tiles("qm1b", D - P)
+        quantize(qm_first, 0, qm_first_grouped[:], E4M3)
+        place(HALF, 3, last_bank[:, HALF:], "x11")
+        for x0, x1 in ((0, P), (P, D - P)):
+            quantize(qm_rest, x0, qm_rest_grouped[:, PACK * x0 : PACK * x1], E4M3)
+        qm_blocks = [(qm_first, 0), (qm_rest, 0), (qm_rest, 1), (qm_rest, 2)]
+        for c, (qm_mx, block) in enumerate(qm_blocks):
+            place(N, c, product("a", qm_mx, E4M3, block, ds_mx, E5M2)[:], f"dk1{c}")
             nc.sync.dma_start(out[c * P : (c + 1) * P, :], windows[c][:])

@@ -203,8 +203,6 @@ def tile_attend_gat_tnh_k_kernel(
         do_parts = [mx_tiles("do0_0", P), mx_tiles("do0_1", P), ds_mx]
         for part, (x0, x1) in zip(do_parts, ((0, P), (P, 2 * P), (2 * P, R))):
             quantize(part, 0, grouped[:, PACK * x0 : PACK * x1], E5M2)
-        for part in do_parts[:2]:
-            product("dp", part, E5M2, 0, keys, E4M3)
         values = gather(v_pool, U32, 0, N, "vw0"), v_bytes
         do_blocks = [(do_parts[0], 0), (do_parts[1], 0), (ds_mx, 0), (ds_mx, 1)]
         dp_banks = [product("dp", part, E5M2, block, values, E4M3) for part, block in do_blocks]

@@ -40,6 +40,20 @@ AT_V_SCALES_NEXT = 36 * KIB
 AT_TANH = 38 * KIB
 AT_DO_NEXT = 38 * KIB
 AT_FOURTH_WINDOW = 38 * KIB
+AT_QM_NEXT_LOW = 11 * KIB
+AT_GATED_NEXT_LOW = 13 * KIB
+AT_QM_NEXT_LOW_CODES = 13 * KIB
+AT_FOURTH_STAGE = 15 * KIB
+AT_DS_NEXT_LOW = 17 * KIB
+AT_SLOPE = 17 * KIB
+AT_DO_NEXT_RAW = 24 * KIB
+AT_TANH_NEXT_LOW = 22 * KIB
+AT_THIRD_STAGE = 26 * KIB
+AT_TANH_NEXT_HIGH = 28 * KIB
+AT_QM_NEXT_HIGH = 22 * KIB
+AT_GATED_NEXT_HIGH = 32 * KIB
+AT_SIXTH_STAGE = 32 * KIB
+AT_QM_NEXT_HIGH_CODES = 33 * KIB
 
 
 def tile_attend_gat_tnh_k_kernel(
@@ -183,7 +197,7 @@ def tile_attend_gat_tnh_k_kernel(
         nc.sync.dma_start(gates[:], rw.rearrange("b (p t) o -> p b (t o)", t=PACK))
         qm_rest_raw = load_rows(qm[0][:, P:], "qm0b")
         q_next_raw = load_rows(qT[1], "q1")
-        do_next_raw = load_rows(doT[1], "do1")
+        do_next_raw = load_rows(doT[1], "do1", AT_DO_NEXT_RAW)
         qm_next_raw = load_rows(qm[1], "qm1")
         windows = [zero_window(nc.vector, f"win{c}") for c in range(2)]
 
@@ -199,7 +213,7 @@ def tile_attend_gat_tnh_k_kernel(
         deal_vector(grouped, do_raw, 0, VECTOR_SHARE)
         v_bytes_next = gather(v_plane, U8, N, N, "vs1", AT_V_SCALES_NEXT)
         p = weights("p0", q_mx, keys, AT_TANH)
-        ds_mx = mx_tiles("ds0", 3 * HALF)
+        ds_mx = mx_tiles("ds0", 5 * HALF)
         do_parts = [mx_tiles("do0_0", P), mx_tiles("do0_1", P), ds_mx]
         for part, (x0, x1) in zip(do_parts, ((0, P), (P, 2 * P), (2 * P, R))):
             quantize(part, 0, grouped[:, PACK * x0 : PACK * x1], E5M2)
@@ -228,6 +242,7 @@ def tile_attend_gat_tnh_k_kernel(
         quantize(qm_second, 0, grouped[:], E4M3)
         place(0, 0, product("a", qm_first, E4M3, 0, ds_mx, E5M2)[:, HALF:], "dk00a", AT_FIRST_STAGE)
         qm_last_grouped = group_gpsimd(qm_rest_raw[:, :, P:], "qm0cg", AT_QM_LAST)
+        qm_low_grouped = group_gpsimd(qm_next_raw[:, :, : 2 * P], "qm1ag", AT_QM_NEXT_LOW)
         grouped = tile([P, PACK * R], BF16, "q1g", AT_Q_NEXT)
         deal(grouped, q_next_raw, 0, R // 2)
         place(HALF, 0, product("a", qm_first, E4M3, 0, ds_mx, E5M2, HALF)[:, HALF:], "dk00b")
@@ -243,28 +258,46 @@ def tile_attend_gat_tnh_k_kernel(
         do_mx = mx_tiles("do1", R)
         quantize(do_mx, 0, grouped[:], E5M2)
         windows.append(zero_window(nc.gpsimd, "win3", AT_FOURTH_WINDOW))
-        place(0, 2, product("a", qm_last, E4M3, 0, ds_mx, E5M2, HALF)[:], "dk02")
-        p = weights("p1", q_mx, keys_next)
-        last_bank = product("a", qm_last, E4M3, 1, ds_mx, E5M2, HALF)
-        place(0, 3, last_bank[:, :HALF], "dk03a")
+        place(0, 2, product("a", qm_last, E4M3, 0, ds_mx, E5M2, HALF)[:], "dk02", AT_THIRD_STAGE)
 
-        dp_banks = [product("dp", do_mx, E5M2, t, values_next, E4M3) for t in range(PACK)]
-        for h in range(2):
-            square(p, h)
-        ds = tile([P, N * PACK], BF16, "ds1")
-        for h in range(2):
-            minus_ds(p, gated(1, dp_banks, h, f"x1{h}"), h, ds[:, h * HALF * PACK : (h + 1) * HALF * PACK])
-        ds_mx = mx_tiles("ds1", N)
-        quantize(ds_mx, 0, ds[:], E5M2)
-        qm_first_grouped = group(qm_next_raw[:, :, :P], "qm1a")
-        qm_first = mx_tiles("qm1a", P)
-        qm_rest_grouped = group(qm_next_raw[:, :, P:], "qm1b")
-        qm_rest = mx_tiles("qm1b", D - P)
-        quantize(qm_first, 0, qm_first_grouped[:], E4M3)
-        place(HALF, 3, last_bank[:, HALF:], "x11")
-        for x0, x1 in ((0, P), (P, D - P)):
-            quantize(qm_rest, x0, qm_rest_grouped[:, PACK * x0 : PACK * x1], E4M3)
-        qm_blocks = [(qm_first, 0), (qm_rest, 0), (qm_rest, 1), (qm_rest, 2)]
-        for c, (qm_mx, block) in enumerate(qm_blocks):
-            place(N, c, product("a", qm_mx, E4M3, block, ds_mx, E5M2)[:], f"dk1{c}")
+        banks = [product("dp", q_mx, E4M3, t, keys_next, E4M3) for t in range(PACK)]
+        dp_banks = [product("a", do_mx, E5M2, t, values_next, E4M3) for t in range(PACK)]
+        p_low = tile([P, 1, RUN, PACK, LINE], F32, "p10", AT_TANH_NEXT_LOW)
+        for t in range(PACK):
+            nc.scalar.activation(p_low[:, 0, :, t, :], by_lines(banks[t])[:, 0], ACT.Tanh)
+        square(p_low, 0)
+        p_high = tile([P, RUN, PACK, LINE], F32, "p11", AT_TANH_NEXT_HIGH)
+        for t in range(PACK):
+            nc.scalar.activation(p_high[:, :, t, :], banks[t][:, HALF:].rearrange("p (c i) -> p c i", i=LINE), ACT.Tanh)
+        x_low = gated(1, dp_banks, 0, "x10", AT_GATED_NEXT_LOW)
+        nc.scalar.activation(p_high[:], p_high[:], ACT.Square)
+        ds = tile([P, HALF * PACK], BF16, "ds10", AT_DS_NEXT_LOW)
+        minus_ds(p_low, x_low, 0, ds[:])
+        qm_low = tile([P, 2 * P], U32, "qm1a_codes", AT_QM_NEXT_LOW_CODES), tile([P, 2 * P], U8, "qm1a_scales")
+        quantize(qm_low, 0, qm_low_grouped[:], E4M3)
+        quantize(ds_mx, 3 * HALF, ds[:], E5M2)
+        place(0, 3, product("dp", qm_last, E4M3, 1, ds_mx, E5M2, HALF)[:], "dk03", AT_FOURTH_STAGE)
+        x_high = tile([P, RUN, PACK, LINE], F32, "x11", AT_GATED_NEXT_HIGH)
+        for t in range(PACK):
+            nc.scalar.activation(
+                x_high[:, :, t, :],
+                dp_banks[t][:, HALF:].rearrange("p (c i) -> p c i", i=LINE),
+                ACT.Copy,
+                scale=gates[:, 1, t : t + 1],
+            )
+        slope = tile([P, RUN, PACK, LINE], F32, "w11", AT_SLOPE)
+        nc.gpsimd.tensor_scalar(slope[:], p_high[:], 1.0, -1.0, ALU.mult, ALU.add)
+        ds = tile([P, HALF * PACK], BF16, "ds11")
+        nc.gpsimd.tensor_tensor(ds[:].rearrange("p (c i t) -> p c t i", i=LINE, t=PACK), slope[:], x_high[:], ALU.mult)
+        place(N, 0, product("dp", qm_low, E4M3, 0, ds_mx, E5M2, 2 * HALF)[:, HALF:], "dk10a")
+        qm_high_grouped = group(qm_next_raw[:, :, 2 * P :], "qm1bg", AT_QM_NEXT_HIGH)
+        quantize(ds_mx, 4 * HALF, ds[:], E5M2)
+        qm_high = tile([P, 2 * P], U32, "qm1b_codes", AT_QM_NEXT_HIGH_CODES), tile([P, 2 * P], U8, "qm1b_scales")
+        quantize(qm_high, 0, qm_high_grouped[:], E4M3)
+        place(N, 1, product("dp", qm_low, E4M3, 1, ds_mx, E5M2, 2 * HALF)[:, HALF:], "dk11a", AT_SIXTH_STAGE)
+        for c in range(2):
+            place(N + HALF, c, product("dp", qm_low, E4M3, c, ds_mx, E5M2, 3 * HALF)[:, HALF:], f"dk1{c}b")
+            nc.sync.dma_start(out[c * P : (c + 1) * P, :], windows[c][:])
+        for c in range(2, 4):
+            place(N, c, product("dp", qm_high, E4M3, c - 2, ds_mx, E5M2, 3 * HALF)[:], f"dk1{c}")
             nc.sync.dma_start(out[c * P : (c + 1) * P, :], windows[c][:])

@@ -30,16 +30,18 @@ AT_GATED_LOW = 0
 AT_QM_FIRST_CODES = 0
 AT_QM_SECOND = 3 * KIB
 AT_DS_HIGH = 4 * KIB
-AT_QM_LAST = 3 * KIB
+AT_QM_LAST = 3 * KIB + 512
 AT_GATED_HIGH = 8 * KIB
 AT_Q_NEXT = 7 * KIB
 AT_FIRST_STAGE = 11 * KIB
-AT_THIRD_WINDOW = 3 * KIB
+AT_K_PLANE = 48 * KIB
+AT_THIRD_WINDOW = 48 * KIB
+AT_QM_FIRST_RAW = 56 * KIB
 AT_DO_RAW = 36 * KIB
 AT_V_SCALES_NEXT = 36 * KIB
 AT_TANH = 38 * KIB
 AT_DO_NEXT = 38 * KIB
-AT_FOURTH_WINDOW = 38 * KIB
+AT_FOURTH_WINDOW = 56 * KIB
 AT_QM_NEXT_LOW = 11 * KIB
 AT_GATED_NEXT_LOW = 13 * KIB
 AT_QM_NEXT_LOW_CODES = 13 * KIB
@@ -47,13 +49,14 @@ AT_FOURTH_STAGE = 15 * KIB
 AT_DS_NEXT_LOW = 17 * KIB
 AT_SLOPE = 17 * KIB
 AT_DO_NEXT_RAW = 24 * KIB
-AT_TANH_NEXT_LOW = 22 * KIB
+AT_SECOND_STAGE = 25 * KIB
+AT_TANH_NEXT_LOW = 21 * KIB
 AT_THIRD_STAGE = 26 * KIB
 AT_TANH_NEXT_HIGH = 28 * KIB
-AT_QM_NEXT_HIGH = 22 * KIB
+AT_QM_NEXT_HIGH = 5 * KIB + 256
 AT_GATED_NEXT_HIGH = 32 * KIB
 AT_SIXTH_STAGE = 32 * KIB
-AT_QM_NEXT_HIGH_CODES = 33 * KIB
+AT_QM_NEXT_HIGH_CODES = 14 * KIB
 
 
 def tile_attend_gat_tnh_k_kernel(
@@ -76,8 +79,8 @@ def tile_attend_gat_tnh_k_kernel(
             nc.sync.dma_start(raw[:], src.rearrange("(p j) w -> p j w", j=PACK))
             return raw
 
-        def zero_plane(tag):
-            plane = tile([P, T // 4], I32, tag)
+        def zero_plane(tag, offset=None):
+            plane = tile([P, T // 4], I32, tag, offset)
             nc.vector.memset(plane[:], 0)
             return plane
 
@@ -181,7 +184,7 @@ def tile_attend_gat_tnh_k_kernel(
         offsets = keep.tile([P, B * N // GROUP], U16, name="offsets")
         nc.sync.dma_start(offsets[:], offs)
 
-        k_plane = zero_plane("k_plane")
+        k_plane = zero_plane("k_plane", AT_K_PLANE)
         v_plane = zero_plane("v_plane")
         k_pool = tile([P, T], I32, "k_pool")
         nc.sync.dma_start(k_pool[:, : T // 2], word_rows(k_words)[:, : T // 2])
@@ -192,7 +195,7 @@ def tile_attend_gat_tnh_k_kernel(
         do_raw = load_rows(doT[0], "do0", AT_DO_RAW)
         v_pool = tile([P, T], I32, "v_pool")
         nc.sync.dma_start(v_pool[:], word_rows(v_words))
-        qm_first_raw = load_rows(qm[0][:, :P], "qm0a")
+        qm_first_raw = load_rows(qm[0][:, :P], "qm0a", AT_QM_FIRST_RAW)
         gates = tile([P, B, PACK], F32, "gates")
         nc.sync.dma_start(gates[:], rw.rearrange("b (p t) o -> p b (t o)", t=PACK))
         qm_rest_raw = load_rows(qm[0][:, P:], "qm0b")
@@ -202,6 +205,7 @@ def tile_attend_gat_tnh_k_kernel(
         windows = [zero_window(nc.vector, f"win{c}") for c in range(2)]
 
         k_bytes = gather(k_plane, U8, 0, B * N, "ks")
+        windows.append(zero_window(nc.gpsimd, "win2", AT_THIRD_WINDOW))
         v_bytes = gather(v_plane, U8, 0, N, "vs0")
         grouped = tile([P, PACK * R], BF16, "q0g")
         deal(grouped, q_raw, 0, R)
@@ -222,6 +226,7 @@ def tile_attend_gat_tnh_k_kernel(
         dp_banks = [product("dp", part, E5M2, block, values, E4M3) for part, block in do_blocks]
         values_next = gather(v_pool, U32, N, N, "vw1"), v_bytes_next
         qm_first_grouped = group_gpsimd(qm_first_raw[:], "qm0ag")
+        windows.append(zero_window(nc.gpsimd, "win3", AT_FOURTH_WINDOW))
         keys_next = gather(k_pool, U32, N, N, "do0_0_scales"), k_bytes[:, N:]
 
         gated_halves = []
@@ -251,53 +256,62 @@ def tile_attend_gat_tnh_k_kernel(
         quantize(qm_last, 0, qm_last_grouped[:], E4M3)
         q_mx = mx_tiles("q1", R)
         quantize(q_mx, 0, grouped[:], E4M3)
-        windows.append(zero_window(nc.gpsimd, "win2", AT_THIRD_WINDOW))
-        place(0, 1, product("a", qm_second, E4M3, 0, ds_mx, E5M2, HALF)[:], "dk01")
+        qm_high_grouped = group_gpsimd(qm_next_raw[:, :, 2 * P :], "qm1bg", AT_QM_NEXT_HIGH)
+        bank = product("a", qm_second, E4M3, 0, ds_mx, E5M2, HALF)
+        place(0, 1, bank[:, :HALF], "dk01a")
         grouped = tile([P, PACK * R], BF16, "do1g", AT_DO_NEXT)
         deal(grouped, do_next_raw, 0, R)
         do_mx = mx_tiles("do1", R)
         quantize(do_mx, 0, grouped[:], E5M2)
-        windows.append(zero_window(nc.gpsimd, "win3", AT_FOURTH_WINDOW))
+        place(HALF, 1, bank[:, HALF:], "dk01b", AT_SECOND_STAGE)
         place(0, 2, product("a", qm_last, E4M3, 0, ds_mx, E5M2, HALF)[:], "dk02", AT_THIRD_STAGE)
+
+        def half_lines(bank, h):
+            return bank[:, h * HALF : (h + 1) * HALF].rearrange("p (c i) -> p c i", i=LINE)
+
+        def gated_lines(h, tag, offset):
+            x = tile([P, RUN, PACK, LINE], F32, tag, offset)
+            for t in range(PACK):
+                nc.scalar.activation(x[:, :, t, :], half_lines(dp_banks[t], h), ACT.Copy, scale=gates[:, 1, t : t + 1])
+            return x
+
+        def minus_ds_gpsimd(p, x, tag, slope_offset, ds_offset):
+            slope = tile([P, RUN, PACK, LINE], F32, f"w{tag}", slope_offset)
+            nc.gpsimd.tensor_scalar(slope[:], p[:], 1.0, -1.0, ALU.mult, ALU.add)
+            ds = tile([P, HALF * PACK], BF16, f"ds{tag}", ds_offset)
+            nc.gpsimd.tensor_tensor(ds[:].rearrange("p (c i t) -> p c t i", i=LINE, t=PACK), slope[:], x[:], ALU.mult)
+            return ds
 
         banks = [product("dp", q_mx, E4M3, t, keys_next, E4M3) for t in range(PACK)]
         dp_banks = [product("a", do_mx, E5M2, t, values_next, E4M3) for t in range(PACK)]
-        p_low = tile([P, 1, RUN, PACK, LINE], F32, "p10", AT_TANH_NEXT_LOW)
-        for t in range(PACK):
-            nc.scalar.activation(p_low[:, 0, :, t, :], by_lines(banks[t])[:, 0], ACT.Tanh)
-        square(p_low, 0)
+        p_low = tile([P, RUN, PACK, LINE], F32, "p10", AT_TANH_NEXT_LOW)
         p_high = tile([P, RUN, PACK, LINE], F32, "p11", AT_TANH_NEXT_HIGH)
         for t in range(PACK):
-            nc.scalar.activation(p_high[:, :, t, :], banks[t][:, HALF:].rearrange("p (c i) -> p c i", i=LINE), ACT.Tanh)
-        x_low = gated(1, dp_banks, 0, "x10", AT_GATED_NEXT_LOW)
+            nc.scalar.activation(p_low[:, :, t, :], half_lines(banks[t], 0), ACT.Tanh)
+        nc.scalar.activation(p_high[:, :, 0, :], half_lines(banks[0], 1), ACT.Tanh)
+        nc.scalar.activation(p_low[:], p_low[:], ACT.Square)
+        x_low = gated_lines(0, "x10", AT_GATED_NEXT_LOW)
+        ds = minus_ds_gpsimd(p_low, x_low, "10", None, AT_DS_NEXT_LOW)
+        bank = product("dp", qm_last, E4M3, 1, ds_mx, E5M2, HALF)
+        place(0, 3, bank[:, :HALF], "dk03a")
+        for t in range(1, PACK):
+            nc.scalar.activation(p_high[:, :, t, :], half_lines(banks[t], 1), ACT.Tanh)
         nc.scalar.activation(p_high[:], p_high[:], ACT.Square)
-        ds = tile([P, HALF * PACK], BF16, "ds10", AT_DS_NEXT_LOW)
-        minus_ds(p_low, x_low, 0, ds[:])
         qm_low = tile([P, 2 * P], U32, "qm1a_codes", AT_QM_NEXT_LOW_CODES), tile([P, 2 * P], U8, "qm1a_scales")
         quantize(qm_low, 0, qm_low_grouped[:], E4M3)
-        quantize(ds_mx, 3 * HALF, ds[:], E5M2)
-        place(0, 3, product("dp", qm_last, E4M3, 1, ds_mx, E5M2, HALF)[:], "dk03", AT_FOURTH_STAGE)
-        x_high = tile([P, RUN, PACK, LINE], F32, "x11", AT_GATED_NEXT_HIGH)
-        for t in range(PACK):
-            nc.scalar.activation(
-                x_high[:, :, t, :],
-                dp_banks[t][:, HALF:].rearrange("p (c i) -> p c i", i=LINE),
-                ACT.Copy,
-                scale=gates[:, 1, t : t + 1],
-            )
-        slope = tile([P, RUN, PACK, LINE], F32, "w11", AT_SLOPE)
-        nc.gpsimd.tensor_scalar(slope[:], p_high[:], 1.0, -1.0, ALU.mult, ALU.add)
-        ds = tile([P, HALF * PACK], BF16, "ds11")
-        nc.gpsimd.tensor_tensor(ds[:].rearrange("p (c i t) -> p c t i", i=LINE, t=PACK), slope[:], x_high[:], ALU.mult)
-        place(N, 0, product("dp", qm_low, E4M3, 0, ds_mx, E5M2, 2 * HALF)[:, HALF:], "dk10a")
-        qm_high_grouped = group(qm_next_raw[:, :, 2 * P :], "qm1bg", AT_QM_NEXT_HIGH)
-        quantize(ds_mx, 4 * HALF, ds[:], E5M2)
         qm_high = tile([P, 2 * P], U32, "qm1b_codes", AT_QM_NEXT_HIGH_CODES), tile([P, 2 * P], U8, "qm1b_scales")
         quantize(qm_high, 0, qm_high_grouped[:], E4M3)
-        place(N, 1, product("dp", qm_low, E4M3, 1, ds_mx, E5M2, 2 * HALF)[:, HALF:], "dk11a", AT_SIXTH_STAGE)
+        quantize(ds_mx, 3 * HALF, ds[:], E5M2)
+        place(HALF, 3, bank[:, HALF:], "dk03b", AT_FOURTH_STAGE)
+        x_high = gated_lines(1, "x11", AT_GATED_NEXT_HIGH)
+        ds = minus_ds_gpsimd(p_high, x_high, "11", AT_SLOPE, None)
+        qm_blocks = [(qm_low, 0), (qm_low, 1), (qm_high, 0), (qm_high, 1)]
         for c in range(2):
-            place(N + HALF, c, product("dp", qm_low, E4M3, c, ds_mx, E5M2, 3 * HALF)[:, HALF:], f"dk1{c}b")
+            place(N, c, product("dp", qm_blocks[c][0], E4M3, qm_blocks[c][1], ds_mx, E5M2, 2 * HALF)[:, HALF:], f"dk1{c}a")
+        quantize(ds_mx, 4 * HALF, ds[:], E5M2)
+        place(N, 2, product("dp", qm_high, E4M3, 0, ds_mx, E5M2, 2 * HALF)[:, HALF:], "dk12a", AT_SIXTH_STAGE)
+        for c in range(3):
+            place(N + HALF, c, product("dp", qm_blocks[c][0], E4M3, qm_blocks[c][1], ds_mx, E5M2, 3 * HALF)[:, HALF:], f"dk1{c}b")
             nc.sync.dma_start(out[c * P : (c + 1) * P, :], windows[c][:])
-        for c in range(2, 4):
-            place(N, c, product("dp", qm_high, E4M3, c - 2, ds_mx, E5M2, 3 * HALF)[:], f"dk1{c}")
-            nc.sync.dma_start(out[c * P : (c + 1) * P, :], windows[c][:])
+        place(N, 3, product("dp", qm_high, E4M3, 1, ds_mx, E5M2, 3 * HALF)[:], "dk13")
+        nc.sync.dma_start(out[3 * P :, :], windows[3][:])

@@ -15,48 +15,16 @@ E4M3 = mybir.dt.float8_e4m3fn_x4
 E5M2 = mybir.dt.float8_e5m2_x4
 ACT = mybir.ActivationFunctionType
 ALU = mybir.AluOpType
+BYTES_OF = {F32: 4, BF16: 2, I32: 4, U32: 4, U8: 1}
 
 P = 128
 PACK = 4
 LINE = 4
 GROUP = 16
-BANKS = 4
 HALF = N // 2
-RUN = HALF // LINE
-VECTOR_SHARE = 320
-
+QUARTER = N // 4
+BANK_BYTES = 2048
 KIB = 1024
-AT_GATED_LOW = 0
-AT_QM_FIRST_CODES = 0
-AT_QM_SECOND = 3 * KIB
-AT_DS_HIGH = 4 * KIB
-AT_QM_LAST = 3 * KIB + 512
-AT_GATED_HIGH = 8 * KIB
-AT_Q_NEXT = 7 * KIB
-AT_FIRST_STAGE = 11 * KIB
-AT_K_PLANE = 48 * KIB
-AT_THIRD_WINDOW = 48 * KIB
-AT_QM_FIRST_RAW = 56 * KIB
-AT_DO_RAW = 36 * KIB
-AT_V_SCALES_NEXT = 36 * KIB
-AT_TANH = 38 * KIB
-AT_DO_NEXT = 38 * KIB
-AT_FOURTH_WINDOW = 56 * KIB
-AT_QM_NEXT_LOW = 11 * KIB
-AT_GATED_NEXT_LOW = 13 * KIB
-AT_QM_NEXT_LOW_CODES = 13 * KIB
-AT_FOURTH_STAGE = 15 * KIB
-AT_DS_NEXT_LOW = 17 * KIB
-AT_SLOPE = 17 * KIB
-AT_DO_NEXT_RAW = 24 * KIB
-AT_SECOND_STAGE = 25 * KIB
-AT_TANH_NEXT_LOW = 21 * KIB
-AT_THIRD_STAGE = 26 * KIB
-AT_TANH_NEXT_HIGH = 28 * KIB
-AT_QM_NEXT_HIGH = 5 * KIB + 256
-AT_GATED_NEXT_HIGH = 32 * KIB
-AT_SIXTH_STAGE = 32 * KIB
-AT_QM_NEXT_HIGH_CODES = 14 * KIB
 
 
 def tile_attend_gat_tnh_k_kernel(
@@ -65,37 +33,52 @@ def tile_attend_gat_tnh_k_kernel(
     nc = tc.nc
     with ExitStack() as ctx:
         keep = ctx.enter_context(tc.tile_pool(name="keep", bufs=1))
-        sb = ctx.enter_context(tc.tile_pool(name="sb", bufs=1))
         placed = ctx.enter_context(tc.tile_pool(name="placed", bufs=1))
         psum = ctx.enter_context(tc.psum_pool(name="psum", bufs=1))
+        where = {"end": 0}
 
-        def tile(shape, dtype, tag, offset=None):
-            if offset is None:
-                return sb.tile(shape, dtype, name=tag, tag=tag, align_bytes=64)
-            return placed.tile(shape, dtype, name=tag, tag=tag, align_bytes=64, offset=offset)
+        def tile(shape, dtype, name, on=None, skip=0, room=0):
+            size = BYTES_OF[dtype]
+            for extent in shape[1:]:
+                size = size * extent
+            if on is None:
+                where[name] = where["end"]
+                where["end"] = where["end"] + (max(size, room) + 63) // 64 * 64
+            else:
+                where[name] = where[on] + skip
+            return placed.tile(shape, dtype, name=name, tag=name, align_bytes=64, offset=where[name])
 
-        def load_rows(src, tag, offset=None):
-            raw = tile([P, PACK, src.shape[1]], F32, tag, offset)
+        def bank(index, name):
+            return psum.tile([P, N], F32, name=name, tag=f"bank{index}")
+
+        def load_rows(src, name):
+            raw = tile([P, PACK, src.shape[1]], F32, name)
             nc.sync.dma_start(raw[:], src.rearrange("(p j) w -> p j w", j=PACK))
             return raw
 
-        def zero_plane(tag, offset=None):
-            plane = tile([P, T // 4], I32, tag, offset)
+        def zero_plane(name):
+            plane = tile([P, T // 4], I32, name)
             nc.vector.memset(plane[:], 0)
             return plane
+
+        def zero_window(engine, c, on=None, skip=0):
+            window = tile([P, T], F32, f"win{c}", on, skip)
+            engine.memset(window[:], 0.0)
+            return window
+
+        def region(name, size):
+            where[name] = where["end"]
+            where["end"] = where["end"] + size
 
         def load_scales(plane, src):
             rows = src[0].bitcast(I32)
             for f in range(4):
                 nc.sync.dma_start(plane[f:P:32, :], rows[f:16:4, :])
 
-        def word_rows(src):
-            return src[0].rearrange("p n j -> p (n j)").bitcast(I32)
-
-        def zero_window(engine, tag, offset=None):
-            window = tile([P, T], F32, tag, offset)
-            engine.memset(window[:], 0.0)
-            return window
+        def load_words(src, name):
+            pool_tile = tile([P, T], I32, name)
+            nc.sync.dma_start(pool_tile[:], src[0].rearrange("p n j -> p (n j)").bitcast(I32))
+            return pool_tile
 
         def mx_tiles(name, words):
             return tile([P, words], U32, f"{name}_codes"), tile([P, words], U8, f"{name}_scales")
@@ -107,211 +90,177 @@ def tile_attend_gat_tnh_k_kernel(
         def listed(first, count):
             return offsets[:, first // GROUP : (first + count) // GROUP]
 
-        def gather(pool_tile, dtype, first, count, tag, offset=None):
-            got = tile([P, count], dtype, tag, offset)
+        def gather(pool_tile, dtype, first, count, name, on=None, skip=0):
+            got = tile([P, count], dtype, name, on, skip)
             nc.vector.tensor_copy(got[:], pool_tile[:].bitcast(dtype).indirect(listed(first, count)))
             return got
 
-        def deal(grouped, raw, x0, x1):
-            dst = grouped[:].rearrange("p (t m j) -> p m j t", t=PACK, j=PACK)[:, x0 // PACK : x1 // PACK]
-            nc.scalar.copy(dst, raw[:, :, x0:x1].rearrange("p j (m t) -> p m j t", t=PACK))
-
-        def deal_vector(grouped, raw, x0, x1):
-            dst = grouped[:].rearrange("p (u v m j) -> p u m j v", u=2, v=2, j=PACK)[:, :, x0 // PACK : x1 // PACK]
-            nc.vector.tensor_copy(dst, raw[:, :, x0:x1].rearrange("p j (m u v) -> p u m j v", u=2, v=2))
-
-        def group(piece, tag, offset=None):
-            grouped = tile([P, PACK * piece.shape[2]], BF16, tag, offset)
-            dst = grouped[:].rearrange("p (c i j) -> p c j i", i=LINE, j=PACK)
-            nc.scalar.copy(dst, piece.rearrange("p j (c i) -> p c j i", i=LINE))
+        def deal_scalar(raw, name):
+            grouped = tile([P, PACK * R], BF16, name, room=8 * KIB)
+            dst = grouped[:].rearrange("p (t m j) -> p m j t", t=PACK, j=PACK)
+            nc.scalar.copy(dst, raw[:].rearrange("p j (m t) -> p m j t", t=PACK))
             return grouped
 
-        def group_gpsimd(piece, tag, offset=None):
-            grouped = tile([P, PACK * piece.shape[2]], BF16, tag, offset)
+        def deal_vector(raw, name, on=None):
+            grouped = tile([P, PACK * R], BF16, name, on)
+            dst = grouped[:].rearrange("p (u v m j) -> p u m j v", u=2, v=2, j=PACK)
+            nc.vector.tensor_copy(dst, raw[:].rearrange("p j (m u v) -> p u m j v", u=2, v=2))
+            return grouped
+
+        def group_gpsimd(raw, name, on=None, skip=0):
+            grouped = tile([P, PACK * raw.shape[2]], BF16, name, on, skip)
             dst = grouped[:].rearrange("p (c j) -> p c j", j=PACK)
-            nc.gpsimd.tensor_scalar(dst, piece.rearrange("p j c -> p c j"), 1.0, 0.0, ALU.mult, ALU.add)
+            nc.gpsimd.tensor_scalar(dst, raw[:].rearrange("p j c -> p c j"), 1.0, 0.0, ALU.mult, ALU.add)
             return grouped
 
-        def product(ring, lhs, lhs_fmt, block, rhs, rhs_fmt, x0=0):
-            bank = psum.tile([P, N], F32, name=f"{ring}_bank", tag=ring, bufs=BANKS)
+        def product(dst, lhs, lhs_fmt, block, codes, scales, rhs_fmt):
             cols = slice(block * P, (block + 1) * P)
             nc.tensor.matmul_mx(
-                out=bank[:],
+                out=dst,
                 lhsT=lhs[0][:, cols].bitcast(lhs_fmt),
                 lhsT_scale=lhs[1][:, cols],
-                rhs=rhs[0][:, x0 : x0 + N].bitcast(rhs_fmt),
-                rhs_scale=rhs[1][:, x0 : x0 + N],
+                rhs=codes.bitcast(rhs_fmt),
+                rhs_scale=scales,
                 start=True,
                 stop=True,
             )
-            return bank
 
-        def by_lines(bank):
-            return bank[:].rearrange("p (h i c) -> p h c i", h=2, i=LINE)
-
-        def weights(tag, q_mx, k_mx, offset=None):
-            p = tile([P, 2, RUN, PACK, LINE], F32, tag, offset)
+        def slope(b, h, q_mx, k_codes, k_bytes):
+            w = tile([P, HALF // LINE, PACK, LINE], F32, f"w{b}{h}")
+            for pair in range(2):
+                scores = bank(pair, f"a{b}{h}{pair}")
+                for u in range(2):
+                    product(scores[:, u * HALF : (u + 1) * HALF], q_mx, E4M3, 2 * pair + u, k_codes, k_bytes, E4M3)
+                lines = scores[:].rearrange("p (t c i) -> p c t i", t=2, i=LINE)
+                nc.scalar.activation(w[:, :, 2 * pair : 2 * pair + 2, :], lines, ACT.Tanh)
+            nc.scalar.activation(w[:], w[:], ACT.Square)
             for t in range(PACK):
-                bank = product("a", q_mx, E4M3, t, k_mx, E4M3)
-                nc.scalar.activation(p[:, :, :, t, :], by_lines(bank), ACT.Tanh)
-            return p
+                col = slice(b * PACK + t, b * PACK + t + 1)
+                nc.scalar.activation(w[:, :, t, :], w[:, :, t, :], ACT.Identity, scale=minus_gates[:, col], bias=gates[:, col])
+            return w
 
-        def square(p, h):
-            nc.scalar.activation(p[:, h], p[:, h], ACT.Square)
+        def form_ds(b, h, w, do_mx, v_codes, v_bytes, room=0, on=None, skip=0):
+            ds = tile([P, HALF * PACK], BF16, f"ds{b}{h}", on, skip, room)
+            for u in range(2):
+                dp = bank(2 + u, f"dp{b}{h}{u}")
+                cols = slice(u * QUARTER, (u + 1) * QUARTER)
+                for t in range(PACK):
+                    product(dp[:, t * QUARTER : (t + 1) * QUARTER], do_mx, E5M2, t, v_codes[:, cols], v_bytes[:, cols], E4M3)
+                runs = QUARTER // LINE
+                nc.vector.tensor_tensor(
+                    ds[:, u * N : (u + 1) * N].rearrange("p (c i t) -> p c t i", i=LINE, t=PACK),
+                    w[:, u * runs : (u + 1) * runs],
+                    dp[:].rearrange("p (t c i) -> p c t i", t=PACK, i=LINE),
+                    ALU.mult,
+                )
+            return ds
 
-        def gated(b, dp_banks, h, tag, offset=None):
-            x = tile([P, RUN, PACK, LINE], F32, tag, offset)
-            for t in range(PACK):
-                nc.scalar.activation(x[:, :, t, :], by_lines(dp_banks[t])[:, h], ACT.Copy, scale=gates[:, b, t : t + 1])
-            return x
+        def dk(index, c, b, x0, count):
+            dst = bank(index, f"dk{c}{b}{x0}")[:, :count]
+            cols = slice(x0, x0 + count)
+            product(dst, qm_mx[b][c // 2], E4M3, c % 2, ds_mx[b][0][:, cols], ds_mx[b][1][:, cols], E5M2)
+            return dst
 
-        def minus_ds(p, x, h, ds):
-            nc.vector.scalar_tensor_tensor(
-                out=ds.rearrange("p (i y) -> p y i", i=LINE),
-                in0=p[:, h].rearrange("p c t i -> p (c t) i"),
-                scalar=1.0,
-                in1=x[:].rearrange("p c t i -> p (c t) i"),
-                op0=ALU.subtract,
-                op1=ALU.mult,
-            )
+        def stage(engine, part, name, on=None):
+            staged = tile([P, part.shape[1]], F32, name, on, room=N * 4)
+            if engine is nc.scalar:
+                nc.scalar.copy(staged[:], part)
+            else:
+                nc.vector.tensor_copy(staged[:], part)
+            return staged
 
-        def place(first, c, part, tag, offset=None):
-            count = part.shape[1]
-            staged = tile([P, count], F32, tag, offset)
-            nc.scalar.activation(staged[:], part, ACT.Copy, scale=-1.0)
-            nc.vector.tensor_copy(windows[c][:].indirect(listed(first, count)), staged[:])
+        def scatter(engine, c, first, staged):
+            if engine is nc.scalar:
+                for x0 in range(0, staged.shape[1], HALF):
+                    nc.scalar.activation(windows[c][:].indirect(listed(first + x0, HALF)), staged[:, x0 : x0 + HALF], ACT.Copy)
+            else:
+                nc.vector.tensor_copy(windows[c][:].indirect(listed(first, staged.shape[1])), staged[:])
+
+        def store(c):
+            nc.sync.dma_start(out[c * P : (c + 1) * P, :], windows[c][:])
 
         offsets = keep.tile([P, B * N // GROUP], U16, name="offsets")
         nc.sync.dma_start(offsets[:], offs)
 
-        k_plane = zero_plane("k_plane", AT_K_PLANE)
+        k_plane = zero_plane("k_plane")
         v_plane = zero_plane("v_plane")
-        k_pool = tile([P, T], I32, "k_pool")
-        nc.sync.dma_start(k_pool[:, : T // 2], word_rows(k_words)[:, : T // 2])
-        load_scales(k_plane, k_scales)
         q_raw = load_rows(qT[0], "q0")
+        load_scales(k_plane, k_scales)
+        k_pool = load_words(k_words, "k_pool")
+        gates = tile([P, B * PACK], F32, "gates")
+        nc.sync.dma_start(gates[:].rearrange("p (b t) -> p b t", b=B), rw.rearrange("b (p t) o -> p b (t o)", t=PACK))
         load_scales(v_plane, v_scales)
-        nc.sync.dma_start(k_pool[:, T // 2 :], word_rows(k_words)[:, T // 2 :])
-        do_raw = load_rows(doT[0], "do0", AT_DO_RAW)
-        v_pool = tile([P, T], I32, "v_pool")
-        nc.sync.dma_start(v_pool[:], word_rows(v_words))
-        qm_first_raw = load_rows(qm[0][:, :P], "qm0a", AT_QM_FIRST_RAW)
-        gates = tile([P, B, PACK], F32, "gates")
-        nc.sync.dma_start(gates[:], rw.rearrange("b (p t) o -> p b (t o)", t=PACK))
-        qm_rest_raw = load_rows(qm[0][:, P:], "qm0b")
+        do_raw = load_rows(doT[0], "do0")
+        v_pool = load_words(v_words, "v_pool")
+        qm_raw = {(0, 0): load_rows(qm[0][:, :HALF], "qm00")}
         q_next_raw = load_rows(qT[1], "q1")
-        do_next_raw = load_rows(doT[1], "do1", AT_DO_NEXT_RAW)
-        qm_next_raw = load_rows(qm[1], "qm1")
-        windows = [zero_window(nc.vector, f"win{c}") for c in range(2)]
+        do_next_raw = load_rows(doT[1], "do1")
+        for b, u in ((1, 0), (0, 1), (1, 1)):
+            qm_raw[b, u] = load_rows(qm[b][:, u * HALF : (u + 1) * HALF], f"qm{b}{u}")
+        windows = [zero_window(nc.vector, c) for c in range(2)]
+        qm_mx = [[mx_tiles(f"qm{b}{u}", HALF) for u in range(2)] for b in range(B)]
+        ds_mx = [mx_tiles(f"ds{b}", N) for b in range(B)]
 
         k_bytes = gather(k_plane, U8, 0, B * N, "ks")
-        windows.append(zero_window(nc.gpsimd, "win2", AT_THIRD_WINDOW))
-        v_bytes = gather(v_plane, U8, 0, N, "vs0")
-        grouped = tile([P, PACK * R], BF16, "q0g")
-        deal(grouped, q_raw, 0, R)
-        keys = gather(k_pool, U32, 0, N, "kw0"), k_bytes[:, :N]
+        grouped = deal_scalar(q_raw, "q0g")
+        minus_gates = tile([P, B * PACK], F32, "minus_gates")
+        nc.scalar.mul(minus_gates[:], gates[:], -1.0)
         q_mx = mx_tiles("q0", R)
         quantize(q_mx, 0, grouped[:], E4M3)
-        grouped = tile([P, PACK * R], BF16, "do0g")
-        deal(grouped, do_raw, VECTOR_SHARE, R)
-        deal_vector(grouped, do_raw, 0, VECTOR_SHARE)
-        v_bytes_next = gather(v_plane, U8, N, N, "vs1", AT_V_SCALES_NEXT)
-        p = weights("p0", q_mx, keys, AT_TANH)
-        ds_mx = mx_tiles("ds0", 5 * HALF)
-        do_parts = [mx_tiles("do0_0", P), mx_tiles("do0_1", P), ds_mx]
-        for part, (x0, x1) in zip(do_parts, ((0, P), (P, 2 * P), (2 * P, R))):
-            quantize(part, 0, grouped[:, PACK * x0 : PACK * x1], E5M2)
-        values = gather(v_pool, U32, 0, N, "vw0"), v_bytes
-        do_blocks = [(do_parts[0], 0), (do_parts[1], 0), (ds_mx, 0), (ds_mx, 1)]
-        dp_banks = [product("dp", part, E5M2, block, values, E4M3) for part, block in do_blocks]
-        values_next = gather(v_pool, U32, N, N, "vw1"), v_bytes_next
-        qm_first_grouped = group_gpsimd(qm_first_raw[:], "qm0ag")
-        windows.append(zero_window(nc.gpsimd, "win3", AT_FOURTH_WINDOW))
-        keys_next = gather(k_pool, U32, N, N, "do0_0_scales"), k_bytes[:, N:]
+        windows.append(zero_window(nc.gpsimd, 2, on="q0g"))
+        keys = [gather(k_pool, U32, h * HALF, HALF, f"kw0{h}") for h in range(2)]
+        v_bytes = gather(v_plane, U8, 0, N, "vs0")
+        w = [slope(0, h, q_mx, keys[h][:], k_bytes[:, h * HALF : (h + 1) * HALF]) for h in range(2)]
+        grouped = deal_vector(do_raw, "do0g")
+        do_mx = mx_tiles("do0", R)
+        quantize(do_mx, 0, grouped[:], E5M2)
+        values = [gather(v_pool, U32, h * HALF, HALF, f"vw0{h}") for h in range(2)]
+        qm_grouped = group_gpsimd(qm_raw[0, 0], "qm00g")
+        region("first", 10 * KIB)
+        ds = form_ds(0, 0, w[0], do_mx, values[0], v_bytes[:, :HALF], on="first", skip=KIB)
+        quantize(qm_mx[0][0], 0, qm_grouped[:], E4M3)
+        quantize(ds_mx[0], 0, ds[:], E5M2)
+        scatter(nc.scalar, 0, 0, stage(nc.scalar, dk(4, 0, 0, 0, HALF), "sa0"))
+        keys_next = gather(k_pool, U32, N, N, "kw1", on="first")
+        windows.append(zero_window(nc.gpsimd, 3, on="first", skip=2 * KIB))
+        ds = form_ds(0, 1, w[1], do_mx, values[1], v_bytes[:, HALF:], room=4 * KIB)
+        quantize(ds_mx[0], HALF, ds[:], E5M2)
+        scatter(nc.scalar, 1, 0, stage(nc.scalar, dk(5, 1, 0, 0, HALF), "sa1"))
 
-        gated_halves = []
-        for h, offset in enumerate((AT_GATED_LOW, AT_GATED_HIGH)):
-            square(p, h)
-            gated_halves.append(gated(0, dp_banks, h, f"x0{h}", offset))
-        ds = tile([P, HALF * PACK], BF16, "ds00")
-        minus_ds(p, gated_halves[0], 0, ds[:])
-        qm_first = tile([P, P], U32, "qm0a_codes", AT_QM_FIRST_CODES), tile([P, P], U8, "qm0a_scales")
-        quantize(qm_first, 0, qm_first_grouped[:], E4M3)
-        quantize(ds_mx, HALF, ds[:], E5M2)
-        ds = tile([P, HALF * PACK], BF16, "ds01", AT_DS_HIGH)
-        minus_ds(p, gated_halves[1], 1, ds[:])
-        quantize(ds_mx, 2 * HALF, ds[:], E5M2)
-
-        grouped = group(qm_rest_raw[:, :, :P], "qm0bg", AT_QM_SECOND)
-        qm_second = mx_tiles("qm0b", P)
-        quantize(qm_second, 0, grouped[:], E4M3)
-        place(0, 0, product("a", qm_first, E4M3, 0, ds_mx, E5M2)[:, HALF:], "dk00a", AT_FIRST_STAGE)
-        qm_last_grouped = group_gpsimd(qm_rest_raw[:, :, P:], "qm0cg", AT_QM_LAST)
-        qm_low_grouped = group_gpsimd(qm_next_raw[:, :, : 2 * P], "qm1ag", AT_QM_NEXT_LOW)
-        grouped = tile([P, PACK * R], BF16, "q1g", AT_Q_NEXT)
-        deal(grouped, q_next_raw, 0, R // 2)
-        place(HALF, 0, product("a", qm_first, E4M3, 0, ds_mx, E5M2, HALF)[:, HALF:], "dk00b")
-        deal(grouped, q_next_raw, R // 2, R)
-        qm_last = mx_tiles("qm0c", 2 * P)
-        quantize(qm_last, 0, qm_last_grouped[:], E4M3)
+        grouped = deal_vector(q_next_raw, "q1g", on="ds01")
         q_mx = mx_tiles("q1", R)
         quantize(q_mx, 0, grouped[:], E4M3)
-        qm_high_grouped = group_gpsimd(qm_next_raw[:, :, 2 * P :], "qm1bg", AT_QM_NEXT_HIGH)
-        bank = product("a", qm_second, E4M3, 0, ds_mx, E5M2, HALF)
-        place(0, 1, bank[:, :HALF], "dk01a")
-        grouped = tile([P, PACK * R], BF16, "do1g", AT_DO_NEXT)
-        deal(grouped, do_next_raw, 0, R)
+        w = [
+            slope(1, h, q_mx, keys_next[:, h * HALF : (h + 1) * HALF], k_bytes[:, N + h * HALF : N + (h + 1) * HALF])
+            for h in range(2)
+        ]
+        grouped = deal_vector(do_next_raw, "do1g", on="q1g")
+        v_bytes = gather(v_plane, U8, N, N, "vs1", on="do1")
+        qm_grouped = group_gpsimd(qm_raw[1, 0], "qm10g", on="do1", skip=KIB)
         do_mx = mx_tiles("do1", R)
         quantize(do_mx, 0, grouped[:], E5M2)
-        place(HALF, 1, bank[:, HALF:], "dk01b", AT_SECOND_STAGE)
-        place(0, 2, product("a", qm_last, E4M3, 0, ds_mx, E5M2, HALF)[:], "dk02", AT_THIRD_STAGE)
-
-        def half_lines(bank, h):
-            return bank[:, h * HALF : (h + 1) * HALF].rearrange("p (c i) -> p c i", i=LINE)
-
-        def gated_lines(h, tag, offset):
-            x = tile([P, RUN, PACK, LINE], F32, tag, offset)
-            for t in range(PACK):
-                nc.scalar.activation(x[:, :, t, :], half_lines(dp_banks[t], h), ACT.Copy, scale=gates[:, 1, t : t + 1])
-            return x
-
-        def minus_ds_gpsimd(p, x, tag, slope_offset, ds_offset):
-            slope = tile([P, RUN, PACK, LINE], F32, f"w{tag}", slope_offset)
-            nc.gpsimd.tensor_scalar(slope[:], p[:], 1.0, -1.0, ALU.mult, ALU.add)
-            ds = tile([P, HALF * PACK], BF16, f"ds{tag}", ds_offset)
-            nc.gpsimd.tensor_tensor(ds[:].rearrange("p (c i t) -> p c t i", i=LINE, t=PACK), slope[:], x[:], ALU.mult)
-            return ds
-
-        banks = [product("dp", q_mx, E4M3, t, keys_next, E4M3) for t in range(PACK)]
-        dp_banks = [product("a", do_mx, E5M2, t, values_next, E4M3) for t in range(PACK)]
-        p_low = tile([P, RUN, PACK, LINE], F32, "p10", AT_TANH_NEXT_LOW)
-        p_high = tile([P, RUN, PACK, LINE], F32, "p11", AT_TANH_NEXT_HIGH)
-        for t in range(PACK):
-            nc.scalar.activation(p_low[:, :, t, :], half_lines(banks[t], 0), ACT.Tanh)
-        nc.scalar.activation(p_high[:, :, 0, :], half_lines(banks[0], 1), ACT.Tanh)
-        nc.scalar.activation(p_low[:], p_low[:], ACT.Square)
-        x_low = gated_lines(0, "x10", AT_GATED_NEXT_LOW)
-        ds = minus_ds_gpsimd(p_low, x_low, "10", None, AT_DS_NEXT_LOW)
-        bank = product("dp", qm_last, E4M3, 1, ds_mx, E5M2, HALF)
-        place(0, 3, bank[:, :HALF], "dk03a")
-        for t in range(1, PACK):
-            nc.scalar.activation(p_high[:, :, t, :], half_lines(banks[t], 1), ACT.Tanh)
-        nc.scalar.activation(p_high[:], p_high[:], ACT.Square)
-        qm_low = tile([P, 2 * P], U32, "qm1a_codes", AT_QM_NEXT_LOW_CODES), tile([P, 2 * P], U8, "qm1a_scales")
-        quantize(qm_low, 0, qm_low_grouped[:], E4M3)
-        qm_high = tile([P, 2 * P], U32, "qm1b_codes", AT_QM_NEXT_HIGH_CODES), tile([P, 2 * P], U8, "qm1b_scales")
-        quantize(qm_high, 0, qm_high_grouped[:], E4M3)
-        quantize(ds_mx, 3 * HALF, ds[:], E5M2)
-        place(HALF, 3, bank[:, HALF:], "dk03b", AT_FOURTH_STAGE)
-        x_high = gated_lines(1, "x11", AT_GATED_NEXT_HIGH)
-        ds = minus_ds_gpsimd(p_high, x_high, "11", AT_SLOPE, None)
-        qm_blocks = [(qm_low, 0), (qm_low, 1), (qm_high, 0), (qm_high, 1)]
-        for c in range(2):
-            place(N, c, product("dp", qm_blocks[c][0], E4M3, qm_blocks[c][1], ds_mx, E5M2, 2 * HALF)[:, HALF:], f"dk1{c}a")
-        quantize(ds_mx, 4 * HALF, ds[:], E5M2)
-        place(N, 2, product("dp", qm_high, E4M3, 0, ds_mx, E5M2, 2 * HALF)[:, HALF:], "dk12a", AT_SIXTH_STAGE)
-        for c in range(3):
-            place(N + HALF, c, product("dp", qm_blocks[c][0], E4M3, qm_blocks[c][1], ds_mx, E5M2, 3 * HALF)[:, HALF:], f"dk1{c}b")
-            nc.sync.dma_start(out[c * P : (c + 1) * P, :], windows[c][:])
-        place(N, 3, product("dp", qm_high, E4M3, 1, ds_mx, E5M2, 3 * HALF)[:], "dk13")
-        nc.sync.dma_start(out[3 * P :, :], windows[3][:])
+        values = gather(v_pool, U32, N, N, "vw1", on="do1g")
+        qm_high_grouped = group_gpsimd(qm_raw[0, 1], "qm01g", on="do1g", skip=2 * KIB)
+        ds = form_ds(1, 0, w[0], do_mx, values[:, :HALF], v_bytes[:, :HALF], room=4 * KIB)
+        quantize(qm_mx[1][0], 0, qm_grouped[:], E4M3)
+        quantize(ds_mx[1], 0, ds[:], E5M2)
+        quantize(qm_mx[0][1], 0, qm_high_grouped[:], E4M3)
+        qm_high_grouped = group_gpsimd(qm_raw[1, 1], "qm11g", on="qm01g")
+        scatter(nc.vector, 1, HALF, stage(nc.vector, dk(6, 1, 0, HALF, HALF), "sv0", on="ds10"))
+        scatter(nc.scalar, 0, HALF, stage(nc.scalar, dk(0, 0, 0, HALF, HALF), "sa2", on="sa0"))
+        ds = form_ds(1, 1, w[1], do_mx, values[:, HALF:], v_bytes[:, HALF:])
+        quantize(qm_mx[1][1], 0, qm_high_grouped[:], E4M3)
+        quantize(ds_mx[1], HALF, ds[:], E5M2)
+        scatter(nc.scalar, 0, N, stage(nc.scalar, dk(5, 0, 1, 0, HALF), "sa3", on="sa1"))
+        scatter(nc.scalar, 0, N + HALF, stage(nc.scalar, dk(1, 0, 1, HALF, HALF), "sa4", on="sa0"))
+        store(0)
+        staged = [stage(nc.vector, dk(2, 1, 1, 0, N), "sv1", on="ds11"), stage(nc.vector, dk(7, 3, 0, 0, N), "sv2", on="ds10")]
+        scatter(nc.vector, 1, N, staged[0])
+        store(1)
+        scatter(nc.scalar, 2, 0, stage(nc.scalar, dk(4, 2, 0, 0, N), "sa5", on="sa1"))
+        last = stage(nc.vector, dk(3, 3, 1, 0, N), "sv3", on="ds11")
+        scatter(nc.vector, 3, 0, staged[1])
+        scatter(nc.scalar, 2, N, stage(nc.scalar, dk(0, 2, 1, 0, N), "sa6", on="sa0"))
+        store(2)
+        scatter(nc.vector, 3, N, last)
+        store(3)

@@ -51,8 +51,8 @@ def tile_attend_gat_tnh_k_kernel(
         def bank(index, name):
             return psum.tile([P, N], F32, name=name, tag=f"bank{index}")
 
-        def load_rows(src, name):
-            raw = tile([P, PACK, src.shape[1]], F32, name)
+        def load_rows(src, name, room=0):
+            raw = tile([P, PACK, src.shape[1]], F32, name, room=room)
             nc.sync.dma_start(raw[:], src.rearrange("(p j) w -> p j w", j=PACK))
             return raw
 
@@ -174,7 +174,7 @@ def tile_attend_gat_tnh_k_kernel(
                 for x0 in range(0, staged.shape[1], HALF):
                     nc.scalar.activation(windows[c][:].indirect(listed(first + x0, HALF)), staged[:, x0 : x0 + HALF], ACT.Copy)
             else:
-                nc.vector.tensor_copy(windows[c][:].indirect(listed(first, staged.shape[1])), staged[:])
+                nc.vector.tensor_copy(windows[c][:].indirect(listed(first, staged.shape[1])), staged)
 
         def store(c):
             nc.sync.dma_start(out[c * P : (c + 1) * P, :], windows[c][:])
@@ -187,27 +187,27 @@ def tile_attend_gat_tnh_k_kernel(
         q_raw = load_rows(qT[0], "q0")
         load_scales(k_plane, k_scales)
         k_pool = load_words(k_words, "k_pool")
-        gates = tile([P, B * PACK], F32, "gates")
+        gates = tile([P, B * PACK], F32, "gates", room=KIB)
         nc.sync.dma_start(gates[:].rearrange("p (b t) -> p b t", b=B), rw.rearrange("b (p t) o -> p b (t o)", t=PACK))
         load_scales(v_plane, v_scales)
         do_raw = load_rows(doT[0], "do0")
         v_pool = load_words(v_words, "v_pool")
         qm_raw = {(0, 0): load_rows(qm[0][:, :HALF], "qm00")}
-        q_next_raw = load_rows(qT[1], "q1")
+        q_next_raw = load_rows(qT[1], "q1", room=10 * KIB)
         do_next_raw = load_rows(doT[1], "do1")
         for b, u in ((1, 0), (0, 1), (1, 1)):
             qm_raw[b, u] = load_rows(qm[b][:, u * HALF : (u + 1) * HALF], f"qm{b}{u}")
-        windows = [zero_window(nc.vector, c) for c in range(2)]
+        windows = {c: zero_window(nc.vector, c) for c in range(2)}
         qm_mx = [[mx_tiles(f"qm{b}{u}", HALF) for u in range(2)] for b in range(B)]
         ds_mx = [mx_tiles(f"ds{b}", N) for b in range(B)]
 
         k_bytes = gather(k_plane, U8, 0, B * N, "ks")
         grouped = deal_scalar(q_raw, "q0g")
-        minus_gates = tile([P, B * PACK], F32, "minus_gates")
+        minus_gates = tile([P, B * PACK], F32, "minus_gates", room=KIB)
         nc.scalar.mul(minus_gates[:], gates[:], -1.0)
         q_mx = mx_tiles("q0", R)
         quantize(q_mx, 0, grouped[:], E4M3)
-        windows.append(zero_window(nc.gpsimd, 2, on="q0g"))
+        windows[2] = zero_window(nc.gpsimd, 2, on="q0g")
         keys = [gather(k_pool, U32, h * HALF, HALF, f"kw0{h}") for h in range(2)]
         v_bytes = gather(v_plane, U8, 0, N, "vs0")
         w = [slope(0, h, q_mx, keys[h][:], k_bytes[:, h * HALF : (h + 1) * HALF]) for h in range(2)]
@@ -220,47 +220,57 @@ def tile_attend_gat_tnh_k_kernel(
         ds = form_ds(0, 0, w[0], do_mx, values[0], v_bytes[:, :HALF], on="first", skip=KIB)
         quantize(qm_mx[0][0], 0, qm_grouped[:], E4M3)
         quantize(ds_mx[0], 0, ds[:], E5M2)
-        scatter(nc.scalar, 0, 0, stage(nc.scalar, dk(4, 0, 0, 0, HALF), "sa0"))
+        staged = [stage(nc.scalar, dk(4 + c, c, 0, 0, HALF), f"sa{c}") for c in range(2)]
+        for c in range(2):
+            scatter(nc.scalar, c, 0, staged[c][:])
         keys_next = gather(k_pool, U32, N, N, "kw1", on="first")
-        windows.append(zero_window(nc.gpsimd, 3, on="first", skip=2 * KIB))
-        ds = form_ds(0, 1, w[1], do_mx, values[1], v_bytes[:, HALF:], room=4 * KIB)
-        quantize(ds_mx[0], HALF, ds[:], E5M2)
-        scatter(nc.scalar, 1, 0, stage(nc.scalar, dk(5, 1, 0, 0, HALF), "sa1"))
-
-        grouped = deal_vector(q_next_raw, "q1g", on="ds01")
+        grouped = deal_vector(q_next_raw, "q1g", on="do0g")
+        ds = form_ds(0, 1, w[1], do_mx, values[1], v_bytes[:, HALF:], on="q1")
         q_mx = mx_tiles("q1", R)
         quantize(q_mx, 0, grouped[:], E4M3)
+        quantize(ds_mx[0], HALF, ds[:], E5M2)
+
         w = [
             slope(1, h, q_mx, keys_next[:, h * HALF : (h + 1) * HALF], k_bytes[:, N + h * HALF : N + (h + 1) * HALF])
             for h in range(2)
         ]
-        grouped = deal_vector(do_next_raw, "do1g", on="q1g")
+        grouped = deal_vector(do_next_raw, "do1g", on="ds01")
+        where["late"] = where["do1g"] + 2 * KIB
         v_bytes = gather(v_plane, U8, N, N, "vs1", on="do1")
         qm_grouped = group_gpsimd(qm_raw[1, 0], "qm10g", on="do1", skip=KIB)
         do_mx = mx_tiles("do1", R)
         quantize(do_mx, 0, grouped[:], E5M2)
-        values = gather(v_pool, U32, N, N, "vw1", on="do1g")
-        qm_high_grouped = group_gpsimd(qm_raw[0, 1], "qm01g", on="do1g", skip=2 * KIB)
-        ds = form_ds(1, 0, w[0], do_mx, values[:, :HALF], v_bytes[:, :HALF], room=4 * KIB)
+        values = [gather(v_pool, U32, N + h * HALF, HALF, f"vw1{h}", on="do1g", skip=h * KIB) for h in range(2)]
+        qm_high_grouped = group_gpsimd(qm_raw[0, 1], "qm01g", on="late")
+        ds = form_ds(1, 0, w[0], do_mx, values[0], v_bytes[:, :HALF])
         quantize(qm_mx[1][0], 0, qm_grouped[:], E4M3)
         quantize(ds_mx[1], 0, ds[:], E5M2)
+        part = dk(6, 1, 0, HALF, HALF)
+        staged = stage(nc.vector, part, "sv0", on="qm10g")
         quantize(qm_mx[0][1], 0, qm_high_grouped[:], E4M3)
-        qm_high_grouped = group_gpsimd(qm_raw[1, 1], "qm11g", on="qm01g")
-        scatter(nc.vector, 1, HALF, stage(nc.vector, dk(6, 1, 0, HALF, HALF), "sv0", on="ds10"))
-        scatter(nc.scalar, 0, HALF, stage(nc.scalar, dk(0, 0, 0, HALF, HALF), "sa2", on="sa0"))
-        ds = form_ds(1, 1, w[1], do_mx, values[:, HALF:], v_bytes[:, HALF:])
-        quantize(qm_mx[1][1], 0, qm_high_grouped[:], E4M3)
+        qm_high_grouped = group_gpsimd(qm_raw[1, 1], "qm11g", on="late")
+        scatter(nc.vector, 1, HALF, staged[:])
+        staged = [stage(nc.scalar, dk(0, 0, 0, HALF, HALF), "sa2", on="minus_gates"), stage(nc.scalar, dk(5, 0, 1, 0, HALF), "sa3", on="gates")]
+        scatter(nc.scalar, 0, HALF, staged[0][:])
+        scatter(nc.scalar, 0, N, staged[1][:])
+        ds = form_ds(1, 1, w[1], do_mx, values[1], v_bytes[:, HALF:])
+        third = dk(7, 2, 0, 0, N)
+        early = stage(nc.vector, third[:, :HALF], "sv1", on="w11")
         quantize(ds_mx[1], HALF, ds[:], E5M2)
-        scatter(nc.scalar, 0, N, stage(nc.scalar, dk(5, 0, 1, 0, HALF), "sa3", on="sa1"))
-        scatter(nc.scalar, 0, N + HALF, stage(nc.scalar, dk(1, 0, 1, HALF, HALF), "sa4", on="sa0"))
+        quantize(qm_mx[1][1], 0, qm_high_grouped[:], E4M3)
+        windows[3] = zero_window(nc.gpsimd, 3, on="qm11g")
+        scatter(nc.vector, 2, 0, early[:])
+        staged = [stage(nc.scalar, dk(1, 0, 1, HALF, HALF), "sa4", on="sa0"), stage(nc.scalar, third[:, HALF:], "sa5", on="sa1")]
+        scatter(nc.scalar, 0, N + HALF, staged[0][:])
         store(0)
-        staged = [stage(nc.vector, dk(2, 1, 1, 0, N), "sv1", on="ds11"), stage(nc.vector, dk(7, 3, 0, 0, N), "sv2", on="ds10")]
-        scatter(nc.vector, 1, N, staged[0])
+        late = [stage(nc.vector, dk(2, 1, 1, 0, N), "sv2", on="ds11"), stage(nc.vector, dk(4, 3, 0, 0, N), "sv3", on="w10")]
+        scatter(nc.vector, 1, N, late[0][:])
         store(1)
-        scatter(nc.scalar, 2, 0, stage(nc.scalar, dk(4, 2, 0, 0, N), "sa5", on="sa1"))
-        last = stage(nc.vector, dk(3, 3, 1, 0, N), "sv3", on="ds11")
-        scatter(nc.vector, 3, 0, staged[1])
-        scatter(nc.scalar, 2, N, stage(nc.scalar, dk(0, 2, 1, 0, N), "sa6", on="sa0"))
+        last = stage(nc.scalar, dk(0, 2, 1, 0, N), "sa6", on="sv1")
+        scatter(nc.scalar, 2, HALF, staged[1][:])
+        late.append(stage(nc.vector, dk(3, 3, 1, 0, N), "sv4", on="sv2"))
+        scatter(nc.vector, 3, 0, late[1][:])
+        scatter(nc.scalar, 2, N, last[:])
         store(2)
-        scatter(nc.vector, 3, N, last)
+        scatter(nc.vector, 3, N, late[2][:])
         store(3)

@@ -56,8 +56,8 @@ def tile_attend_gat_tnh_k_kernel(
             nc.sync.dma_start(raw[:], src.rearrange("(p j) w -> p j w", j=PACK))
             return raw
 
-        def zero_plane(name):
-            plane = tile([P, T // 4], I32, name)
+        def zero_plane(name, room=0):
+            plane = tile([P, T // 4], I32, name, room=room)
             nc.vector.memset(plane[:], 0)
             return plane
 
@@ -75,10 +75,8 @@ def tile_attend_gat_tnh_k_kernel(
             for f in range(4):
                 nc.sync.dma_start(plane[f:P:32, :], rows[f:16:4, :])
 
-        def load_words(src, name):
-            pool_tile = tile([P, T], I32, name)
-            nc.sync.dma_start(pool_tile[:], src[0].rearrange("p n j -> p (n j)").bitcast(I32))
-            return pool_tile
+        def load_words(pool_tile, src, x0, x1):
+            nc.sync.dma_start(pool_tile[:, x0:x1], src[0].rearrange("p n j -> p (n j)").bitcast(I32)[:, x0:x1])
 
         def mx_tiles(name, words):
             return tile([P, words], U32, f"{name}_codes"), tile([P, words], U8, f"{name}_scales")
@@ -95,11 +93,10 @@ def tile_attend_gat_tnh_k_kernel(
             nc.vector.tensor_copy(got[:], pool_tile[:].bitcast(dtype).indirect(listed(first, count)))
             return got
 
-        def deal_scalar(raw, name):
-            grouped = tile([P, PACK * R], BF16, name, room=8 * KIB)
-            dst = grouped[:].rearrange("p (t m j) -> p m j t", t=PACK, j=PACK)
+        def deal_scalar(grouped, raw, x0):
+            count = raw.shape[2] // PACK
+            dst = grouped[:].rearrange("p (t m j) -> p m j t", t=PACK, j=PACK)[:, x0 // PACK : x0 // PACK + count]
             nc.scalar.copy(dst, raw[:].rearrange("p j (m t) -> p m j t", t=PACK))
-            return grouped
 
         def deal_vector(raw, name, on=None):
             grouped = tile([P, PACK * R], BF16, name, on)
@@ -107,10 +104,23 @@ def tile_attend_gat_tnh_k_kernel(
             nc.vector.tensor_copy(dst, raw[:].rearrange("p j (m u v) -> p u m j v", u=2, v=2))
             return grouped
 
+        def deal_gpsimd(raw, u, name, on=None, skip=0):
+            grouped = tile([P, 2 * R], BF16, name, on, skip)
+            dst = grouped[:].rearrange("p (v m j) -> p m v j", v=2, j=PACK)
+            src = raw[:].rearrange("p j (m u v) -> p u m v j", u=2, v=2)[:, u]
+            nc.gpsimd.tensor_scalar(dst, src, 1.0, 0.0, ALU.mult, ALU.add)
+            return grouped
+
+        def group_scalar(raw, name, on=None):
+            grouped = tile([P, PACK * raw.shape[2]], BF16, name, on)
+            dst = grouped[:].rearrange("p (c i j) -> p c j i", i=LINE, j=PACK)
+            nc.scalar.copy(dst, raw[:].rearrange("p j (c i) -> p c j i", i=LINE))
+            return grouped
+
         def group_gpsimd(raw, name, on=None, skip=0):
             grouped = tile([P, PACK * raw.shape[2]], BF16, name, on, skip)
             dst = grouped[:].rearrange("p (c j) -> p c j", j=PACK)
-            nc.gpsimd.tensor_scalar(dst, raw[:].rearrange("p j c -> p c j"), 1.0, 0.0, ALU.mult, ALU.add)
+            nc.gpsimd.tensor_scalar(dst, raw.rearrange("p j c -> p c j"), 1.0, 0.0, ALU.mult, ALU.add)
             return grouped
 
         def product(dst, lhs, lhs_fmt, block, codes, scales, rhs_fmt):
@@ -125,34 +135,80 @@ def tile_attend_gat_tnh_k_kernel(
                 stop=True,
             )
 
-        def slope(b, h, q_mx, k_codes, k_bytes):
+        def slope(b, h, q_mx, k_codes, k_bytes, engine):
             w = tile([P, HALF // LINE, PACK, LINE], F32, f"w{b}{h}")
             for pair in range(2):
                 scores = bank(pair, f"a{b}{h}{pair}")
                 for u in range(2):
                     product(scores[:, u * HALF : (u + 1) * HALF], q_mx, E4M3, 2 * pair + u, k_codes, k_bytes, E4M3)
                 lines = scores[:].rearrange("p (t c i) -> p c t i", t=2, i=LINE)
-                nc.scalar.activation(w[:, :, 2 * pair : 2 * pair + 2, :], lines, ACT.Tanh)
-            nc.scalar.activation(w[:], w[:], ACT.Square)
+                nc.scalar.activation(w[:, :, 2 * pair : 2 * pair + 2, :], lines, ACT.Sigmoid, scale=2.0)
+            nc.scalar.activation(w[:], w[:], ACT.Square, bias=-0.5)
             for t in range(PACK):
                 col = slice(b * PACK + t, b * PACK + t + 1)
-                nc.scalar.activation(w[:, :, t, :], w[:, :, t, :], ACT.Identity, scale=minus_gates[:, col], bias=gates[:, col])
+                if engine is nc.scalar:
+                    nc.scalar.activation(w[:, :, t, :], w[:, :, t, :], ACT.Identity, scale=four_gates[:, col], bias=gates[:, col])
+                else:
+                    nc.gpsimd.tensor_scalar(w[:, :, t, :], w[:, :, t, :], four_gates[:, col], gates[:, col], ALU.mult, ALU.add)
             return w
 
-        def form_ds(b, h, w, do_mx, v_codes, v_bytes, room=0, on=None, skip=0):
-            ds = tile([P, HALF * PACK], BF16, f"ds{b}{h}", on, skip, room)
+        def dp_quarters(b, h, do_mx, v_codes, v_bytes):
+            banks = [bank(2 + u, f"dp{b}{h}{u}") for u in range(2)]
             for u in range(2):
-                dp = bank(2 + u, f"dp{b}{h}{u}")
                 cols = slice(u * QUARTER, (u + 1) * QUARTER)
                 for t in range(PACK):
-                    product(dp[:, t * QUARTER : (t + 1) * QUARTER], do_mx, E5M2, t, v_codes[:, cols], v_bytes[:, cols], E4M3)
-                runs = QUARTER // LINE
+                    product(banks[u][:, t * QUARTER : (t + 1) * QUARTER], do_mx, E5M2, t, v_codes[:, cols], v_bytes[:, cols], E4M3)
+            return banks
+
+        def form_ds(b, h, w, banks, on=None, skip=0):
+            ds = tile([P, HALF * PACK], BF16, f"ds{b}{h}", on, skip)
+            runs = QUARTER // LINE
+            for u in range(2):
                 nc.vector.tensor_tensor(
                     ds[:, u * N : (u + 1) * N].rearrange("p (c i t) -> p c t i", i=LINE, t=PACK),
                     w[:, u * runs : (u + 1) * runs],
-                    dp[:].rearrange("p (t c i) -> p c t i", t=PACK, i=LINE),
+                    banks[u][:].rearrange("p (t c i) -> p c t i", t=PACK, i=LINE),
                     ALU.mult,
                 )
+            return ds
+
+        def sigmoids(b, h, q_mx, k_codes, k_bytes):
+            s = tile([P, HALF // LINE, PACK, LINE], F32, f"w{b}{h}")
+            for pair in range(2):
+                scores = bank(pair, f"a{b}{h}{pair}")
+                for u in range(2):
+                    product(scores[:, u * HALF : (u + 1) * HALF], q_mx, E4M3, 2 * pair + u, k_codes, k_bytes, E4M3)
+                lines = scores[:].rearrange("p (t i c) -> p c t i", t=2, i=LINE)
+                nc.scalar.activation(s[:, :, 2 * pair : 2 * pair + 2, :], lines, ACT.Sigmoid, scale=2.0)
+            return s
+
+        def dp_pairs(b, h, do_mx, v_codes, v_bytes):
+            banks = [bank(2 + pair, f"dp{b}{h}{pair}") for pair in range(2)]
+            for t in range(PACK):
+                product(banks[t // 2][:, t % 2 * HALF : (t % 2 + 1) * HALF], do_mx, E5M2, t, v_codes[:], v_bytes, E4M3)
+            return banks
+
+        def gated(b, y, s, banks, pair):
+            for t in (2 * pair, 2 * pair + 1):
+                nc.vector.scalar_tensor_tensor(
+                    out=y[:, :, t, :],
+                    in0=banks[pair][:, t % 2 * HALF : (t % 2 + 1) * HALF].rearrange("p (i c) -> p c i", i=LINE),
+                    scalar=four_gates[:, b * PACK + t : b * PACK + t + 1],
+                    in1=s[:, :, t, :],
+                    op0=ALU.mult,
+                    op1=ALU.mult,
+                )
+
+        def finish_ds(b, h, s, y, on=None, skip=0):
+            ds = tile([P, HALF * PACK], BF16, f"ds{b}{h}", on, skip)
+            nc.vector.scalar_tensor_tensor(
+                out=ds[:].rearrange("p (i y) -> p y i", i=LINE),
+                in0=s[:].rearrange("p c t i -> p (c t) i"),
+                scalar=1.0,
+                in1=y[:].rearrange("p c t i -> p (c t) i"),
+                op0=ALU.subtract,
+                op1=ALU.mult,
+            )
             return ds
 
         def dk(index, c, b, x0, count):
@@ -184,93 +240,113 @@ def tile_attend_gat_tnh_k_kernel(
 
         k_plane = zero_plane("k_plane")
         v_plane = zero_plane("v_plane")
-        q_raw = load_rows(qT[0], "q0")
+        q_raw = [load_rows(qT[0][:, :HALF], "q0a", room=8 * KIB)]
         load_scales(k_plane, k_scales)
-        k_pool = load_words(k_words, "k_pool")
-        gates = tile([P, B * PACK], F32, "gates", room=KIB)
-        nc.sync.dma_start(gates[:].rearrange("p (b t) -> p b t", b=B), rw.rearrange("b (p t) o -> p b (t o)", t=PACK))
+        q_raw.append(load_rows(qT[0][:, HALF:], "q0b"))
         load_scales(v_plane, v_scales)
+        k_pool = tile([P, T], I32, "k_pool")
+        load_words(k_pool, k_words, 0, T)
+        rw_raw = tile([P, B * PACK], F32, "rw_raw", room=N)
+        nc.sync.dma_start(rw_raw[:].rearrange("p (b t) -> p b t", b=B), rw.rearrange("b (p t) o -> p b (t o)", t=PACK))
         do_raw = load_rows(doT[0], "do0")
-        v_pool = load_words(v_words, "v_pool")
-        qm_raw = {(0, 0): load_rows(qm[0][:, :HALF], "qm00")}
-        q_next_raw = load_rows(qT[1], "q1", room=10 * KIB)
+        v_pool = tile([P, T], I32, "v_pool")
+        load_words(v_pool, v_words, 0, T)
+        qm_raw = {(0, u): load_rows(qm[0][:, u * HALF : (u + 1) * HALF], f"qm0{u}") for u in range(2)}
+        q_next_raw = load_rows(qT[1], "q1")
         do_next_raw = load_rows(doT[1], "do1")
-        for b, u in ((1, 0), (0, 1), (1, 1)):
-            qm_raw[b, u] = load_rows(qm[b][:, u * HALF : (u + 1) * HALF], f"qm{b}{u}")
+        for u in range(2):
+            qm_raw[1, u] = load_rows(qm[1][:, u * HALF : (u + 1) * HALF], f"qm1{u}")
         windows = {c: zero_window(nc.vector, c) for c in range(2)}
         qm_mx = [[mx_tiles(f"qm{b}{u}", HALF) for u in range(2)] for b in range(B)]
         ds_mx = [mx_tiles(f"ds{b}", N) for b in range(B)]
 
         k_bytes = gather(k_plane, U8, 0, B * N, "ks")
-        grouped = deal_scalar(q_raw, "q0g")
-        minus_gates = tile([P, B * PACK], F32, "minus_gates", room=KIB)
-        nc.scalar.mul(minus_gates[:], gates[:], -1.0)
+        v_bytes = gather(v_plane, U8, 0, N, "vs0")
+        grouped = tile([P, PACK * R], BF16, "q0g", room=8 * KIB)
+        for h in range(2):
+            deal_scalar(grouped, q_raw[h], h * HALF)
+        windows[2] = zero_window(nc.gpsimd, 2, on="q0a")
+        four_gates = tile([P, B * PACK], F32, "four_gates")
+        nc.scalar.mul(four_gates[:], rw_raw[:], -4.0)
+        gates = tile([P, B * PACK], F32, "gates")
+        nc.scalar.mul(gates[:], four_gates[:], -0.25)
         q_mx = mx_tiles("q0", R)
         quantize(q_mx, 0, grouped[:], E4M3)
-        windows[2] = zero_window(nc.gpsimd, 2, on="q0g")
-        keys = [gather(k_pool, U32, h * HALF, HALF, f"kw0{h}") for h in range(2)]
-        v_bytes = gather(v_plane, U8, 0, N, "vs0")
-        w = [slope(0, h, q_mx, keys[h][:], k_bytes[:, h * HALF : (h + 1) * HALF]) for h in range(2)]
+        windows[3] = zero_window(nc.gpsimd, 3, on="q0g")
+        keys = [gather(k_pool, U32, 0, HALF, "kw00")]
+        v_bytes_next = gather(v_plane, U8, N, N, "vs1", on="rw_raw")
+        keys.append(gather(k_pool, U32, HALF, HALF, "kw01"))
+        w = [slope(0, 0, q_mx, keys[0][:], k_bytes[:, :HALF], nc.gpsimd)]
         grouped = deal_vector(do_raw, "do0g")
+        w.append(slope(0, 1, q_mx, keys[1][:], k_bytes[:, HALF:N], nc.scalar))
         do_mx = mx_tiles("do0", R)
         quantize(do_mx, 0, grouped[:], E5M2)
         values = [gather(v_pool, U32, h * HALF, HALF, f"vw0{h}") for h in range(2)]
-        qm_grouped = group_gpsimd(qm_raw[0, 0], "qm00g")
-        region("first", 10 * KIB)
-        ds = form_ds(0, 0, w[0], do_mx, values[0], v_bytes[:, :HALF], on="first", skip=KIB)
-        quantize(qm_mx[0][0], 0, qm_grouped[:], E4M3)
+        blocks = [group_gpsimd(qm_raw[0, 0][:, :, c * P : (c + 1) * P], f"qm00g{c}") for c in range(2)]
+        ds = form_ds(0, 0, w[0], dp_quarters(0, 0, do_mx, values[0], v_bytes[:, :HALF]))
+        banks = dp_quarters(0, 1, do_mx, values[1], v_bytes[:, HALF:])
+        quantize(qm_mx[0][0], 0, blocks[0][:], E4M3)
         quantize(ds_mx[0], 0, ds[:], E5M2)
-        staged = [stage(nc.scalar, dk(4 + c, c, 0, 0, HALF), f"sa{c}") for c in range(2)]
+        parts = [dk(4, 0, 0, 0, HALF)]
+        quantize(qm_mx[0][0], P, blocks[1][:], E4M3)
+        parts.append(dk(5, 1, 0, 0, HALF))
+        dealt = deal_gpsimd(q_next_raw, 0, "q1g0", on="qm00g0")
+        region("first", 7 * KIB)
+        ds = form_ds(0, 1, w[1], banks, on="first", skip=2 * KIB)
+        staged = [stage(nc.scalar, parts[0], "s00a"), stage(nc.vector, parts[1], "s10a")]
         for c in range(2):
             scatter(nc.scalar, c, 0, staged[c][:])
-        keys_next = gather(k_pool, U32, N, N, "kw1", on="first")
-        grouped = deal_vector(q_next_raw, "q1g", on="do0g")
-        ds = form_ds(0, 1, w[1], do_mx, values[1], v_bytes[:, HALF:], on="q1")
         q_mx = mx_tiles("q1", R)
-        quantize(q_mx, 0, grouped[:], E4M3)
+        quantize(q_mx, 0, dealt[:], E4M3)
         quantize(ds_mx[0], HALF, ds[:], E5M2)
+        parts = [dk(6 + c, c, 0, HALF, HALF) for c in range(2)]
+        keys_next = gather(k_pool, U32, N, N, "kw1", on="first", skip=KIB // 2)
+        dealt = deal_gpsimd(q_next_raw, 1, "q1g1", on="first", skip=7 * KIB // 2)
+        staged = [stage(nc.vector, parts[c], f"s{c}0b") for c in range(2)]
+        scatter(nc.scalar, 0, HALF, staged[0][:])
 
-        w = [
-            slope(1, h, q_mx, keys_next[:, h * HALF : (h + 1) * HALF], k_bytes[:, N + h * HALF : N + (h + 1) * HALF])
+        quantize(q_mx, HALF, dealt[:], E4M3)
+        s = [
+            sigmoids(1, h, q_mx, keys_next[:, h * HALF : (h + 1) * HALF], k_bytes[:, N + h * HALF : N + (h + 1) * HALF])
             for h in range(2)
         ]
-        grouped = deal_vector(do_next_raw, "do1g", on="ds01")
-        where["late"] = where["do1g"] + 2 * KIB
-        v_bytes = gather(v_plane, U8, N, N, "vs1", on="do1")
-        qm_grouped = group_gpsimd(qm_raw[1, 0], "qm10g", on="do1", skip=KIB)
+        v_bytes = v_bytes_next
+        values = [gather(v_pool, U32, N + h * HALF, HALF, f"vw1{h}", on="q1g1", skip=(h - 1) * KIB + 64) for h in range(2)]
+        qm_grouped = group_gpsimd(qm_raw[0, 1][:], "qm01g", on="q1g1", skip=KIB + 64)
+        quantize(qm_mx[0][1], 0, qm_grouped[:], E4M3)
+        parts = [dk(4 + c, 2 + c, 0, 0, N) for c in range(2)]
+        dealt = [deal_gpsimd(do_next_raw, 0, "do1g0", on="qm01g")]
+        scatter(nc.vector, 1, HALF, staged[1][:])
+        dealt.append(deal_gpsimd(do_next_raw, 1, "do1g1"))
+        staged = [stage(nc.vector, parts[c], f"s{2 + c}0", on="s10b" if c == 0 else None) for c in range(2)]
+        for c in range(2):
+            scatter(nc.scalar, 2 + c, 0, staged[c][:])
         do_mx = mx_tiles("do1", R)
-        quantize(do_mx, 0, grouped[:], E5M2)
-        values = [gather(v_pool, U32, N + h * HALF, HALF, f"vw1{h}", on="do1g", skip=h * KIB) for h in range(2)]
-        qm_high_grouped = group_gpsimd(qm_raw[0, 1], "qm01g", on="late")
-        ds = form_ds(1, 0, w[0], do_mx, values[0], v_bytes[:, :HALF])
+        for u in range(2):
+            quantize(do_mx, u * HALF, dealt[u][:], E5M2)
+        qm_grouped = group_gpsimd(qm_raw[1, 0][:], "qm10g", on="do1g1")
+        banks = dp_pairs(1, 0, do_mx, values[0], v_bytes[:, :HALF])
+        y = tile([P, HALF // LINE, PACK, LINE], F32, "y10")
+        for pair in range(2):
+            gated(1, y, s[0], banks, pair)
+        banks = dp_pairs(1, 1, do_mx, values[1], v_bytes[:, HALF:])
+        ds = finish_ds(1, 0, s[0], y)
         quantize(qm_mx[1][0], 0, qm_grouped[:], E4M3)
         quantize(ds_mx[1], 0, ds[:], E5M2)
-        part = dk(6, 1, 0, HALF, HALF)
-        staged = stage(nc.vector, part, "sv0", on="qm10g")
-        quantize(qm_mx[0][1], 0, qm_high_grouped[:], E4M3)
-        qm_high_grouped = group_gpsimd(qm_raw[1, 1], "qm11g", on="late")
-        scatter(nc.vector, 1, HALF, staged[:])
-        staged = [stage(nc.scalar, dk(0, 0, 0, HALF, HALF), "sa2", on="minus_gates"), stage(nc.scalar, dk(5, 0, 1, 0, HALF), "sa3", on="gates")]
-        scatter(nc.scalar, 0, HALF, staged[0][:])
-        scatter(nc.scalar, 0, N, staged[1][:])
-        ds = form_ds(1, 1, w[1], do_mx, values[1], v_bytes[:, HALF:])
-        third = dk(7, 2, 0, 0, N)
-        early = stage(nc.vector, third[:, :HALF], "sv1", on="w11")
+        parts = [dk(6 + c, c, 1, 0, HALF) for c in range(2)]
+        qm_grouped = group_gpsimd(qm_raw[1, 1][:], "qm11g", on="ds10")
+        y = tile([P, HALF // LINE, PACK, LINE], F32, "y11", on="y10")
+        gated(1, y, s[1], banks, 0)
+        staged = [stage(nc.vector, parts[c], f"s{c}1a") for c in range(2)]
+        gated(1, y, s[1], banks, 1)
+        for c in range(2):
+            scatter(nc.scalar, c, N, staged[c][:])
+        ds = finish_ds(1, 1, s[1], y)
+        quantize(qm_mx[1][1], 0, qm_grouped[:], E4M3)
         quantize(ds_mx[1], HALF, ds[:], E5M2)
-        quantize(qm_mx[1][1], 0, qm_high_grouped[:], E4M3)
-        windows[3] = zero_window(nc.gpsimd, 3, on="qm11g")
-        scatter(nc.vector, 2, 0, early[:])
-        staged = [stage(nc.scalar, dk(1, 0, 1, HALF, HALF), "sa4", on="sa0"), stage(nc.scalar, third[:, HALF:], "sa5", on="sa1")]
-        scatter(nc.scalar, 0, N + HALF, staged[0][:])
-        store(0)
-        late = [stage(nc.vector, dk(2, 1, 1, 0, N), "sv2", on="ds11"), stage(nc.vector, dk(4, 3, 0, 0, N), "sv3", on="w10")]
-        scatter(nc.vector, 1, N, late[0][:])
-        store(1)
-        last = stage(nc.scalar, dk(0, 2, 1, 0, N), "sa6", on="sv1")
-        scatter(nc.scalar, 2, HALF, staged[1][:])
-        late.append(stage(nc.vector, dk(3, 3, 1, 0, N), "sv4", on="sv2"))
-        scatter(nc.vector, 3, 0, late[1][:])
-        scatter(nc.scalar, 2, N, last[:])
-        store(2)
-        scatter(nc.vector, 3, N, late[2][:])
-        store(3)
+        for c in range(2):
+            scatter(nc.scalar, c, N + HALF, stage(nc.vector, dk(c, c, 1, HALF, HALF), f"s{c}1b")[:])
+            store(c)
+        for c in range(2, 4):
+            scatter(nc.scalar, c, N, stage(nc.vector, dk(c, c, 1, 0, N), f"s{c}1")[:])
+            store(c)

@@ -23,7 +23,7 @@ LINE = 4
 GROUP = 16
 HALF = N // 2
 QUARTER = N // 4
-BANK_BYTES = 2048
+SCALAR_MOST = 384
 KIB = 1024
 
 
@@ -104,7 +104,11 @@ def tile_attend_gat_tnh_k_kernel(
             nc.vector.tensor_copy(dst, raw[:].rearrange("p j (m u v) -> p u m j v", u=2, v=2))
             return grouped
 
-        def deal_gpsimd(raw, u, name, on=None, skip=0):
+        def deal_gpsimd(grouped, raw):
+            dst = grouped[:].rearrange("p (t m j) -> p m t j", t=PACK, j=PACK)
+            nc.gpsimd.tensor_scalar(dst, raw[:].rearrange("p j (m t) -> p m t j", t=PACK), 1.0, 0.0, ALU.mult, ALU.add)
+
+        def deal_half(raw, u, name, on=None, skip=0):
             grouped = tile([P, 2 * R], BF16, name, on, skip)
             dst = grouped[:].rearrange("p (v m j) -> p m v j", v=2, j=PACK)
             src = raw[:].rearrange("p j (m u v) -> p u m v j", u=2, v=2)[:, u]
@@ -172,10 +176,10 @@ def tile_attend_gat_tnh_k_kernel(
                 )
             return ds
 
-        def sigmoids(b, h, q_mx, k_codes, k_bytes):
+        def sigmoids(b, h, q_mx, k_codes, k_bytes, first_bank=0):
             s = tile([P, HALF // LINE, PACK, LINE], F32, f"w{b}{h}")
             for pair in range(2):
-                scores = bank(pair, f"a{b}{h}{pair}")
+                scores = bank(first_bank + pair, f"a{b}{h}{pair}")
                 for u in range(2):
                     product(scores[:, u * HALF : (u + 1) * HALF], q_mx, E4M3, 2 * pair + u, k_codes, k_bytes, E4M3)
                 lines = scores[:].rearrange("p (t i c) -> p c t i", t=2, i=LINE)
@@ -217,8 +221,8 @@ def tile_attend_gat_tnh_k_kernel(
             product(dst, qm_mx[b][c // 2], E4M3, c % 2, ds_mx[b][0][:, cols], ds_mx[b][1][:, cols], E5M2)
             return dst
 
-        def stage(engine, part, name, on=None):
-            staged = tile([P, part.shape[1]], F32, name, on, room=N * 4)
+        def stage(engine, part, name, on=None, skip=0):
+            staged = tile([P, part.shape[1]], F32, name, on, skip)
             if engine is nc.scalar:
                 nc.scalar.copy(staged[:], part)
             else:
@@ -227,8 +231,9 @@ def tile_attend_gat_tnh_k_kernel(
 
         def scatter(engine, c, first, staged):
             if engine is nc.scalar:
-                for x0 in range(0, staged.shape[1], HALF):
-                    nc.scalar.activation(windows[c][:].indirect(listed(first + x0, HALF)), staged[:, x0 : x0 + HALF], ACT.Copy)
+                for x0 in range(0, staged.shape[1], SCALAR_MOST):
+                    x1 = min(x0 + SCALAR_MOST, staged.shape[1])
+                    nc.scalar.activation(windows[c][:].indirect(listed(first + x0, x1 - x0)), staged[:, x0:x1], ACT.Copy)
             else:
                 nc.vector.tensor_copy(windows[c][:].indirect(listed(first, staged.shape[1])), staged)
 
@@ -251,11 +256,11 @@ def tile_attend_gat_tnh_k_kernel(
         do_raw = load_rows(doT[0], "do0")
         v_pool = tile([P, T], I32, "v_pool")
         load_words(v_pool, v_words, 0, T)
-        qm_raw = {(0, u): load_rows(qm[0][:, u * HALF : (u + 1) * HALF], f"qm0{u}") for u in range(2)}
+        qm_raw = {(0, 0): load_rows(qm[0][:, :HALF], "qm00")}
         q_next_raw = load_rows(qT[1], "q1")
         do_next_raw = load_rows(doT[1], "do1")
-        for u in range(2):
-            qm_raw[1, u] = load_rows(qm[1][:, u * HALF : (u + 1) * HALF], f"qm1{u}")
+        for b, u in ((1, 0), (0, 1), (1, 1)):
+            qm_raw[b, u] = load_rows(qm[b][:, u * HALF : (u + 1) * HALF], f"qm{b}{u}")
         windows = {c: zero_window(nc.vector, c) for c in range(2)}
         qm_mx = [[mx_tiles(f"qm{b}{u}", HALF) for u in range(2)] for b in range(B)]
         ds_mx = [mx_tiles(f"ds{b}", N) for b in range(B)]
@@ -282,6 +287,7 @@ def tile_attend_gat_tnh_k_kernel(
         do_mx = mx_tiles("do0", R)
         quantize(do_mx, 0, grouped[:], E5M2)
         values = [gather(v_pool, U32, h * HALF, HALF, f"vw0{h}") for h in range(2)]
+        values_next = [gather(v_pool, U32, N, HALF, "vw10", on="do0g")]
         blocks = [group_gpsimd(qm_raw[0, 0][:, :, c * P : (c + 1) * P], f"qm00g{c}") for c in range(2)]
         ds = form_ds(0, 0, w[0], dp_quarters(0, 0, do_mx, values[0], v_bytes[:, :HALF]))
         banks = dp_quarters(0, 1, do_mx, values[1], v_bytes[:, HALF:])
@@ -289,43 +295,31 @@ def tile_attend_gat_tnh_k_kernel(
         quantize(ds_mx[0], 0, ds[:], E5M2)
         parts = [dk(4, 0, 0, 0, HALF)]
         quantize(qm_mx[0][0], P, blocks[1][:], E4M3)
-        parts.append(dk(5, 1, 0, 0, HALF))
-        dealt = deal_gpsimd(q_next_raw, 0, "q1g0", on="qm00g0")
-        region("first", 7 * KIB)
-        ds = form_ds(0, 1, w[1], banks, on="first", skip=2 * KIB)
-        staged = [stage(nc.scalar, parts[0], "s00a"), stage(nc.vector, parts[1], "s10a")]
-        for c in range(2):
-            scatter(nc.scalar, c, 0, staged[c][:])
+        grouped = tile([P, PACK * R], BF16, "q1g")
+        deal_scalar(grouped, q_next_raw, 0)
+        scatter(nc.scalar, 0, 0, stage(nc.scalar, parts[0], "s00a", on="q1")[:])
+        ds = form_ds(0, 1, w[1], banks)
+        keys_next = gather(k_pool, U32, N, N, "kw1", on="w01")
+        dealt = [deal_half(do_next_raw, 0, "do1g0", on="qm00g0")]
+
         q_mx = mx_tiles("q1", R)
-        quantize(q_mx, 0, dealt[:], E4M3)
+        quantize(q_mx, 0, grouped[:], E4M3)
+        s = [sigmoids(1, 0, q_mx, keys_next[:, :HALF], k_bytes[:, N : N + HALF])]
         quantize(ds_mx[0], HALF, ds[:], E5M2)
         parts = [dk(6 + c, c, 0, HALF, HALF) for c in range(2)]
-        keys_next = gather(k_pool, U32, N, N, "kw1", on="first", skip=KIB // 2)
-        dealt = deal_gpsimd(q_next_raw, 1, "q1g1", on="first", skip=7 * KIB // 2)
-        staged = [stage(nc.vector, parts[c], f"s{c}0b") for c in range(2)]
-        scatter(nc.scalar, 0, HALF, staged[0][:])
-
-        quantize(q_mx, HALF, dealt[:], E4M3)
-        s = [
-            sigmoids(1, h, q_mx, keys_next[:, h * HALF : (h + 1) * HALF], k_bytes[:, N + h * HALF : N + (h + 1) * HALF])
-            for h in range(2)
-        ]
-        v_bytes = v_bytes_next
-        values = [gather(v_pool, U32, N + h * HALF, HALF, f"vw1{h}", on="q1g1", skip=(h - 1) * KIB + 64) for h in range(2)]
-        qm_grouped = group_gpsimd(qm_raw[0, 1][:], "qm01g", on="q1g1", skip=KIB + 64)
-        quantize(qm_mx[0][1], 0, qm_grouped[:], E4M3)
-        parts = [dk(4 + c, 2 + c, 0, 0, N) for c in range(2)]
-        dealt = [deal_gpsimd(do_next_raw, 0, "do1g0", on="qm01g")]
-        scatter(nc.vector, 1, HALF, staged[1][:])
-        dealt.append(deal_gpsimd(do_next_raw, 1, "do1g1"))
-        staged = [stage(nc.vector, parts[c], f"s{2 + c}0", on="s10b" if c == 0 else None) for c in range(2)]
-        for c in range(2):
-            scatter(nc.scalar, 2 + c, 0, staged[c][:])
+        dealt.append(deal_half(do_next_raw, 1, "do1g1", on="ds01"))
+        values = values_next + [gather(v_pool, U32, N + HALF, HALF, "vw11", on="q1g")]
+        second = [stage(nc.vector, parts[0], "s00b", on="v_pool")]
+        held = parts[1]
+        first = dk(0, 1, 0, 0, HALF)
         do_mx = mx_tiles("do1", R)
         for u in range(2):
             quantize(do_mx, u * HALF, dealt[u][:], E5M2)
-        qm_grouped = group_gpsimd(qm_raw[1, 0][:], "qm10g", on="do1g1")
+        v_bytes = v_bytes_next
         banks = dp_pairs(1, 0, do_mx, values[0], v_bytes[:, :HALF])
+        scatter(nc.scalar, 1, 0, stage(nc.scalar, first, "s10a")[:])
+        s.append(sigmoids(1, 1, q_mx, keys_next[:, HALF:], k_bytes[:, N + HALF :], 4))
+        qm_grouped = group_gpsimd(qm_raw[1, 0][:], "qm10g", on="do1g1")
         y = tile([P, HALF // LINE, PACK, LINE], F32, "y10")
         for pair in range(2):
             gated(1, y, s[0], banks, pair)
@@ -333,20 +327,38 @@ def tile_attend_gat_tnh_k_kernel(
         ds = finish_ds(1, 0, s[0], y)
         quantize(qm_mx[1][0], 0, qm_grouped[:], E4M3)
         quantize(ds_mx[1], 0, ds[:], E5M2)
-        parts = [dk(6 + c, c, 1, 0, HALF) for c in range(2)]
-        qm_grouped = group_gpsimd(qm_raw[1, 1][:], "qm11g", on="ds10")
+        parts = [dk(c, c, 1, 0, HALF) for c in range(2)]
+        scatter(nc.scalar, 0, HALF, second[0][:])
+        qm_grouped = group_gpsimd(qm_raw[0, 1][:], "qm01g", on="ds10")
         y = tile([P, HALF // LINE, PACK, LINE], F32, "y11", on="y10")
-        gated(1, y, s[1], banks, 0)
-        staged = [stage(nc.vector, parts[c], f"s{c}1a") for c in range(2)]
-        gated(1, y, s[1], banks, 1)
-        for c in range(2):
-            scatter(nc.scalar, c, N, staged[c][:])
-        ds = finish_ds(1, 1, s[1], y)
-        quantize(qm_mx[1][1], 0, qm_grouped[:], E4M3)
+        for pair in range(2):
+            gated(1, y, s[1], banks, pair)
+        staged = [stage(nc.scalar, parts[c], f"s{c}1a") for c in range(2)]
+        scatter(nc.scalar, 0, N, staged[0][:])
+        region("last", 3 * KIB)
+        ds = finish_ds(1, 1, s[1], y, on="last")
+        second.append(stage(nc.vector, held, "s10b", on="y11"))
+        quantize(qm_mx[0][1], 0, qm_grouped[:], E4M3)
         quantize(ds_mx[1], HALF, ds[:], E5M2)
-        for c in range(2):
-            scatter(nc.scalar, c, N + HALF, stage(nc.vector, dk(c, c, 1, HALF, HALF), f"s{c}1b")[:])
-            store(c)
-        for c in range(2, 4):
-            scatter(nc.scalar, c, N, stage(nc.vector, dk(c, c, 1, 0, N), f"s{c}1")[:])
-            store(c)
+        parts = [dk(6 + c, c, 1, HALF, HALF) for c in range(2)]
+        whole = [dk(2 + c, 2 + c, 0, 0, N) for c in range(2)]
+        qm_grouped = group_gpsimd(qm_raw[1, 1][:], "qm11g", on="ds11")
+        scatter(nc.vector, 1, HALF, second[1][:])
+        scatter(nc.vector, 1, N, staged[1][:])
+        quantize(qm_mx[1][1], 0, qm_grouped[:], E4M3)
+        whole = whole + [dk(4 + c, 2 + c, 1, 0, N) for c in range(2)]
+        staged = [stage(nc.scalar, parts[0], "s01b"), stage(nc.vector, parts[1], "s11b", on="qm11g")]
+        late = [stage(nc.vector, whole[1], "s30", on="qm11g", skip=KIB)]
+        scatter(nc.scalar, 0, N + HALF, staged[0][:])
+        store(0)
+        scatter(nc.vector, 1, N + HALF, staged[1][:])
+        store(1)
+        both = tile([P, B * N], F32, "s2")
+        for b in range(B):
+            nc.scalar.copy(both[:, b * N : (b + 1) * N], whole[2 * b])
+        late.append(stage(nc.vector, whole[3], "s31"))
+        for b in range(B):
+            scatter(nc.vector, 3, b * N, late[b][:])
+        store(3)
+        scatter(nc.scalar, 2, 0, both[:])
+        store(2)

@@ -262,7 +262,7 @@ def tile_attend_gat_tnh_k_kernel(
         for b, u in ((1, 0), (0, 1), (1, 1)):
             qm_raw[b, u] = load_rows(qm[b][:, u * HALF : (u + 1) * HALF], f"qm{b}{u}")
         windows = {c: zero_window(nc.vector, c) for c in range(2)}
-        qm_mx = [[mx_tiles(f"qm{b}{u}", HALF) for u in range(2)] for b in range(B)]
+        qm_mx = [[mx_tiles("qm00", HALF)], [mx_tiles(f"qm1{u}", HALF) for u in range(2)]]
         ds_mx = [mx_tiles(f"ds{b}", N) for b in range(B)]
 
         k_bytes = gather(k_plane, U8, 0, B * N, "ks")
@@ -287,7 +287,7 @@ def tile_attend_gat_tnh_k_kernel(
         do_mx = mx_tiles("do0", R)
         quantize(do_mx, 0, grouped[:], E5M2)
         values = [gather(v_pool, U32, h * HALF, HALF, f"vw0{h}") for h in range(2)]
-        values_next = [gather(v_pool, U32, N, HALF, "vw10", on="do0g")]
+        keys_next = [gather(k_pool, U32, N, HALF, "kw10", on="do0g")]
         blocks = [group_gpsimd(qm_raw[0, 0][:, :, c * P : (c + 1) * P], f"qm00g{c}") for c in range(2)]
         ds = form_ds(0, 0, w[0], dp_quarters(0, 0, do_mx, values[0], v_bytes[:, :HALF]))
         banks = dp_quarters(0, 1, do_mx, values[1], v_bytes[:, HALF:])
@@ -295,70 +295,65 @@ def tile_attend_gat_tnh_k_kernel(
         quantize(ds_mx[0], 0, ds[:], E5M2)
         parts = [dk(4, 0, 0, 0, HALF)]
         quantize(qm_mx[0][0], P, blocks[1][:], E4M3)
-        grouped = tile([P, PACK * R], BF16, "q1g")
-        deal_scalar(grouped, q_next_raw, 0)
-        scatter(nc.scalar, 0, 0, stage(nc.scalar, parts[0], "s00a", on="q1")[:])
-        ds = form_ds(0, 1, w[1], banks)
-        keys_next = gather(k_pool, U32, N, N, "kw1", on="w01")
-        dealt = [deal_half(do_next_raw, 0, "do1g0", on="qm00g0")]
+        parts.append(dk(5, 1, 0, 0, HALF))
+        staged = [stage(nc.scalar, parts[c], f"s{c}0a") for c in range(2)]
+        for c in range(2):
+            scatter(nc.scalar, c, 0, staged[c][:])
+        grouped = deal_vector(q_next_raw, "q1g", on="w00")
+        ds = form_ds(0, 1, w[1], banks, on="q1")
 
         q_mx = mx_tiles("q1", R)
         quantize(q_mx, 0, grouped[:], E4M3)
-        s = [sigmoids(1, 0, q_mx, keys_next[:, :HALF], k_bytes[:, N : N + HALF])]
+        s = [sigmoids(1, 0, q_mx, keys_next[0][:], k_bytes[:, N : N + HALF])]
         quantize(ds_mx[0], HALF, ds[:], E5M2)
         parts = [dk(6 + c, c, 0, HALF, HALF) for c in range(2)]
-        dealt.append(deal_half(do_next_raw, 1, "do1g1", on="ds01"))
-        values = values_next + [gather(v_pool, U32, N + HALF, HALF, "vw11", on="q1g")]
-        second = [stage(nc.vector, parts[0], "s00b", on="v_pool")]
-        held = parts[1]
-        first = dk(0, 1, 0, 0, HALF)
+        grouped = deal_vector(do_next_raw, "do1g", on="ds01")
+        keys_next.append(gather(k_pool, U32, N + HALF, HALF, "kw11", on="do1"))
+        staged = [stage(nc.scalar, parts[c], f"s{c}0b", on="kw10" if c == 0 else None) for c in range(2)]
+        scatter(nc.scalar, 0, HALF, staged[0][:])
+        s.append(sigmoids(1, 1, q_mx, keys_next[1][:], k_bytes[:, N + HALF :], 4))
+        scatter(nc.scalar, 1, HALF, staged[1][:])
         do_mx = mx_tiles("do1", R)
-        for u in range(2):
-            quantize(do_mx, u * HALF, dealt[u][:], E5M2)
+        quantize(do_mx, 0, grouped[:], E5M2)
+        values = [gather(v_pool, U32, N + h * HALF, HALF, f"vw1{h}", on="do1g", skip=h * KIB) for h in range(2)]
+        qm_grouped = [group_gpsimd(qm_raw[1, 0][:], "qm10g", on="do1g", skip=2 * KIB), group_gpsimd(qm_raw[0, 1][:], "qm01g", on="k_pool")]
         v_bytes = v_bytes_next
         banks = dp_pairs(1, 0, do_mx, values[0], v_bytes[:, :HALF])
-        scatter(nc.scalar, 1, 0, stage(nc.scalar, first, "s10a")[:])
-        s.append(sigmoids(1, 1, q_mx, keys_next[:, HALF:], k_bytes[:, N + HALF :], 4))
-        qm_grouped = group_gpsimd(qm_raw[1, 0][:], "qm10g", on="do1g1")
-        y = tile([P, HALF // LINE, PACK, LINE], F32, "y10")
+        y = tile([P, HALF // LINE, PACK, LINE], F32, "y10", room=5 * KIB)
         for pair in range(2):
             gated(1, y, s[0], banks, pair)
         banks = dp_pairs(1, 1, do_mx, values[1], v_bytes[:, HALF:])
         ds = finish_ds(1, 0, s[0], y)
-        quantize(qm_mx[1][0], 0, qm_grouped[:], E4M3)
+        quantize(qm_mx[1][0], 0, qm_grouped[0][:], E4M3)
         quantize(ds_mx[1], 0, ds[:], E5M2)
         parts = [dk(c, c, 1, 0, HALF) for c in range(2)]
-        scatter(nc.scalar, 0, HALF, second[0][:])
-        qm_grouped = group_gpsimd(qm_raw[0, 1][:], "qm01g", on="ds10")
-        y = tile([P, HALF // LINE, PACK, LINE], F32, "y11", on="y10")
+        qm_mx[0].append((tile([P, HALF], U32, "qm01_codes", on="y10"), tile([P, HALF], U8, "qm01_scales")))
+        quantize(qm_mx[0][1], 0, qm_grouped[1][:], E4M3)
+        whole = [dk(6 + c, 2 + c, 0, 0, N) for c in range(2)]
+        qm_grouped = group_gpsimd(qm_raw[1, 1][:], "qm11g", on="qm01g")
+        y = tile([P, HALF // LINE, PACK, LINE], F32, "y11", on="y10", skip=KIB)
         for pair in range(2):
             gated(1, y, s[1], banks, pair)
         staged = [stage(nc.scalar, parts[c], f"s{c}1a") for c in range(2)]
-        scatter(nc.scalar, 0, N, staged[0][:])
-        region("last", 3 * KIB)
-        ds = finish_ds(1, 1, s[1], y, on="last")
-        second.append(stage(nc.vector, held, "s10b", on="y11"))
-        quantize(qm_mx[0][1], 0, qm_grouped[:], E4M3)
-        quantize(ds_mx[1], HALF, ds[:], E5M2)
-        parts = [dk(6 + c, c, 1, HALF, HALF) for c in range(2)]
-        whole = [dk(2 + c, 2 + c, 0, 0, N) for c in range(2)]
-        qm_grouped = group_gpsimd(qm_raw[1, 1][:], "qm11g", on="ds11")
-        scatter(nc.vector, 1, HALF, second[1][:])
-        scatter(nc.vector, 1, N, staged[1][:])
+        for c in range(2):
+            scatter(nc.scalar, c, N, staged[c][:])
+        ds = finish_ds(1, 1, s[1], y, on="k_pool", skip=2 * KIB)
         quantize(qm_mx[1][1], 0, qm_grouped[:], E4M3)
-        whole = whole + [dk(4 + c, 2 + c, 1, 0, N) for c in range(2)]
-        staged = [stage(nc.scalar, parts[0], "s01b"), stage(nc.vector, parts[1], "s11b", on="qm11g")]
-        late = [stage(nc.vector, whole[1], "s30", on="qm11g", skip=KIB)]
+        quantize(ds_mx[1], HALF, ds[:], E5M2)
+        mine = [stage(nc.vector, whole[0], "s20", on="k_pool", skip=KIB)]
+        last = [dk(4 + c, c, 1, HALF, HALF) for c in range(2)]
+        whole = whole + [dk(2 + c, 2 + c, 1, 0, N) for c in range(2)]
+        scatter(nc.vector, 2, 0, mine[0][:])
+        mine.append(stage(nc.scalar, whole[2], "s21"))
+        staged = [stage(nc.scalar, last[c], f"s{c}1b") for c in range(2)]
+        mine.append(stage(nc.scalar, whole[1], "s30", on="s20"))
         scatter(nc.scalar, 0, N + HALF, staged[0][:])
         store(0)
-        scatter(nc.vector, 1, N + HALF, staged[1][:])
-        store(1)
-        both = tile([P, B * N], F32, "s2")
-        for b in range(B):
-            nc.scalar.copy(both[:, b * N : (b + 1) * N], whole[2 * b])
-        late.append(stage(nc.vector, whole[3], "s31"))
-        for b in range(B):
-            scatter(nc.vector, 3, b * N, late[b][:])
-        store(3)
-        scatter(nc.scalar, 2, 0, both[:])
+        scatter(nc.vector, 2, N, mine[1][:])
         store(2)
+        mine.append(stage(nc.scalar, whole[3], "s31"))
+        scatter(nc.scalar, 1, N + HALF, staged[1][:])
+        store(1)
+        for b in range(B):
+            scatter(nc.vector, 3, b * N, mine[2 + b][:])
+        store(3)

@@ -51,8 +51,8 @@ def tile_attend_gat_tnh_k_kernel(
         def bank(index, name):
             return psum.tile([P, N], F32, name=name, tag=f"bank{index}")
 
-        def load_rows(src, name, room=0):
-            raw = tile([P, PACK, src.shape[1]], F32, name, room=room)
+        def load_rows(src, name, on=None):
+            raw = tile([P, PACK, src.shape[1]], F32, name, on)
             nc.sync.dma_start(raw[:], src.rearrange("(p j) w -> p j w", j=PACK))
             return raw
 
@@ -139,22 +139,27 @@ def tile_attend_gat_tnh_k_kernel(
                 stop=True,
             )
 
-        def slope(b, h, q_mx, k_codes, k_bytes, engine):
+        def slope(b, h, q_mx, k_codes, k_bytes, engine, first_bank=0, on=None, skip=0):
             w = tile([P, HALF // LINE, PACK, LINE], F32, f"w{b}{h}")
             for pair in range(2):
-                scores = bank(pair, f"a{b}{h}{pair}")
+                scores = bank(first_bank + pair, f"a{b}{h}{pair}")
                 for u in range(2):
                     product(scores[:, u * HALF : (u + 1) * HALF], q_mx, E4M3, 2 * pair + u, k_codes, k_bytes, E4M3)
                 lines = scores[:].rearrange("p (t c i) -> p c t i", t=2, i=LINE)
                 nc.scalar.activation(w[:, :, 2 * pair : 2 * pair + 2, :], lines, ACT.Sigmoid, scale=2.0)
             nc.scalar.activation(w[:], w[:], ACT.Square, bias=-0.5)
+            if engine is None:
+                return w
+            return gate(b, w, w, engine)
+
+        def gate(b, dst, w, engine):
             for t in range(PACK):
                 col = slice(b * PACK + t, b * PACK + t + 1)
                 if engine is nc.scalar:
-                    nc.scalar.activation(w[:, :, t, :], w[:, :, t, :], ACT.Identity, scale=four_gates[:, col], bias=gates[:, col])
+                    nc.scalar.activation(dst[:, :, t, :], w[:, :, t, :], ACT.Identity, scale=four_gates[:, col], bias=gates[:, col])
                 else:
-                    nc.gpsimd.tensor_scalar(w[:, :, t, :], w[:, :, t, :], four_gates[:, col], gates[:, col], ALU.mult, ALU.add)
-            return w
+                    nc.gpsimd.tensor_scalar(dst[:, :, t, :], w[:, :, t, :], four_gates[:, col], gates[:, col], ALU.mult, ALU.add)
+            return dst
 
         def dp_quarters(b, h, do_mx, v_codes, v_bytes):
             banks = [bank(2 + u, f"dp{b}{h}{u}") for u in range(2)]
@@ -245,7 +250,8 @@ def tile_attend_gat_tnh_k_kernel(
 
         k_plane = zero_plane("k_plane")
         v_plane = zero_plane("v_plane")
-        q_raw = [load_rows(qT[0][:, :HALF], "q0a", room=8 * KIB)]
+        where["top"] = 216 * KIB
+        q_raw = [load_rows(qT[0][:, :HALF], "q0a", on="top")]
         load_scales(k_plane, k_scales)
         q_raw.append(load_rows(qT[0][:, HALF:], "q0b"))
         load_scales(v_plane, v_scales)
@@ -293,67 +299,71 @@ def tile_attend_gat_tnh_k_kernel(
         banks = dp_quarters(0, 1, do_mx, values[1], v_bytes[:, HALF:])
         quantize(qm_mx[0][0], 0, blocks[0][:], E4M3)
         quantize(ds_mx[0], 0, ds[:], E5M2)
-        parts = [dk(4, 0, 0, 0, HALF)]
         quantize(qm_mx[0][0], P, blocks[1][:], E4M3)
-        parts.append(dk(5, 1, 0, 0, HALF))
-        staged = [stage(nc.scalar, parts[c], f"s{c}0a") for c in range(2)]
-        for c in range(2):
-            scatter(nc.scalar, c, 0, staged[c][:])
-        grouped = deal_vector(q_next_raw, "q1g", on="w00")
-        ds = form_ds(0, 1, w[1], banks, on="q1")
+        parts = [dk(4 + c, c, 0, 0, HALF) for c in range(2)]
+        grouped = tile([P, PACK * R], BF16, "q1g")
+        deal_scalar(grouped, q_next_raw, 0)
+        first = [stage(nc.scalar, parts[0], "s00a", on="q1")]
+        held = parts[1]
+        ds = form_ds(0, 1, w[1], banks)
+        keys_next.append(gather(k_pool, U32, N + HALF, HALF, "kw11", on="w01"))
+        values = [gather(v_pool, U32, N, HALF, "vw10", on="w01", skip=KIB)]
 
-        q_mx = mx_tiles("q1", R)
-        quantize(q_mx, 0, grouped[:], E4M3)
-        s = [sigmoids(1, 0, q_mx, keys_next[0][:], k_bytes[:, N : N + HALF])]
         quantize(ds_mx[0], HALF, ds[:], E5M2)
         parts = [dk(6 + c, c, 0, HALF, HALF) for c in range(2)]
-        grouped = deal_vector(do_next_raw, "do1g", on="ds01")
-        keys_next.append(gather(k_pool, U32, N + HALF, HALF, "kw11", on="do1"))
-        staged = [stage(nc.scalar, parts[c], f"s{c}0b", on="kw10" if c == 0 else None) for c in range(2)]
-        scatter(nc.scalar, 0, HALF, staged[0][:])
-        s.append(sigmoids(1, 1, q_mx, keys_next[1][:], k_bytes[:, N + HALF :], 4))
-        scatter(nc.scalar, 1, HALF, staged[1][:])
+        q_mx = mx_tiles("q1", R)
+        quantize(q_mx, 0, grouped[:], E4M3)
+        qm_grouped = [group_gpsimd(qm_raw[1, 0][:], "qm10g", on="q1g")]
+        grouped = tile([P, PACK * R], BF16, "do1g")
+        deal_scalar(grouped, do_next_raw, 0)
+        first.append(stage(nc.scalar, held, "s10a", on="do1"))
+        squares = [slope(1, 0, q_mx, keys_next[0][:], k_bytes[:, N : N + HALF], None)]
+        second = [stage(nc.scalar, parts[0], "s00b", on="kw10")]
+        held = parts[1]
+        squares.append(slope(1, 1, q_mx, keys_next[1][:], k_bytes[:, N + HALF :], nc.scalar, 4))
+        scatter(nc.vector, 0, 0, first[0][:])
         do_mx = mx_tiles("do1", R)
         quantize(do_mx, 0, grouped[:], E5M2)
-        values = [gather(v_pool, U32, N + h * HALF, HALF, f"vw1{h}", on="do1g", skip=h * KIB) for h in range(2)]
-        qm_grouped = [group_gpsimd(qm_raw[1, 0][:], "qm10g", on="do1g", skip=2 * KIB), group_gpsimd(qm_raw[0, 1][:], "qm01g", on="k_pool")]
         v_bytes = v_bytes_next
-        banks = dp_pairs(1, 0, do_mx, values[0], v_bytes[:, :HALF])
-        y = tile([P, HALF // LINE, PACK, LINE], F32, "y10", room=5 * KIB)
-        for pair in range(2):
-            gated(1, y, s[0], banks, pair)
-        banks = dp_pairs(1, 1, do_mx, values[1], v_bytes[:, HALF:])
-        ds = finish_ds(1, 0, s[0], y)
+        banks = dp_quarters(1, 0, do_mx, values[0], v_bytes[:, :HALF])
         quantize(qm_mx[1][0], 0, qm_grouped[0][:], E4M3)
+        qm_grouped = [group_gpsimd(qm_raw[0, 1][:], "qm01g", on="qm10g")]
+        values.append(gather(v_pool, U32, N + HALF, HALF, "vw11", on="do1g"))
+        scatter(nc.vector, 1, 0, first[1][:])
+        w = gate(1, tile([P, HALF // LINE, PACK, LINE], F32, "g10"), squares[0], nc.gpsimd)
+        scatter(nc.vector, 0, HALF, second[0][:])
+        qm_grouped.append(group_gpsimd(qm_raw[1, 1][:], "qm11g", on="w10"))
+        ds = form_ds(1, 0, w, banks)
+        banks = dp_quarters(1, 1, do_mx, values[1], v_bytes[:, HALF:])
+        qm_mx[0].append((tile([P, HALF], U32, "qm01_codes", on="g10"), tile([P, HALF], U8, "qm01_scales")))
+        quantize(qm_mx[0][1], 0, qm_grouped[0][:], E4M3)
+        whole = [dk(6, 2, 0, 0, N)]
         quantize(ds_mx[1], 0, ds[:], E5M2)
         parts = [dk(c, c, 1, 0, HALF) for c in range(2)]
-        qm_mx[0].append((tile([P, HALF], U32, "qm01_codes", on="y10"), tile([P, HALF], U8, "qm01_scales")))
-        quantize(qm_mx[0][1], 0, qm_grouped[1][:], E4M3)
-        whole = [dk(6 + c, 2 + c, 0, 0, N) for c in range(2)]
-        qm_grouped = group_gpsimd(qm_raw[1, 1][:], "qm11g", on="qm01g")
-        y = tile([P, HALF // LINE, PACK, LINE], F32, "y11", on="y10", skip=KIB)
-        for pair in range(2):
-            gated(1, y, s[1], banks, pair)
-        staged = [stage(nc.scalar, parts[c], f"s{c}1a") for c in range(2)]
-        for c in range(2):
-            scatter(nc.scalar, c, N, staged[c][:])
-        ds = finish_ds(1, 1, s[1], y, on="k_pool", skip=2 * KIB)
-        quantize(qm_mx[1][1], 0, qm_grouped[:], E4M3)
+        quantize(qm_mx[1][1], 0, qm_grouped[1][:], E4M3)
+        ds = form_ds(1, 1, squares[1], banks, on="qm11g")
+        second.append(stage(nc.vector, held, "s10b", on="w11"))
+        whole.append(dk(7, 3, 0, 0, N))
+        third = [stage(nc.scalar, parts[c], f"s{c}1a") for c in range(2)]
+        both = tile([P, B * N], F32, "s2", on="top", skip=8 * KIB)
+        nc.scalar.copy(both[:, :N], whole[0])
+        scatter(nc.scalar, 0, N, third[0][:])
         quantize(ds_mx[1], HALF, ds[:], E5M2)
-        mine = [stage(nc.vector, whole[0], "s20", on="k_pool", skip=KIB)]
-        last = [dk(4 + c, c, 1, HALF, HALF) for c in range(2)]
+        parts = [dk(4 + c, c, 1, HALF, HALF) for c in range(2)]
         whole = whole + [dk(2 + c, 2 + c, 1, 0, N) for c in range(2)]
-        scatter(nc.vector, 2, 0, mine[0][:])
-        mine.append(stage(nc.scalar, whole[2], "s21"))
-        staged = [stage(nc.scalar, last[c], f"s{c}1b") for c in range(2)]
-        mine.append(stage(nc.scalar, whole[1], "s30", on="s20"))
-        scatter(nc.scalar, 0, N + HALF, staged[0][:])
+        scatter(nc.vector, 1, HALF, second[1][:])
+        scatter(nc.vector, 1, N, third[1][:])
+        fourth = [stage(nc.scalar, parts[c], f"s{c}1b") for c in range(2)]
+        scatter(nc.scalar, 0, N + HALF, fourth[0][:])
         store(0)
-        scatter(nc.vector, 2, N, mine[1][:])
-        store(2)
-        mine.append(stage(nc.scalar, whole[3], "s31"))
-        scatter(nc.scalar, 1, N + HALF, staged[1][:])
+        scatter(nc.vector, 1, N + HALF, fourth[1][:])
         store(1)
+        late = [stage(nc.scalar, whole[1], "s30", on="s10b")]
+        nc.scalar.copy(both[:, N:], whole[2])
+        scatter(nc.scalar, 2, 0, both[:, :SCALAR_MOST])
+        late.append(stage(nc.scalar, whole[3], "s31"))
+        scatter(nc.scalar, 2, SCALAR_MOST, both[:, SCALAR_MOST:])
+        store(2)
         for b in range(B):
-            scatter(nc.vector, 3, b * N, mine[2 + b][:])
+            scatter(nc.vector, 3, b * N, late[b][:])
         store(3)

@@ -23,8 +23,8 @@ LINE = 4
 GROUP = 16
 HALF = N // 2
 QUARTER = N // 4
-SCALAR_MOST = 384
-KIB = 1024
+SCALAR_MOST = 256
+ALIGN = 64
 
 
 def tile_attend_gat_tnh_k_kernel(
@@ -43,10 +43,14 @@ def tile_attend_gat_tnh_k_kernel(
                 size = size * extent
             if on is None:
                 where[name] = where["end"]
-                where["end"] = where["end"] + (max(size, room) + 63) // 64 * 64
+                where["end"] = where["end"] + (max(size, room) + ALIGN - 1) // ALIGN * ALIGN
             else:
                 where[name] = where[on] + skip
-            return placed.tile(shape, dtype, name=name, tag=name, align_bytes=64, offset=where[name])
+            return placed.tile(shape, dtype, name=name, tag=name, align_bytes=ALIGN, offset=where[name])
+
+        def region(name, size):
+            where[name] = where["end"]
+            where["end"] = where["end"] + size
 
         def bank(index, name):
             return psum.tile([P, N], F32, name=name, tag=f"bank{index}")
@@ -56,9 +60,9 @@ def tile_attend_gat_tnh_k_kernel(
             nc.sync.dma_start(raw[:], src.rearrange("(p j) w -> p j w", j=PACK))
             return raw
 
-        def zero_plane(name, room=0):
-            plane = tile([P, T // 4], I32, name, room=room)
-            nc.vector.memset(plane[:], 0)
+        def zero_plane(engine, name):
+            plane = tile([P, T // 4], I32, name)
+            engine.memset(plane[:], 0)
             return plane
 
         def zero_window(engine, c, on=None, skip=0):
@@ -66,20 +70,18 @@ def tile_attend_gat_tnh_k_kernel(
             engine.memset(window[:], 0.0)
             return window
 
-        def region(name, size):
-            where[name] = where["end"]
-            where["end"] = where["end"] + size
-
         def load_scales(plane, src):
             rows = src[0].bitcast(I32)
             for f in range(4):
                 nc.sync.dma_start(plane[f:P:32, :], rows[f:16:4, :])
 
-        def load_words(pool_tile, src, x0, x1):
-            nc.sync.dma_start(pool_tile[:, x0:x1], src[0].rearrange("p n j -> p (n j)").bitcast(I32)[:, x0:x1])
+        def load_words(src, name):
+            pool_tile = tile([P, T], I32, name)
+            nc.sync.dma_start(pool_tile[:], src[0].rearrange("p n j -> p (n j)").bitcast(I32))
+            return pool_tile
 
-        def mx_tiles(name, words):
-            return tile([P, words], U32, f"{name}_codes"), tile([P, words], U8, f"{name}_scales")
+        def mx_tiles(name, words, room=0):
+            return tile([P, words], U32, f"{name}_codes", room=room), tile([P, words], U8, f"{name}_scales")
 
         def quantize(mx, x0, grouped, fmt):
             cols = slice(x0, x0 + grouped.shape[1] // PACK)
@@ -96,30 +98,17 @@ def tile_attend_gat_tnh_k_kernel(
         def deal_scalar(grouped, raw, x0):
             count = raw.shape[2] // PACK
             dst = grouped[:].rearrange("p (t m j) -> p m j t", t=PACK, j=PACK)[:, x0 // PACK : x0 // PACK + count]
-            nc.scalar.copy(dst, raw[:].rearrange("p j (m t) -> p m j t", t=PACK))
+            nc.scalar.copy(dst, raw.rearrange("p j (m t) -> p m j t", t=PACK))
 
-        def deal_vector(raw, name, on=None):
-            grouped = tile([P, PACK * R], BF16, name, on)
-            dst = grouped[:].rearrange("p (u v m j) -> p u m j v", u=2, v=2, j=PACK)
-            nc.vector.tensor_copy(dst, raw[:].rearrange("p j (m u v) -> p u m j v", u=2, v=2))
-            return grouped
+        def deal_vector(grouped, raw, x0):
+            count = raw.shape[2] // PACK
+            dst = grouped[:].rearrange("p (u v m j) -> p u m j v", u=2, v=2, j=PACK)[:, :, x0 // PACK : x0 // PACK + count]
+            nc.vector.tensor_copy(dst, raw.rearrange("p j (m u v) -> p u m j v", u=2, v=2))
 
-        def deal_gpsimd(grouped, raw):
-            dst = grouped[:].rearrange("p (t m j) -> p m t j", t=PACK, j=PACK)
-            nc.gpsimd.tensor_scalar(dst, raw[:].rearrange("p j (m t) -> p m t j", t=PACK), 1.0, 0.0, ALU.mult, ALU.add)
-
-        def deal_half(raw, u, name, on=None, skip=0):
-            grouped = tile([P, 2 * R], BF16, name, on, skip)
-            dst = grouped[:].rearrange("p (v m j) -> p m v j", v=2, j=PACK)
-            src = raw[:].rearrange("p j (m u v) -> p u m v j", u=2, v=2)[:, u]
-            nc.gpsimd.tensor_scalar(dst, src, 1.0, 0.0, ALU.mult, ALU.add)
-            return grouped
-
-        def group_scalar(raw, name, on=None):
-            grouped = tile([P, PACK * raw.shape[2]], BF16, name, on)
-            dst = grouped[:].rearrange("p (c i j) -> p c j i", i=LINE, j=PACK)
-            nc.scalar.copy(dst, raw[:].rearrange("p j (c i) -> p c j i", i=LINE))
-            return grouped
+        def deal_gpsimd(grouped, raw, x0):
+            count = raw.shape[2] // PACK
+            dst = grouped[:].rearrange("p (t m j) -> p m t j", t=PACK, j=PACK)[:, x0 // PACK : x0 // PACK + count]
+            nc.gpsimd.tensor_scalar(dst, raw.rearrange("p j (m t) -> p m t j", t=PACK), 1.0, 0.0, ALU.mult, ALU.add)
 
         def group_gpsimd(raw, name, on=None, skip=0):
             grouped = tile([P, PACK * raw.shape[2]], BF16, name, on, skip)
@@ -139,99 +128,66 @@ def tile_attend_gat_tnh_k_kernel(
                 stop=True,
             )
 
-        def slope(b, h, q_mx, k_codes, k_bytes, engine, first_bank=0, on=None, skip=0):
-            w = tile([P, HALF // LINE, PACK, LINE], F32, f"w{b}{h}")
+        def squares(b, h, q_mx, first_bank):
+            w = tile([P, PACK, HALF], F32, f"w{b}{h}")
+            cols = slice(b * N + h * HALF, b * N + (h + 1) * HALF)
             for pair in range(2):
                 scores = bank(first_bank + pair, f"a{b}{h}{pair}")
                 for u in range(2):
-                    product(scores[:, u * HALF : (u + 1) * HALF], q_mx, E4M3, 2 * pair + u, k_codes, k_bytes, E4M3)
-                lines = scores[:].rearrange("p (t c i) -> p c t i", t=2, i=LINE)
-                nc.scalar.activation(w[:, :, 2 * pair : 2 * pair + 2, :], lines, ACT.Sigmoid, scale=2.0)
-            nc.scalar.activation(w[:], w[:], ACT.Square, bias=-0.5)
-            if engine is None:
-                return w
-            return gate(b, w, w, engine)
+                    product(scores[:, u * HALF : (u + 1) * HALF], q_mx, E4M3, 2 * pair + u, keys[:, cols], k_bytes[:, cols], E4M3)
+                part = w[:, 2 * pair : 2 * pair + 2, :].rearrange("p t c -> p (t c)")
+                nc.scalar.activation(part, scores[:], ACT.Sigmoid, scale=2.0)
+            for pair in range(2):
+                part = w[:, 2 * pair : 2 * pair + 2, :].rearrange("p t c -> p (t c)")
+                nc.scalar.activation(part, part, ACT.Square, bias=-0.5)
+            return w
 
-        def gate(b, dst, w, engine):
+        def gate(engine, b, w, dst=None):
+            dst = w if dst is None else dst
             for t in range(PACK):
                 col = slice(b * PACK + t, b * PACK + t + 1)
                 if engine is nc.scalar:
-                    nc.scalar.activation(dst[:, :, t, :], w[:, :, t, :], ACT.Identity, scale=four_gates[:, col], bias=gates[:, col])
+                    nc.scalar.activation(dst[:, t, :], w[:, t, :], ACT.Identity, scale=four_gates[:, col], bias=gates[:, col])
                 else:
-                    nc.gpsimd.tensor_scalar(dst[:, :, t, :], w[:, :, t, :], four_gates[:, col], gates[:, col], ALU.mult, ALU.add)
+                    nc.gpsimd.tensor_scalar(dst[:, t, :], w[:, t, :], four_gates[:, col], gates[:, col], ALU.mult, ALU.add)
             return dst
 
-        def dp_quarters(b, h, do_mx, v_codes, v_bytes):
-            banks = [bank(2 + u, f"dp{b}{h}{u}") for u in range(2)]
+        def dp_quarters(b, h, do_mx, v_codes, first_bank):
+            banks = [bank(first_bank + u, f"dp{b}{h}{u}") for u in range(2)]
             for u in range(2):
                 cols = slice(u * QUARTER, (u + 1) * QUARTER)
+                x0 = b * N + h * HALF + u * QUARTER
                 for t in range(PACK):
-                    product(banks[u][:, t * QUARTER : (t + 1) * QUARTER], do_mx, E5M2, t, v_codes[:, cols], v_bytes[:, cols], E4M3)
+                    product(banks[u][:, t * QUARTER : (t + 1) * QUARTER], do_mx, E5M2, t, v_codes[:, cols], v_bytes[:, x0 : x0 + QUARTER], E4M3)
             return banks
 
-        def form_ds(b, h, w, banks, on=None, skip=0):
-            ds = tile([P, HALF * PACK], BF16, f"ds{b}{h}", on, skip)
-            runs = QUARTER // LINE
+        def form_ds(b, h, w, banks):
+            ds = tile([P, HALF * PACK], BF16, f"ds{b}{h}")
             for u in range(2):
                 nc.vector.tensor_tensor(
                     ds[:, u * N : (u + 1) * N].rearrange("p (c i t) -> p c t i", i=LINE, t=PACK),
-                    w[:, u * runs : (u + 1) * runs],
+                    w[:, :, u * QUARTER : (u + 1) * QUARTER].rearrange("p t (c i) -> p c t i", i=LINE),
                     banks[u][:].rearrange("p (t c i) -> p c t i", t=PACK, i=LINE),
                     ALU.mult,
                 )
-            return ds
+            for u in range(2):
+                quantize(ds_mx[b], h * HALF + u * QUARTER, ds[:, u * N : (u + 1) * N], E5M2)
 
-        def sigmoids(b, h, q_mx, k_codes, k_bytes, first_bank=0):
-            s = tile([P, HALF // LINE, PACK, LINE], F32, f"w{b}{h}")
-            for pair in range(2):
-                scores = bank(first_bank + pair, f"a{b}{h}{pair}")
-                for u in range(2):
-                    product(scores[:, u * HALF : (u + 1) * HALF], q_mx, E4M3, 2 * pair + u, k_codes, k_bytes, E4M3)
-                lines = scores[:].rearrange("p (t i c) -> p c t i", t=2, i=LINE)
-                nc.scalar.activation(s[:, :, 2 * pair : 2 * pair + 2, :], lines, ACT.Sigmoid, scale=2.0)
-            return s
-
-        def dp_pairs(b, h, do_mx, v_codes, v_bytes):
-            banks = [bank(2 + pair, f"dp{b}{h}{pair}") for pair in range(2)]
-            for t in range(PACK):
-                product(banks[t // 2][:, t % 2 * HALF : (t % 2 + 1) * HALF], do_mx, E5M2, t, v_codes[:], v_bytes, E4M3)
-            return banks
-
-        def gated(b, y, s, banks, pair):
-            for t in (2 * pair, 2 * pair + 1):
-                nc.vector.scalar_tensor_tensor(
-                    out=y[:, :, t, :],
-                    in0=banks[pair][:, t % 2 * HALF : (t % 2 + 1) * HALF].rearrange("p (i c) -> p c i", i=LINE),
-                    scalar=four_gates[:, b * PACK + t : b * PACK + t + 1],
-                    in1=s[:, :, t, :],
-                    op0=ALU.mult,
-                    op1=ALU.mult,
-                )
-
-        def finish_ds(b, h, s, y, on=None, skip=0):
-            ds = tile([P, HALF * PACK], BF16, f"ds{b}{h}", on, skip)
-            nc.vector.scalar_tensor_tensor(
-                out=ds[:].rearrange("p (i y) -> p y i", i=LINE),
-                in0=s[:].rearrange("p c t i -> p (c t) i"),
-                scalar=1.0,
-                in1=y[:].rearrange("p c t i -> p (c t) i"),
-                op0=ALU.subtract,
-                op1=ALU.mult,
-            )
-            return ds
-
-        def dk(index, c, b, x0, count):
-            dst = bank(index, f"dk{c}{b}{x0}")[:, :count]
-            cols = slice(x0, x0 + count)
-            product(dst, qm_mx[b][c // 2], E4M3, c % 2, ds_mx[b][0][:, cols], ds_mx[b][1][:, cols], E5M2)
+        def dk_pair(index, u, b, h):
+            dst = bank(index, f"dk{u}{b}{h}")
+            cols = slice(h * HALF, (h + 1) * HALF)
+            for c in range(2):
+                product(dst[:, c * HALF : (c + 1) * HALF], qm_mx[b, u], E4M3, c, ds_mx[b][0][:, cols], ds_mx[b][1][:, cols], E5M2)
             return dst
 
-        def stage(engine, part, name, on=None, skip=0):
+        def dk_whole(index, c, b):
+            dst = bank(index, f"dk{c}{b}")
+            product(dst[:], qm_mx[b, c // 2], E4M3, c % 2, ds_mx[b][0][:], ds_mx[b][1][:], E5M2)
+            return dst
+
+        def stage(part, name, on=None, skip=0):
             staged = tile([P, part.shape[1]], F32, name, on, skip)
-            if engine is nc.scalar:
-                nc.scalar.copy(staged[:], part)
-            else:
-                nc.vector.tensor_copy(staged[:], part)
+            nc.scalar.copy(staged[:], part)
             return staged
 
         def scatter(engine, c, first, staged):
@@ -247,123 +203,102 @@ def tile_attend_gat_tnh_k_kernel(
 
         offsets = keep.tile([P, B * N // GROUP], U16, name="offsets")
         nc.sync.dma_start(offsets[:], offs)
-
-        k_plane = zero_plane("k_plane")
-        v_plane = zero_plane("v_plane")
-        where["top"] = 216 * KIB
-        q_raw = [load_rows(qT[0][:, :HALF], "q0a", on="top")]
+        k_plane = zero_plane(nc.vector, "k_plane")
+        v_plane = zero_plane(nc.vector, "v_plane")
+        k_pool = load_words(k_words, "k_pool")
+        region("late_windows", 2 * T * 4)
+        rw_raw = tile([P, 2 * ALIGN // 4], F32, "rw_raw", on="late_windows", skip=T * 4 - ALIGN)
+        nc.sync.dma_start(
+            rw_raw[:, : B * PACK].rearrange("p (b t) -> p b t", b=B), rw.rearrange("b (p t) o -> p b (t o)", t=PACK)
+        )
         load_scales(k_plane, k_scales)
-        q_raw.append(load_rows(qT[0][:, HALF:], "q0b"))
-        load_scales(v_plane, v_scales)
-        k_pool = tile([P, T], I32, "k_pool")
-        load_words(k_pool, k_words, 0, T)
-        rw_raw = tile([P, B * PACK], F32, "rw_raw", room=N)
-        nc.sync.dma_start(rw_raw[:].rearrange("p (b t) -> p b t", b=B), rw.rearrange("b (p t) o -> p b (t o)", t=PACK))
+        q_raw = [load_rows(qT[0][:, h * HALF : (h + 1) * HALF], f"q0{h}") for h in range(2)]
         do_raw = load_rows(doT[0], "do0")
-        v_pool = tile([P, T], I32, "v_pool")
-        load_words(v_pool, v_words, 0, T)
-        qm_raw = {(0, 0): load_rows(qm[0][:, :HALF], "qm00")}
+        load_scales(v_plane, v_scales)
+        v_pool = load_words(v_words, "v_pool")
+        qm_raw = [load_rows(qm[0][:, :HALF], "qm00")]
         q_next_raw = load_rows(qT[1], "q1")
         do_next_raw = load_rows(doT[1], "do1")
-        for b, u in ((1, 0), (0, 1), (1, 1)):
-            qm_raw[b, u] = load_rows(qm[b][:, u * HALF : (u + 1) * HALF], f"qm{b}{u}")
+        qm_raw.append(load_rows(qm[0][:, HALF:], "qm01"))
+        qm_next_raw = load_rows(qm[1], "qm1")
         windows = {c: zero_window(nc.vector, c) for c in range(2)}
-        qm_mx = [[mx_tiles("qm00", HALF)], [mx_tiles(f"qm1{u}", HALF) for u in range(2)]]
-        ds_mx = [mx_tiles(f"ds{b}", N) for b in range(B)]
-
-        k_bytes = gather(k_plane, U8, 0, B * N, "ks")
-        v_bytes = gather(v_plane, U8, 0, N, "vs0")
-        grouped = tile([P, PACK * R], BF16, "q0g", room=8 * KIB)
-        for h in range(2):
-            deal_scalar(grouped, q_raw[h], h * HALF)
-        windows[2] = zero_window(nc.gpsimd, 2, on="q0a")
         four_gates = tile([P, B * PACK], F32, "four_gates")
-        nc.scalar.mul(four_gates[:], rw_raw[:], -4.0)
+        nc.gpsimd.tensor_scalar(four_gates[:], rw_raw[:, : B * PACK], -4.0, 0.0, ALU.mult, ALU.add)
         gates = tile([P, B * PACK], F32, "gates")
-        nc.scalar.mul(gates[:], four_gates[:], -0.25)
+        nc.gpsimd.tensor_scalar(gates[:], rw_raw[:, : B * PACK], 1.0, 0.0, ALU.mult, ALU.add)
+        for c in (2, 3):
+            windows[c] = zero_window(nc.gpsimd, c, on="late_windows", skip=(c - 2) * T * 4)
+        qm_mx = {(b, u): mx_tiles(f"qm{b}{u}", HALF) for b in range(B) for u in range(2)}
+        ds_mx = [mx_tiles("ds0", N), mx_tiles("ds1", N, room=3 * HALF * 4)]
+
+        keys = gather(k_pool, U32, 0, B * N, "keys")
+        k_bytes = gather(k_plane, U8, 0, B * N, "k_bytes")
+
+        grouped = tile([P, PACK * R], BF16, "q0g")
+        for h in range(2):
+            deal_scalar(grouped, q_raw[h][:], h * HALF)
         q_mx = mx_tiles("q0", R)
         quantize(q_mx, 0, grouped[:], E4M3)
-        windows[3] = zero_window(nc.gpsimd, 3, on="q0g")
-        keys = [gather(k_pool, U32, 0, HALF, "kw00")]
-        v_bytes_next = gather(v_plane, U8, N, N, "vs1", on="rw_raw")
-        keys.append(gather(k_pool, U32, HALF, HALF, "kw01"))
-        w = [slope(0, 0, q_mx, keys[0][:], k_bytes[:, :HALF], nc.gpsimd)]
-        grouped = deal_vector(do_raw, "do0g")
-        w.append(slope(0, 1, q_mx, keys[1][:], k_bytes[:, HALF:N], nc.scalar))
+        grouped = tile([P, PACK * R], BF16, "do0g")
+        deal_scalar(grouped, do_raw[:, :, :HALF], 0)
+        deal_vector(grouped, do_raw[:, :, HALF:], HALF)
+        v_bytes = gather(v_plane, U8, 0, B * N, "v_bytes")
         do_mx = mx_tiles("do0", R)
         quantize(do_mx, 0, grouped[:], E5M2)
+        w = [gate(nc.gpsimd, 0, squares(0, 0, q_mx, 0))]
+        blocks = [group_gpsimd(qm_raw[0][:, :, c * P : (c + 1) * P], f"qm00g{c}") for c in range(2)]
+        w.append(gate(nc.scalar, 0, squares(0, 1, q_mx, 2)))
         values = [gather(v_pool, U32, h * HALF, HALF, f"vw0{h}") for h in range(2)]
-        keys_next = [gather(k_pool, U32, N, HALF, "kw10", on="do0g")]
-        blocks = [group_gpsimd(qm_raw[0, 0][:, :, c * P : (c + 1) * P], f"qm00g{c}") for c in range(2)]
-        ds = form_ds(0, 0, w[0], dp_quarters(0, 0, do_mx, values[0], v_bytes[:, :HALF]))
-        banks = dp_quarters(0, 1, do_mx, values[1], v_bytes[:, HALF:])
-        quantize(qm_mx[0][0], 0, blocks[0][:], E4M3)
-        quantize(ds_mx[0], 0, ds[:], E5M2)
-        quantize(qm_mx[0][0], P, blocks[1][:], E4M3)
-        parts = [dk(4 + c, c, 0, 0, HALF) for c in range(2)]
-        grouped = tile([P, PACK * R], BF16, "q1g")
-        deal_scalar(grouped, q_next_raw, 0)
-        first = [stage(nc.scalar, parts[0], "s00a", on="q1")]
-        held = parts[1]
-        ds = form_ds(0, 1, w[1], banks)
-        keys_next.append(gather(k_pool, U32, N + HALF, HALF, "kw11", on="w01"))
-        values = [gather(v_pool, U32, N, HALF, "vw10", on="w01", skip=KIB)]
+        banks = [dp_quarters(0, h, do_mx, values[h], 4 + 2 * h) for h in range(2)]
+        form_ds(0, 0, w[0], banks[0])
+        for c in range(2):
+            quantize(qm_mx[0, 0], c * P, blocks[c][:], E4M3)
+        values = gather(v_pool, U32, N, N, "vw1", on="w00")
+        low = [dk_pair(0, 0, 0, 0)]
+        form_ds(0, 1, w[1], banks[1])
+        low.append(dk_pair(1, 0, 0, 1))
 
-        quantize(ds_mx[0], HALF, ds[:], E5M2)
-        parts = [dk(6 + c, c, 0, HALF, HALF) for c in range(2)]
+        grouped = tile([P, PACK * R], BF16, "q1g")
+        for x0 in range(0, R, HALF):
+            deal_scalar(grouped, q_next_raw[:, :, x0 : x0 + HALF], x0)
         q_mx = mx_tiles("q1", R)
         quantize(q_mx, 0, grouped[:], E4M3)
-        qm_grouped = [group_gpsimd(qm_raw[1, 0][:], "qm10g", on="q1g")]
-        grouped = tile([P, PACK * R], BF16, "do1g")
-        deal_scalar(grouped, do_next_raw, 0)
-        first.append(stage(nc.scalar, held, "s10a", on="do1"))
-        squares = [slope(1, 0, q_mx, keys_next[0][:], k_bytes[:, N : N + HALF], None)]
-        second = [stage(nc.scalar, parts[0], "s00b", on="kw10")]
-        held = parts[1]
-        squares.append(slope(1, 1, q_mx, keys_next[1][:], k_bytes[:, N + HALF :], nc.scalar, 4))
-        scatter(nc.vector, 0, 0, first[0][:])
+        scatter(nc.vector, 0, 0, stage(low[0][:, :HALF], "s000", on="q1")[:])
+        quantize(qm_mx[0, 1], 0, group_gpsimd(qm_raw[1][:], "qm01g", on="q1g")[:], E4M3)
+        grouped = tile([P, PACK * R], BF16, "do1g", on="q1", skip=N * 4)
+        for x0 in range(0, R, HALF):
+            deal_scalar(grouped, do_next_raw[:, :, x0 : x0 + HALF], x0)
         do_mx = mx_tiles("do1", R)
         quantize(do_mx, 0, grouped[:], E5M2)
-        v_bytes = v_bytes_next
-        banks = dp_quarters(1, 0, do_mx, values[0], v_bytes[:, :HALF])
-        quantize(qm_mx[1][0], 0, qm_grouped[0][:], E4M3)
-        qm_grouped = [group_gpsimd(qm_raw[0, 1][:], "qm01g", on="qm10g")]
-        values.append(gather(v_pool, U32, N + HALF, HALF, "vw11", on="do1g"))
-        scatter(nc.vector, 1, 0, first[1][:])
-        w = gate(1, tile([P, HALF // LINE, PACK, LINE], F32, "g10"), squares[0], nc.gpsimd)
-        scatter(nc.vector, 0, HALF, second[0][:])
-        qm_grouped.append(group_gpsimd(qm_raw[1, 1][:], "qm11g", on="w10"))
-        ds = form_ds(1, 0, w, banks)
-        banks = dp_quarters(1, 1, do_mx, values[1], v_bytes[:, HALF:])
-        qm_mx[0].append((tile([P, HALF], U32, "qm01_codes", on="g10"), tile([P, HALF], U8, "qm01_scales")))
-        quantize(qm_mx[0][1], 0, qm_grouped[0][:], E4M3)
-        whole = [dk(6, 2, 0, 0, N)]
-        quantize(ds_mx[1], 0, ds[:], E5M2)
-        parts = [dk(c, c, 1, 0, HALF) for c in range(2)]
-        quantize(qm_mx[1][1], 0, qm_grouped[1][:], E4M3)
-        ds = form_ds(1, 1, squares[1], banks, on="qm11g")
-        second.append(stage(nc.vector, held, "s10b", on="w11"))
-        whole.append(dk(7, 3, 0, 0, N))
-        third = [stage(nc.scalar, parts[c], f"s{c}1a") for c in range(2)]
-        both = tile([P, B * N], F32, "s2", on="top", skip=8 * KIB)
-        nc.scalar.copy(both[:, :N], whole[0])
-        scatter(nc.scalar, 0, N, third[0][:])
-        quantize(ds_mx[1], HALF, ds[:], E5M2)
-        parts = [dk(4 + c, c, 1, HALF, HALF) for c in range(2)]
-        whole = whole + [dk(2 + c, 2 + c, 1, 0, N) for c in range(2)]
-        scatter(nc.vector, 1, HALF, second[1][:])
-        scatter(nc.vector, 1, N, third[1][:])
-        fourth = [stage(nc.scalar, parts[c], f"s{c}1b") for c in range(2)]
-        scatter(nc.scalar, 0, N + HALF, fourth[0][:])
+        scatter(nc.vector, 1, 0, stage(low[0][:, HALF:], "s100", on="do1")[:])
+        low = stage(low[1][:], "s01", on="do1", skip=N * 4)
+        for c in range(2):
+            scatter(nc.vector, c, HALF, low[:, c * HALF : (c + 1) * HALF])
+        quantize(qm_mx[1, 0], 0, group_gpsimd(qm_next_raw[:, :, :HALF], "qm10g", on="do1g")[:], E4M3)
+        w = [gate(nc.gpsimd, 1, squares(1, 0, q_mx, 2), tile([P, PACK, HALF], F32, "g10"))]
+        grouped = group_gpsimd(qm_next_raw[:, :, HALF:], "qm11g", on="w10")
+        w.append(gate(nc.gpsimd, 1, squares(1, 1, q_mx, 6)))
+        form_ds(1, 0, w[0], dp_quarters(1, 0, do_mx, values[:, :HALF], 4))
+        quantize(qm_mx[1, 1], 0, grouped[:], E4M3)
+        banks = dp_quarters(1, 1, do_mx, values[:, HALF:], 2)
+        high = [dk_whole(7, 3, 0), dk_whole(6, 2, 0)]
+        low = dk_pair(0, 0, 1, 0)
+        scatter(nc.vector, 3, 0, stage(high[0][:, :HALF], "s30")[:])
+        scatter(nc.scalar, 2, 0, stage(high[1][:], "s20")[:])
+        form_ds(1, 1, w[1], banks)
+        lows = [stage(low[:], "s10", on="w11")]
+        lows.append(stage(dk_pair(1, 0, 1, 1)[:], "s11"))
+        last = [dk_whole(4 + c, 2 + c, 1) for c in range(2)]
+        staged = stage(last[0][:], "s21")
+        late = tile([P, 3 * HALF], F32, "late", on="ds1_codes")
+        nc.scalar.copy(late[:, :HALF], high[0][:, HALF:])
+        nc.scalar.copy(late[:, HALF:], last[1][:])
+        for h in range(2):
+            for c in range(2):
+                scatter(nc.vector, c, N + h * HALF, lows[h][:, c * HALF : (c + 1) * HALF])
         store(0)
-        scatter(nc.vector, 1, N + HALF, fourth[1][:])
         store(1)
-        late = [stage(nc.scalar, whole[1], "s30", on="s10b")]
-        nc.scalar.copy(both[:, N:], whole[2])
-        scatter(nc.scalar, 2, 0, both[:, :SCALAR_MOST])
-        late.append(stage(nc.scalar, whole[3], "s31"))
-        scatter(nc.scalar, 2, SCALAR_MOST, both[:, SCALAR_MOST:])
+        scatter(nc.scalar, 2, N, staged[:])
         store(2)
-        for b in range(B):
-            scatter(nc.vector, 3, b * N, late[b][:])
+        scatter(nc.vector, 3, HALF, late[:])
         store(3)

@@ -23,7 +23,7 @@ LINE = 4
 GROUP = 16
 HALF = N // 2
 QUARTER = N // 4
-SCALAR_MOST = 256
+SCALAR_MOST = 384
 ALIGN = 64
 
 
@@ -161,8 +161,8 @@ def tile_attend_gat_tnh_k_kernel(
                     product(banks[u][:, t * QUARTER : (t + 1) * QUARTER], do_mx, E5M2, t, v_codes[:, cols], v_bytes[:, x0 : x0 + QUARTER], E4M3)
             return banks
 
-        def form_ds(b, h, w, banks):
-            ds = tile([P, HALF * PACK], BF16, f"ds{b}{h}")
+        def form_ds(b, h, w, banks, room=0):
+            ds = tile([P, HALF * PACK], BF16, f"ds{b}{h}", room=room)
             for u in range(2):
                 nc.vector.tensor_tensor(
                     ds[:, u * N : (u + 1) * N].rearrange("p (c i t) -> p c t i", i=LINE, t=PACK),
@@ -206,11 +206,8 @@ def tile_attend_gat_tnh_k_kernel(
         k_plane = zero_plane(nc.vector, "k_plane")
         v_plane = zero_plane(nc.vector, "v_plane")
         k_pool = load_words(k_words, "k_pool")
-        region("late_windows", 2 * T * 4)
-        rw_raw = tile([P, 2 * ALIGN // 4], F32, "rw_raw", on="late_windows", skip=T * 4 - ALIGN)
-        nc.sync.dma_start(
-            rw_raw[:, : B * PACK].rearrange("p (b t) -> p b t", b=B), rw.rearrange("b (p t) o -> p b (t o)", t=PACK)
-        )
+        rw_raw = tile([P, B * PACK], F32, "rw_raw", room=T * 4)
+        nc.sync.dma_start(rw_raw[:].rearrange("p (b t) -> p b t", b=B), rw.rearrange("b (p t) o -> p b (t o)", t=PACK))
         load_scales(k_plane, k_scales)
         q_raw = [load_rows(qT[0][:, h * HALF : (h + 1) * HALF], f"q0{h}") for h in range(2)]
         do_raw = load_rows(doT[0], "do0")
@@ -223,13 +220,12 @@ def tile_attend_gat_tnh_k_kernel(
         qm_next_raw = load_rows(qm[1], "qm1")
         windows = {c: zero_window(nc.vector, c) for c in range(2)}
         four_gates = tile([P, B * PACK], F32, "four_gates")
-        nc.gpsimd.tensor_scalar(four_gates[:], rw_raw[:, : B * PACK], -4.0, 0.0, ALU.mult, ALU.add)
+        nc.gpsimd.tensor_scalar(four_gates[:], rw_raw[:], -4.0, 0.0, ALU.mult, ALU.add)
         gates = tile([P, B * PACK], F32, "gates")
-        nc.gpsimd.tensor_scalar(gates[:], rw_raw[:, : B * PACK], 1.0, 0.0, ALU.mult, ALU.add)
-        for c in (2, 3):
-            windows[c] = zero_window(nc.gpsimd, c, on="late_windows", skip=(c - 2) * T * 4)
-        qm_mx = {(b, u): mx_tiles(f"qm{b}{u}", HALF) for b in range(B) for u in range(2)}
-        ds_mx = [mx_tiles("ds0", N), mx_tiles("ds1", N, room=3 * HALF * 4)]
+        nc.gpsimd.tensor_scalar(gates[:], rw_raw[:], 1.0, 0.0, ALU.mult, ALU.add)
+        windows[3] = zero_window(nc.gpsimd, 3, on="rw_raw")
+        qm_mx = {(0, u): mx_tiles(f"qm0{u}", HALF) for u in range(2)}
+        ds_mx = [mx_tiles("ds0", N), mx_tiles("ds1", N)]
 
         keys = gather(k_pool, U32, 0, B * N, "keys")
         k_bytes = gather(k_plane, U8, 0, B * N, "k_bytes")
@@ -245,7 +241,7 @@ def tile_attend_gat_tnh_k_kernel(
         v_bytes = gather(v_plane, U8, 0, B * N, "v_bytes")
         do_mx = mx_tiles("do0", R)
         quantize(do_mx, 0, grouped[:], E5M2)
-        w = [gate(nc.gpsimd, 0, squares(0, 0, q_mx, 0))]
+        w = [gate(nc.gpsimd, 0, squares(0, 0, q_mx, 0), tile([P, PACK, HALF], F32, "g00", on="do0g"))]
         blocks = [group_gpsimd(qm_raw[0][:, :, c * P : (c + 1) * P], f"qm00g{c}") for c in range(2)]
         w.append(gate(nc.scalar, 0, squares(0, 1, q_mx, 2)))
         values = [gather(v_pool, U32, h * HALF, HALF, f"vw0{h}") for h in range(2)]
@@ -253,7 +249,7 @@ def tile_attend_gat_tnh_k_kernel(
         form_ds(0, 0, w[0], banks[0])
         for c in range(2):
             quantize(qm_mx[0, 0], c * P, blocks[c][:], E4M3)
-        values = gather(v_pool, U32, N, N, "vw1", on="w00")
+        values = gather(v_pool, U32, N, N, "vw1", on="g00")
         low = [dk_pair(0, 0, 0, 0)]
         form_ds(0, 1, w[1], banks[1])
         low.append(dk_pair(1, 0, 0, 1))
@@ -274,31 +270,33 @@ def tile_attend_gat_tnh_k_kernel(
         low = stage(low[1][:], "s01", on="do1", skip=N * 4)
         for c in range(2):
             scatter(nc.vector, c, HALF, low[:, c * HALF : (c + 1) * HALF])
-        quantize(qm_mx[1, 0], 0, group_gpsimd(qm_next_raw[:, :, :HALF], "qm10g", on="do1g")[:], E4M3)
-        w = [gate(nc.gpsimd, 1, squares(1, 0, q_mx, 2), tile([P, PACK, HALF], F32, "g10"))]
-        grouped = group_gpsimd(qm_next_raw[:, :, HALF:], "qm11g", on="w10")
-        w.append(gate(nc.gpsimd, 1, squares(1, 1, q_mx, 6)))
+        grouped = tile([P, PACK * D], BF16, "qm1g", on="do1g")
+        for x0 in range(0, D, HALF):
+            dst = grouped[:, PACK * x0 : PACK * (x0 + HALF)].rearrange("p (c j) -> p c j", j=PACK)
+            nc.gpsimd.tensor_scalar(dst, qm_next_raw[:, :, x0 : x0 + HALF].rearrange("p j c -> p c j"), 1.0, 0.0, ALU.mult, ALU.add)
+        w = [gate(nc.gpsimd, 1, squares(1, 0, q_mx, 2)), gate(nc.gpsimd, 1, squares(1, 1, q_mx, 6))]
         form_ds(1, 0, w[0], dp_quarters(1, 0, do_mx, values[:, :HALF], 4))
-        quantize(qm_mx[1, 1], 0, grouped[:], E4M3)
         banks = dp_quarters(1, 1, do_mx, values[:, HALF:], 2)
-        high = [dk_whole(7, 3, 0), dk_whole(6, 2, 0)]
-        low = dk_pair(0, 0, 1, 0)
-        scatter(nc.vector, 3, 0, stage(high[0][:, :HALF], "s30")[:])
-        scatter(nc.scalar, 2, 0, stage(high[1][:], "s20")[:])
-        form_ds(1, 1, w[1], banks)
-        lows = [stage(low[:], "s10", on="w11")]
+        qm_next = (tile([P, D], U32, "qm1_codes", on="w10"), tile([P, D], U8, "qm1_scales"))
+        quantize(qm_next, 0, grouped[:], E4M3)
+        for u in range(2):
+            qm_mx[1, u] = [part[:, u * HALF : (u + 1) * HALF] for part in qm_next]
+        late = tile([P, 2, B * N], F32, "late")
+        for c in (1, 0):
+            nc.scalar.copy(late[:, c, :N], dk_whole(7 - c, 2 + c, 0)[:])
+        scatter(nc.scalar, 3, 0, late[:, 1, :384])
+        lows = [stage(dk_pair(0, 0, 1, 0)[:], "s10")]
+        nc.scalar.copy(late[:, :, N : N + HALF], dk_pair(4, 1, 1, 0)[:].rearrange("p (c x) -> p c x", c=2))
+        form_ds(1, 1, w[1], banks, room=T * 4)
         lows.append(stage(dk_pair(1, 0, 1, 1)[:], "s11"))
-        last = [dk_whole(4 + c, 2 + c, 1) for c in range(2)]
-        staged = stage(last[0][:], "s21")
-        late = tile([P, 3 * HALF], F32, "late", on="ds1_codes")
-        nc.scalar.copy(late[:, :HALF], high[0][:, HALF:])
-        nc.scalar.copy(late[:, HALF:], last[1][:])
+        windows[2] = zero_window(nc.gpsimd, 2, on="ds11")
+        nc.scalar.copy(late[:, :, N + HALF :], dk_pair(5, 1, 1, 1)[:].rearrange("p (c x) -> p c x", c=2))
         for h in range(2):
             for c in range(2):
                 scatter(nc.vector, c, N + h * HALF, lows[h][:, c * HALF : (c + 1) * HALF])
         store(0)
         store(1)
-        scatter(nc.scalar, 2, N, staged[:])
+        scatter(nc.scalar, 2, 0, late[:, 0, :])
         store(2)
-        scatter(nc.vector, 3, HALF, late[:])
+        scatter(nc.vector, 3, 384, late[:, 1, 384:])
         store(3)

@@ -128,17 +128,20 @@ def tile_attend_gat_tnh_k_kernel(
                 stop=True,
             )
 
+        def slope_tile(name, on=None):
+            return tile([P, HALF // LINE, PACK, LINE], F32, name, on)
+
         def squares(b, h, q_mx, first_bank):
-            w = tile([P, PACK, HALF], F32, f"w{b}{h}")
+            w = slope_tile(f"w{b}{h}")
             cols = slice(b * N + h * HALF, b * N + (h + 1) * HALF)
             for pair in range(2):
                 scores = bank(first_bank + pair, f"a{b}{h}{pair}")
                 for u in range(2):
                     product(scores[:, u * HALF : (u + 1) * HALF], q_mx, E4M3, 2 * pair + u, keys[:, cols], k_bytes[:, cols], E4M3)
-                part = w[:, 2 * pair : 2 * pair + 2, :].rearrange("p t c -> p (t c)")
-                nc.scalar.activation(part, scores[:], ACT.Sigmoid, scale=2.0)
+                lines = scores[:].rearrange("p (t c i) -> p c t i", t=2, i=LINE)
+                nc.scalar.activation(w[:, :, 2 * pair : 2 * pair + 2, :], lines, ACT.Sigmoid, scale=2.0)
             for pair in range(2):
-                part = w[:, 2 * pair : 2 * pair + 2, :].rearrange("p t c -> p (t c)")
+                part = w[:, :, 2 * pair : 2 * pair + 2, :]
                 nc.scalar.activation(part, part, ACT.Square, bias=-0.5)
             return w
 
@@ -147,9 +150,9 @@ def tile_attend_gat_tnh_k_kernel(
             for t in range(PACK):
                 col = slice(b * PACK + t, b * PACK + t + 1)
                 if engine is nc.scalar:
-                    nc.scalar.activation(dst[:, t, :], w[:, t, :], ACT.Identity, scale=four_gates[:, col], bias=gates[:, col])
+                    nc.scalar.activation(dst[:, :, t, :], w[:, :, t, :], ACT.Identity, scale=four_gates[:, col], bias=gates[:, col])
                 else:
-                    nc.gpsimd.tensor_scalar(dst[:, t, :], w[:, t, :], four_gates[:, col], gates[:, col], ALU.mult, ALU.add)
+                    nc.gpsimd.tensor_scalar(dst[:, :, t, :], w[:, :, t, :], four_gates[:, col], gates[:, col], ALU.mult, ALU.add)
             return dst
 
         def dp_quarters(b, h, do_mx, v_codes, first_bank):
@@ -166,7 +169,7 @@ def tile_attend_gat_tnh_k_kernel(
             for u in range(2):
                 nc.vector.tensor_tensor(
                     ds[:, u * N : (u + 1) * N].rearrange("p (c i t) -> p c t i", i=LINE, t=PACK),
-                    w[:, :, u * QUARTER : (u + 1) * QUARTER].rearrange("p t (c i) -> p c t i", i=LINE),
+                    w[:, u * QUARTER // LINE : (u + 1) * QUARTER // LINE],
                     banks[u][:].rearrange("p (t c i) -> p c t i", t=PACK, i=LINE),
                     ALU.mult,
                 )
@@ -241,7 +244,7 @@ def tile_attend_gat_tnh_k_kernel(
         v_bytes = gather(v_plane, U8, 0, B * N, "v_bytes")
         do_mx = mx_tiles("do0", R)
         quantize(do_mx, 0, grouped[:], E5M2)
-        w = [gate(nc.gpsimd, 0, squares(0, 0, q_mx, 0), tile([P, PACK, HALF], F32, "g00", on="do0g"))]
+        w = [gate(nc.gpsimd, 0, squares(0, 0, q_mx, 0), slope_tile("g00", on="do0g"))]
         blocks = [group_gpsimd(qm_raw[0][:, :, c * P : (c + 1) * P], f"qm00g{c}") for c in range(2)]
         w.append(gate(nc.scalar, 0, squares(0, 1, q_mx, 2)))
         values = [gather(v_pool, U32, h * HALF, HALF, f"vw0{h}") for h in range(2)]

@@ -23,7 +23,6 @@ LINE = 4
 GROUP = 16
 HALF = N // 2
 QUARTER = N // 4
-SCALAR_MOST = 384
 ALIGN = 64
 
 
@@ -116,6 +115,13 @@ def tile_attend_gat_tnh_k_kernel(
             nc.gpsimd.tensor_scalar(dst, raw.rearrange("p j c -> p c j"), 1.0, 0.0, ALU.mult, ALU.add)
             return grouped
 
+        def group(engine, grouped, raw, x0, x1):
+            dst, src = grouped[:, PACK * x0 : PACK * x1], raw[:, :, x0:x1]
+            if engine is nc.vector:
+                nc.vector.tensor_copy(dst.rearrange("p (c i j) -> p c j i", i=LINE, j=PACK), src.rearrange("p j (c i) -> p c j i", i=LINE))
+            else:
+                nc.gpsimd.tensor_scalar(dst.rearrange("p (c j) -> p c j", j=PACK), src.rearrange("p j c -> p c j"), 1.0, 0.0, ALU.mult, ALU.add)
+
         def product(dst, lhs, lhs_fmt, block, codes, scales, rhs_fmt):
             cols = slice(block * P, (block + 1) * P)
             nc.tensor.matmul_mx(
@@ -152,7 +158,7 @@ def tile_attend_gat_tnh_k_kernel(
                 if engine is nc.scalar:
                     nc.scalar.activation(dst[:, :, t, :], w[:, :, t, :], ACT.Identity, scale=four_gates[:, col], bias=gates[:, col])
                 else:
-                    nc.gpsimd.tensor_scalar(dst[:, :, t, :], w[:, :, t, :], four_gates[:, col], gates[:, col], ALU.mult, ALU.add)
+                    engine.tensor_scalar(dst[:, :, t, :], w[:, :, t, :], four_gates[:, col], gates[:, col], ALU.mult, ALU.add)
             return dst
 
         def dp_quarters(b, h, do_mx, v_codes, first_bank):
@@ -164,8 +170,8 @@ def tile_attend_gat_tnh_k_kernel(
                     product(banks[u][:, t * QUARTER : (t + 1) * QUARTER], do_mx, E5M2, t, v_codes[:, cols], v_bytes[:, x0 : x0 + QUARTER], E4M3)
             return banks
 
-        def form_ds(b, h, w, banks, room=0):
-            ds = tile([P, HALF * PACK], BF16, f"ds{b}{h}", room=room)
+        def form_ds(b, h, w, banks, room=0, on=None):
+            ds = tile([P, HALF * PACK], BF16, f"ds{b}{h}", on, room=room)
             for u in range(2):
                 nc.vector.tensor_tensor(
                     ds[:, u * N : (u + 1) * N].rearrange("p (c i t) -> p c t i", i=LINE, t=PACK),
@@ -188,16 +194,20 @@ def tile_attend_gat_tnh_k_kernel(
             product(dst[:], qm_mx[b, c // 2], E4M3, c % 2, ds_mx[b][0][:], ds_mx[b][1][:], E5M2)
             return dst
 
-        def stage(part, name, on=None, skip=0):
+        def leave(engine, dst, part):
+            if engine is nc.scalar:
+                nc.scalar.copy(dst, part)
+            else:
+                nc.vector.tensor_copy(dst, part)
+
+        def stage(engine, part, name, on=None, skip=0):
             staged = tile([P, part.shape[1]], F32, name, on, skip)
-            nc.scalar.copy(staged[:], part)
+            leave(engine, staged[:], part)
             return staged
 
         def scatter(engine, c, first, staged):
             if engine is nc.scalar:
-                for x0 in range(0, staged.shape[1], SCALAR_MOST):
-                    x1 = min(x0 + SCALAR_MOST, staged.shape[1])
-                    nc.scalar.activation(windows[c][:].indirect(listed(first + x0, x1 - x0)), staged[:, x0:x1], ACT.Copy)
+                nc.scalar.activation(windows[c][:].indirect(listed(first, staged.shape[1])), staged, ACT.Copy, scale=ones[:])
             else:
                 nc.vector.tensor_copy(windows[c][:].indirect(listed(first, staged.shape[1])), staged)
 
@@ -226,7 +236,9 @@ def tile_attend_gat_tnh_k_kernel(
         nc.gpsimd.tensor_scalar(four_gates[:], rw_raw[:], -4.0, 0.0, ALU.mult, ALU.add)
         gates = tile([P, B * PACK], F32, "gates")
         nc.gpsimd.tensor_scalar(gates[:], rw_raw[:], 1.0, 0.0, ALU.mult, ALU.add)
-        windows[3] = zero_window(nc.gpsimd, 3, on="rw_raw")
+        ones = tile([P, 1], F32, "ones")
+        nc.gpsimd.memset(ones[:], 1.0)
+        windows[2] = zero_window(nc.gpsimd, 2, on="rw_raw")
         qm_mx = {(0, u): mx_tiles(f"qm0{u}", HALF) for u in range(2)}
         ds_mx = [mx_tiles("ds0", N), mx_tiles("ds1", N)]
 
@@ -252,54 +264,50 @@ def tile_attend_gat_tnh_k_kernel(
         form_ds(0, 0, w[0], banks[0])
         for c in range(2):
             quantize(qm_mx[0, 0], c * P, blocks[c][:], E4M3)
-        values = gather(v_pool, U32, N, N, "vw1", on="g00")
-        low = [dk_pair(0, 0, 0, 0)]
-        form_ds(0, 1, w[1], banks[1])
-        low.append(dk_pair(1, 0, 0, 1))
+        low = stage(nc.scalar, dk_pair(0, 0, 0, 0)[:], "s00")
+        for c in range(2):
+            scatter(nc.scalar, c, 0, low[:, c * HALF : (c + 1) * HALF])
 
         grouped = tile([P, PACK * R], BF16, "q1g")
-        for x0 in range(0, R, HALF):
-            deal_scalar(grouped, q_next_raw[:, :, x0 : x0 + HALF], x0)
+        deal_scalar(grouped, q_next_raw[:, :, :HALF], 0)
+        deal_vector(grouped, q_next_raw[:, :, HALF:], HALF)
         q_mx = mx_tiles("q1", R)
         quantize(q_mx, 0, grouped[:], E4M3)
-        scatter(nc.vector, 0, 0, stage(low[0][:, :HALF], "s000", on="q1")[:])
-        quantize(qm_mx[0, 1], 0, group_gpsimd(qm_raw[1][:], "qm01g", on="q1g")[:], E4M3)
-        grouped = tile([P, PACK * R], BF16, "do1g", on="q1", skip=N * 4)
-        for x0 in range(0, R, HALF):
-            deal_scalar(grouped, do_next_raw[:, :, x0 : x0 + HALF], x0)
+        form_ds(0, 1, w[1], banks[1])
+        grouped = tile([P, PACK * R], BF16, "do1g")
+        deal_vector(grouped, do_next_raw[:], 0)
         do_mx = mx_tiles("do1", R)
         quantize(do_mx, 0, grouped[:], E5M2)
-        scatter(nc.vector, 1, 0, stage(low[0][:, HALF:], "s100", on="do1")[:])
-        low = stage(low[1][:], "s01", on="do1", skip=N * 4)
-        for c in range(2):
-            scatter(nc.vector, c, HALF, low[:, c * HALF : (c + 1) * HALF])
-        grouped = tile([P, PACK * D], BF16, "qm1g", on="do1g")
-        for x0 in range(0, D, HALF):
-            dst = grouped[:, PACK * x0 : PACK * (x0 + HALF)].rearrange("p (c j) -> p c j", j=PACK)
-            nc.gpsimd.tensor_scalar(dst, qm_next_raw[:, :, x0 : x0 + HALF].rearrange("p j c -> p c j"), 1.0, 0.0, ALU.mult, ALU.add)
-        w = [gate(nc.gpsimd, 1, squares(1, 0, q_mx, 2)), gate(nc.gpsimd, 1, squares(1, 1, q_mx, 6))]
-        form_ds(1, 0, w[0], dp_quarters(1, 0, do_mx, values[:, :HALF], 4))
-        banks = dp_quarters(1, 1, do_mx, values[:, HALF:], 2)
-        qm_next = (tile([P, D], U32, "qm1_codes", on="w10"), tile([P, D], U8, "qm1_scales"))
+        values = gather(v_pool, U32, N, N, "vw1", on="do1")
+        grouped = tile([P, PACK * HALF], BF16, "qm01g", on="do1g")
+        group(nc.gpsimd, grouped, qm_raw[1], 0, P)
+        group(nc.vector, grouped, qm_raw[1], P, HALF)
+        quantize(qm_mx[0, 1], 0, grouped[:], E4M3)
+        grouped = tile([P, PACK * D], BF16, "qm1g")
+        group(nc.vector, grouped, qm_next_raw, 0, D)
+        qm_next = mx_tiles("qm1", D)
         quantize(qm_next, 0, grouped[:], E4M3)
         for u in range(2):
             qm_mx[1, u] = [part[:, u * HALF : (u + 1) * HALF] for part in qm_next]
-        late = tile([P, 2, B * N], F32, "late")
-        for c in (1, 0):
-            nc.scalar.copy(late[:, c, :N], dk_whole(7 - c, 2 + c, 0)[:])
-        scatter(nc.scalar, 3, 0, late[:, 1, :384])
-        lows = [stage(dk_pair(0, 0, 1, 0)[:], "s10")]
-        nc.scalar.copy(late[:, :, N : N + HALF], dk_pair(4, 1, 1, 0)[:].rearrange("p (c x) -> p c x", c=2))
-        form_ds(1, 1, w[1], banks, room=T * 4)
-        lows.append(stage(dk_pair(1, 0, 1, 1)[:], "s11"))
-        windows[2] = zero_window(nc.gpsimd, 2, on="ds11")
-        nc.scalar.copy(late[:, :, N + HALF :], dk_pair(5, 1, 1, 1)[:].rearrange("p (c x) -> p c x", c=2))
-        for h in range(2):
-            for c in range(2):
-                scatter(nc.vector, c, N + h * HALF, lows[h][:, c * HALF : (c + 1) * HALF])
-        store(0)
+        w = [squares(1, h, q_mx, 2 + 2 * h) for h in range(2)]
+        form_ds(1, 0, gate(nc.vector, 1, w[0]), dp_quarters(1, 0, do_mx, values[:, :HALF], 6))
+        low = stage(nc.scalar, dk_pair(5, 0, 0, 1)[:], "s01")
+        for c in range(2):
+            scatter(nc.scalar, c, HALF, low[:, c * HALF : (c + 1) * HALF])
+        high = [dk_whole(c, 2 + c, 0) for c in range(2)]
+        scatter(nc.scalar, 2, 0, stage(nc.scalar, high[0][:], "s20")[:])
+        form_ds(1, 1, gate(nc.vector, 1, w[1]), dp_quarters(1, 1, do_mx, values[:, HALF:], 2), room=T * 4)
+        windows[3] = zero_window(nc.gpsimd, 3, on="ds11")
+        late = tile([P, B * N], F32, "late", on="w11")
+        leave(nc.vector, late[:, :N], high[1][:])
+        last = {c: dk_whole(4 + i, c, 1) for i, c in enumerate((1, 0, 3, 2))}
+        staged = {c: stage(nc.vector, last[c][:], f"s{c}1x") for c in (1, 0)}
+        scatter(nc.vector, 1, N, staged[1][:])
         store(1)
-        scatter(nc.scalar, 2, 0, late[:, 0, :])
-        store(2)
-        scatter(nc.vector, 3, 384, late[:, 1, 384:])
+        leave(nc.vector, late[:, N:], last[3][:])
+        staged[2] = stage(nc.vector, last[2][:], "s21x")
+        for c in (0, 2):
+            scatter(nc.scalar, c, N, staged[c][:])
+            store(c)
+        scatter(nc.vector, 3, 0, late[:])
         store(3)

@@ -23,6 +23,7 @@ LINE = 4
 GROUP = 16
 HALF = N // 2
 QUARTER = N // 4
+KIB = 1024
 ALIGN = 64
 
 
@@ -182,6 +183,17 @@ def tile_attend_gat_tnh_k_kernel(
             for u in range(2):
                 quantize(ds_mx[b], h * HALF + u * QUARTER, ds[:, u * N : (u + 1) * N], E5M2)
 
+        def form_only(b, h, w, banks, on=None, skip=0):
+            ds = tile([P, HALF * PACK], BF16, f"ds{b}{h}", on, skip)
+            for u in range(2):
+                nc.vector.tensor_tensor(
+                    ds[:, u * N : (u + 1) * N].rearrange("p (c i t) -> p c t i", i=LINE, t=PACK),
+                    w[:, u * QUARTER // LINE : (u + 1) * QUARTER // LINE],
+                    banks[u][:].rearrange("p (t c i) -> p c t i", t=PACK, i=LINE),
+                    ALU.mult,
+                )
+            return ds
+
         def dk_pair(index, u, b, h):
             dst = bank(index, f"dk{u}{b}{h}")
             cols = slice(h * HALF, (h + 1) * HALF)
@@ -219,8 +231,10 @@ def tile_attend_gat_tnh_k_kernel(
         k_plane = zero_plane(nc.vector, "k_plane")
         v_plane = zero_plane(nc.vector, "v_plane")
         k_pool = load_words(k_words, "k_pool")
-        rw_raw = tile([P, B * PACK], F32, "rw_raw", room=T * 4)
-        nc.sync.dma_start(rw_raw[:].rearrange("p (b t) -> p b t", b=B), rw.rearrange("b (p t) o -> p b (t o)", t=PACK))
+        region("late_windows", 2 * T * 4)
+        rw_wide = tile([P, 2 * ALIGN // 4], F32, "rw_raw", on="late_windows", skip=T * 4 - ALIGN)
+        rw_raw = rw_wide[:, : B * PACK]
+        nc.sync.dma_start(rw_raw.rearrange("p (b t) -> p b t", b=B), rw.rearrange("b (p t) o -> p b (t o)", t=PACK))
         load_scales(k_plane, k_scales)
         q_raw = [load_rows(qT[0][:, h * HALF : (h + 1) * HALF], f"q0{h}") for h in range(2)]
         do_raw = load_rows(doT[0], "do0")
@@ -233,14 +247,16 @@ def tile_attend_gat_tnh_k_kernel(
         qm_next_raw = load_rows(qm[1], "qm1")
         windows = {c: zero_window(nc.vector, c) for c in range(2)}
         four_gates = tile([P, B * PACK], F32, "four_gates")
-        nc.gpsimd.tensor_scalar(four_gates[:], rw_raw[:], -4.0, 0.0, ALU.mult, ALU.add)
+        nc.gpsimd.tensor_scalar(four_gates[:], rw_raw, -4.0, 0.0, ALU.mult, ALU.add)
         gates = tile([P, B * PACK], F32, "gates")
-        nc.gpsimd.tensor_scalar(gates[:], rw_raw[:], 1.0, 0.0, ALU.mult, ALU.add)
+        nc.gpsimd.tensor_scalar(gates[:], rw_raw, 1.0, 0.0, ALU.mult, ALU.add)
         ones = tile([P, 1], F32, "ones")
         nc.gpsimd.memset(ones[:], 1.0)
-        windows[2] = zero_window(nc.gpsimd, 2, on="rw_raw")
-        qm_mx = {(0, u): mx_tiles(f"qm0{u}", HALF) for u in range(2)}
-        ds_mx = [mx_tiles("ds0", N), mx_tiles("ds1", N)]
+        for c in (2, 3):
+            windows[c] = zero_window(nc.gpsimd, c, on="late_windows", skip=(c - 2) * T * 4)
+        qm_mx = {}
+        qm_mx[0, 0] = mx_tiles("qm00", HALF)
+        ds_mx = {0: mx_tiles("ds0", N)}
 
         keys = gather(k_pool, U32, 0, B * N, "keys")
         k_bytes = gather(k_plane, U8, 0, B * N, "k_bytes")
@@ -256,58 +272,74 @@ def tile_attend_gat_tnh_k_kernel(
         v_bytes = gather(v_plane, U8, 0, B * N, "v_bytes")
         do_mx = mx_tiles("do0", R)
         quantize(do_mx, 0, grouped[:], E5M2)
-        w = [gate(nc.gpsimd, 0, squares(0, 0, q_mx, 0), slope_tile("g00", on="do0g"))]
-        blocks = [group_gpsimd(qm_raw[0][:, :, c * P : (c + 1) * P], f"qm00g{c}") for c in range(2)]
+        values = [gather(v_pool, U32, 0, HALF, "vw00")]
+        squared = squares(0, 0, q_mx, 0)
+        blocks = [tile([P, PACK * P], BF16, "qm00g0")]
+        group(nc.vector, blocks[0], qm_raw[0], 0, P)
+        w = [gate(nc.vector, 0, squared, slope_tile("g00"))]
+        quantize(qm_mx[0, 0], 0, blocks[0][:], E4M3)
+        blocks.append(tile([P, PACK * P], BF16, "qm00g1", on="w00"))
+        group(nc.gpsimd, blocks[1], qm_raw[0][:, :, P:], 0, P)
         w.append(gate(nc.scalar, 0, squares(0, 1, q_mx, 2)))
-        values = [gather(v_pool, U32, h * HALF, HALF, f"vw0{h}") for h in range(2)]
-        banks = [dp_quarters(0, h, do_mx, values[h], 4 + 2 * h) for h in range(2)]
-        form_ds(0, 0, w[0], banks[0])
-        for c in range(2):
-            quantize(qm_mx[0, 0], c * P, blocks[c][:], E4M3)
-        low = stage(nc.scalar, dk_pair(0, 0, 0, 0)[:], "s00")
-        for c in range(2):
-            scatter(nc.scalar, c, 0, low[:, c * HALF : (c + 1) * HALF])
+        form_ds(0, 0, w[0], dp_quarters(0, 0, do_mx, values[0], 4))
+        quantize(qm_mx[0, 0], P, blocks[1][:], E4M3)
+        low = [dk_pair(0, 0, 0, 0)]
 
         grouped = tile([P, PACK * R], BF16, "q1g")
         deal_scalar(grouped, q_next_raw[:, :, :HALF], 0)
         deal_vector(grouped, q_next_raw[:, :, HALF:], HALF)
+        scatter(nc.scalar, 0, 0, stage(nc.scalar, low[0][:, :HALF], "s00", on="q1", skip=6 * KIB)[:])
+        values.append(gather(v_pool, U32, HALF, HALF, "vw01", on="g00"))
+        banks = dp_quarters(0, 1, do_mx, values[1], 6)
         q_mx = mx_tiles("q1", R)
         quantize(q_mx, 0, grouped[:], E4M3)
-        form_ds(0, 1, w[1], banks[1])
-        grouped = tile([P, PACK * R], BF16, "do1g")
+        grouped = tile([P, PACK * R], BF16, "do1g", on="q1", skip=2 * KIB)
         deal_vector(grouped, do_next_raw[:], 0)
         do_mx = mx_tiles("do1", R)
         quantize(do_mx, 0, grouped[:], E5M2)
         values = gather(v_pool, U32, N, N, "vw1", on="do1")
-        grouped = tile([P, PACK * HALF], BF16, "qm01g", on="do1g")
-        group(nc.gpsimd, grouped, qm_raw[1], 0, P)
-        group(nc.vector, grouped, qm_raw[1], P, HALF)
+        ds = form_only(0, 1, w[1], banks, on="do1", skip=2 * KIB)
+        grouped = tile([P, PACK * HALF], BF16, "qm01g", on="q1", skip=3 * KIB)
+        group(nc.gpsimd, grouped, qm_raw[1], 0, HALF)
+        qm_mx[0, 1] = (tile([P, HALF], U32, "qm01_codes"), tile([P, HALF], U8, "qm01_scales"))
+        quantize(ds_mx[0], HALF, ds[:], E5M2)
+        first = stage(nc.vector, low[0][:, HALF:], "s10", on="qm01")
         quantize(qm_mx[0, 1], 0, grouped[:], E4M3)
-        grouped = tile([P, PACK * D], BF16, "qm1g")
-        group(nc.vector, grouped, qm_next_raw, 0, D)
-        qm_next = mx_tiles("qm1", D)
-        quantize(qm_next, 0, grouped[:], E4M3)
-        for u in range(2):
-            qm_mx[1, u] = [part[:, u * HALF : (u + 1) * HALF] for part in qm_next]
-        w = [squares(1, h, q_mx, 2 + 2 * h) for h in range(2)]
-        form_ds(1, 0, gate(nc.vector, 1, w[0]), dp_quarters(1, 0, do_mx, values[:, :HALF], 6))
-        low = stage(nc.scalar, dk_pair(5, 0, 0, 1)[:], "s01")
-        for c in range(2):
-            scatter(nc.scalar, c, HALF, low[:, c * HALF : (c + 1) * HALF])
-        high = [dk_whole(c, 2 + c, 0) for c in range(2)]
-        scatter(nc.scalar, 2, 0, stage(nc.scalar, high[0][:], "s20")[:])
-        form_ds(1, 1, gate(nc.vector, 1, w[1]), dp_quarters(1, 1, do_mx, values[:, HALF:], 2), room=T * 4)
-        windows[3] = zero_window(nc.gpsimd, 3, on="ds11")
-        late = tile([P, B * N], F32, "late", on="w11")
-        leave(nc.vector, late[:, :N], high[1][:])
-        last = {c: dk_whole(4 + i, c, 1) for i, c in enumerate((1, 0, 3, 2))}
-        staged = {c: stage(nc.vector, last[c][:], f"s{c}1x") for c in (1, 0)}
-        scatter(nc.vector, 1, N, staged[1][:])
-        store(1)
-        leave(nc.vector, late[:, N:], last[3][:])
-        staged[2] = stage(nc.vector, last[2][:], "s21x")
-        for c in (0, 2):
-            scatter(nc.scalar, c, N, staged[c][:])
+        scatter(nc.vector, 1, 0, first[:])
+        low.append(dk_pair(1, 0, 0, 1))
+        w = [gate(nc.gpsimd, 1, squares(1, 0, q_mx, 2), slope_tile("g10", on="q1"))]
+        w.append(gate(nc.gpsimd, 1, squares(1, 1, q_mx, 4), slope_tile("g11")))
+        grouped = tile([P, PACK * HALF], BF16, "qm10g", on="w11")
+        group(nc.gpsimd, grouped, qm_next_raw, 0, HALF)
+        scatter(nc.scalar, 0, HALF, stage(nc.scalar, low[1][:, :HALF], "s01", on="q1_codes")[:])
+        scatter(nc.vector, 1, HALF, stage(nc.vector, low[1][:, HALF:], "s11")[:])
+        banks = [dp_quarters(1, h, do_mx, values[:, h * HALF : (h + 1) * HALF], 6 - 4 * h) for h in range(2)]
+        high = [dk_whole(4 + c, 2 + c, 0) for c in range(2)]
+        staged = {2: stage(nc.scalar, high[0][:], "s20")}
+        late = tile([P, B * N], F32, "late")
+        leave(nc.scalar, late[:, :N], high[1][:])
+        scatter(nc.scalar, 2, 0, staged[2][:])
+        scatter(nc.scalar, 3, 0, late[:, :384])
+        ds = [form_only(1, h, w[h], banks[h]) for h in range(2)]
+        qm_mx[1, 0] = (tile([P, HALF], U32, "qm10_codes", on="g11"), tile([P, HALF], U8, "qm10_scales"))
+        ds_mx[1] = (tile([P, N], U32, "ds1_codes", on="g11", skip=N * 4), tile([P, N], U8, "ds1_scales"))
+        quantize(qm_mx[1, 0], 0, grouped[:], E4M3)
+        for h in range(2):
+            quantize(ds_mx[1], h * HALF, ds[h][:], E5M2)
+        grouped = tile([P, PACK * HALF], BF16, "qm11g", on="qm10g")
+        group(nc.vector, grouped, qm_next_raw[:, :, HALF:], 0, HALF)
+        last = {c: dk_whole(6 + i, c, 1) for i, c in enumerate((0, 1))}
+        staged[1] = stage(nc.vector, last[1][:], "s11x")
+        qm_mx[1, 1] = mx_tiles("qm11", HALF)
+        quantize(qm_mx[1, 1], 0, grouped[:], E4M3)
+        for i, c in enumerate((3, 2)):
+            last[c] = dk_whole(i, c, 1)
+        staged[0] = stage(nc.scalar, last[0][:], "s01x")
+        for c, engine in ((0, nc.scalar), (1, nc.vector)):
+            scatter(engine, c, N, staged[c][:])
             store(c)
-        scatter(nc.vector, 3, 0, late[:])
+        leave(nc.vector, late[:, N:], last[3][:])
+        scatter(nc.scalar, 2, N, stage(nc.scalar, last[2][:], "s21x")[:])
+        store(2)
+        scatter(nc.vector, 3, 384, late[:, 384:])
         store(3)

@@ -105,6 +105,10 @@ def tile_attend_gat_tnh_k_kernel(
             dst = grouped[:].rearrange("p (u v m j) -> p u m j v", u=2, v=2, j=PACK)[:, :, x0 // PACK : x0 // PACK + count]
             nc.vector.tensor_copy(dst, raw.rearrange("p j (m u v) -> p u m j v", u=2, v=2))
 
+        def deal_pair(grouped, raw, u):
+            dst = grouped[:].rearrange("p (u v m j) -> p u m j v", u=2, v=2, j=PACK)[:, u]
+            nc.vector.tensor_copy(dst, raw.rearrange("p j (m u v) -> p u m j v", u=2, v=2)[:, u])
+
         def deal_gpsimd(grouped, raw, x0):
             count = raw.shape[2] // PACK
             dst = grouped[:].rearrange("p (t m j) -> p m t j", t=PACK, j=PACK)[:, x0 // PACK : x0 // PACK + count]
@@ -294,14 +298,16 @@ def tile_attend_gat_tnh_k_kernel(
         q_mx = mx_tiles("q1", R)
         quantize(q_mx, 0, grouped[:], E4M3)
         grouped = tile([P, PACK * R], BF16, "do1g", on="q1", skip=2 * KIB)
-        deal_vector(grouped, do_next_raw[:], 0)
+        for u in range(2):
+            deal_pair(grouped, do_next_raw[:], u)
         do_mx = mx_tiles("do1", R)
-        quantize(do_mx, 0, grouped[:], E5M2)
-        values = gather(v_pool, U32, N, N, "vw1", on="do1")
+        for u in range(2):
+            quantize(do_mx, u * HALF, grouped[:, u * PACK * HALF : (u + 1) * PACK * HALF], E5M2)
         ds = form_only(0, 1, w[1], banks, on="do1", skip=2 * KIB)
+        values = gather(v_pool, U32, N, N, "vw1", on="do1")
         grouped = tile([P, PACK * HALF], BF16, "qm01g", on="q1", skip=3 * KIB)
         group(nc.gpsimd, grouped, qm_raw[1], 0, HALF)
-        qm_mx[0, 1] = (tile([P, HALF], U32, "qm01_codes"), tile([P, HALF], U8, "qm01_scales"))
+        qm_mx[0, 1] = mx_tiles("qm01", HALF)
         quantize(ds_mx[0], HALF, ds[:], E5M2)
         first = stage(nc.vector, low[0][:, HALF:], "s10", on="qm01")
         quantize(qm_mx[0, 1], 0, grouped[:], E4M3)
@@ -311,26 +317,27 @@ def tile_attend_gat_tnh_k_kernel(
         w.append(gate(nc.gpsimd, 1, squares(1, 1, q_mx, 4), slope_tile("g11")))
         grouped = tile([P, PACK * HALF], BF16, "qm10g", on="w11")
         group(nc.gpsimd, grouped, qm_next_raw, 0, HALF)
-        scatter(nc.scalar, 0, HALF, stage(nc.scalar, low[1][:, :HALF], "s01", on="q1_codes")[:])
-        scatter(nc.vector, 1, HALF, stage(nc.vector, low[1][:, HALF:], "s11")[:])
-        banks = [dp_quarters(1, h, do_mx, values[:, h * HALF : (h + 1) * HALF], 6 - 4 * h) for h in range(2)]
         high = [dk_whole(4 + c, 2 + c, 0) for c in range(2)]
+        second = stage(nc.scalar, low[1][:], "s01", on="q1_codes")
         staged = {2: stage(nc.scalar, high[0][:], "s20")}
         late = tile([P, B * N], F32, "late")
         leave(nc.scalar, late[:, :N], high[1][:])
+        scatter(nc.vector, 0, HALF, second[:, :HALF])
+        scatter(nc.scalar, 1, HALF, second[:, HALF:])
         scatter(nc.scalar, 2, 0, staged[2][:])
-        scatter(nc.scalar, 3, 0, late[:, :384])
+        scatter(nc.scalar, 3, 0, late[:, :256])
+        banks = [dp_quarters(1, h, do_mx, values[:, h * HALF : (h + 1) * HALF], 6 - 4 * h) for h in range(2)]
         ds = [form_only(1, h, w[h], banks[h]) for h in range(2)]
-        qm_mx[1, 0] = (tile([P, HALF], U32, "qm10_codes", on="g11"), tile([P, HALF], U8, "qm10_scales"))
-        ds_mx[1] = (tile([P, N], U32, "ds1_codes", on="g11", skip=N * 4), tile([P, N], U8, "ds1_scales"))
+        ds_mx[1] = (tile([P, N], U32, "ds1_codes", on="w11", skip=2 * KIB), tile([P, N], U8, "ds1_scales"))
+        qm_mx[1, 0] = mx_tiles("qm10", HALF)
+        quantize(ds_mx[1], 0, ds[0][:], E5M2)
         quantize(qm_mx[1, 0], 0, grouped[:], E4M3)
-        for h in range(2):
-            quantize(ds_mx[1], h * HALF, ds[h][:], E5M2)
-        grouped = tile([P, PACK * HALF], BF16, "qm11g", on="qm10g")
+        quantize(ds_mx[1], HALF, ds[1][:], E5M2)
+        grouped = tile([P, PACK * HALF], BF16, "qm11g", on="g11")
         group(nc.vector, grouped, qm_next_raw[:, :, HALF:], 0, HALF)
-        last = {c: dk_whole(6 + i, c, 1) for i, c in enumerate((0, 1))}
+        last = {c: dk_whole(6 + i, c, 1) for i, c in enumerate((1, 0))}
         staged[1] = stage(nc.vector, last[1][:], "s11x")
-        qm_mx[1, 1] = mx_tiles("qm11", HALF)
+        qm_mx[1, 1] = (tile([P, HALF], U32, "qm11_codes", on="qm10_codes"), tile([P, HALF], U8, "qm11_scales"))
         quantize(qm_mx[1, 1], 0, grouped[:], E4M3)
         for i, c in enumerate((3, 2)):
             last[c] = dk_whole(i, c, 1)
@@ -341,5 +348,5 @@ def tile_attend_gat_tnh_k_kernel(
         leave(nc.vector, late[:, N:], last[3][:])
         scatter(nc.scalar, 2, N, stage(nc.scalar, last[2][:], "s21x")[:])
         store(2)
-        scatter(nc.vector, 3, 384, late[:, 384:])
+        scatter(nc.vector, 3, 256, late[:, 256:])
         store(3)

from contextlib import ExitStack

import concourse.mybir as mybir

B, N, T, D, R = 2, 512, 2048, 512, 512
FLOPS = 3 * 2 * B * N * D * R

F32 = mybir.dt.float32
BF16 = mybir.dt.bfloat16
I32 = mybir.dt.int32
U32 = mybir.dt.uint32
U16 = mybir.dt.uint16
U8 = mybir.dt.uint8
E4M3 = mybir.dt.float8_e4m3fn_x4
E5M2 = mybir.dt.float8_e5m2_x4
ACT = mybir.ActivationFunctionType
ALU = mybir.AluOpType
BYTES_OF = {F32: 4, BF16: 2, I32: 4, U32: 4, U8: 1}

P = 128
PACK = 4
LINE = 4
GROUP = 16
HALF = N // 2
QUARTER = N // 4
KIB = 1024
ALIGN = 64


def tile_attend_gat_tnh_k_kernel(
    tc, qT, k_words, k_scales, v_words, v_scales, doT, rw, qm, offs, out
):
    nc = tc.nc
    with ExitStack() as ctx:
        keep = ctx.enter_context(tc.tile_pool(name="keep", bufs=1))
        placed = ctx.enter_context(tc.tile_pool(name="placed", bufs=1))
        psum = ctx.enter_context(tc.psum_pool(name="psum", bufs=1))
        where = {"end": 0}

        def tile(shape, dtype, name, on=None, skip=0, room=0):
            size = BYTES_OF[dtype]
            for extent in shape[1:]:
                size = size * extent
            if on is None:
                where[name] = where["end"]
                where["end"] = where["end"] + (max(size, room) + ALIGN - 1) // ALIGN * ALIGN
            else:
                where[name] = where[on] + skip
            return placed.tile(shape, dtype, name=name, tag=name, align_bytes=ALIGN, offset=where[name])

        def region(name, size):
            where[name] = where["end"]
            where["end"] = where["end"] + size

        def bank(index, name):
            return psum.tile([P, N], F32, name=name, tag=f"bank{index}")

        def load_rows(src, name, on=None):
            raw = tile([P, PACK, src.shape[1]], F32, name, on)
            nc.sync.dma_start(raw[:], src.rearrange("(p j) w -> p j w", j=PACK))
            return raw

        def zero_plane(engine, name):
            plane = tile([P, T // 4], I32, name)
            engine.memset(plane[:], 0)
            return plane

        def zero_window(engine, c, on=None, skip=0):
            window = tile([P, T], F32, f"win{c}", on, skip)
            engine.memset(window[:], 0.0)
            return window

        def load_scales(plane, src):
            rows = src[0].bitcast(I32)
            for f in range(4):
                nc.sync.dma_start(plane[f:P:32, :], rows[f:16:4, :])

        def load_words(src, name):
            pool_tile = tile([P, T], I32, name)
            nc.sync.dma_start(pool_tile[:], src[0].rearrange("p n j -> p (n j)").bitcast(I32))
            return pool_tile

        def mx_tiles(name, words, room=0):
            return tile([P, words], U32, f"{name}_codes", room=room), tile([P, words], U8, f"{name}_scales")

        def quantize(mx, x0, grouped, fmt):
            cols = slice(x0, x0 + grouped.shape[1] // PACK)
            nc.vector.quantize_mx(out=mx[0][:, cols].bitcast(fmt), scales=mx[1][:, cols], in_=grouped)

        def listed(first, count):
            return offsets[:, first // GROUP : (first + count) // GROUP]

        def gather(pool_tile, dtype, first, count, name, on=None, skip=0):
            got = tile([P, count], dtype, name, on, skip)
            nc.vector.tensor_copy(got[:], pool_tile[:].bitcast(dtype).indirect(listed(first, count)))
            return got

        def deal_scalar(grouped, raw, x0):
            count = raw.shape[2] // PACK
            dst = grouped[:].rearrange("p (t m j) -> p m j t", t=PACK, j=PACK)[:, x0 // PACK : x0 // PACK + count]
            nc.scalar.copy(dst, raw.rearrange("p j (m t) -> p m j t", t=PACK))

        def deal_vector(grouped, raw, x0):
            count = raw.shape[2] // PACK
            dst = grouped[:].rearrange("p (u v m j) -> p u m j v", u=2, v=2, j=PACK)[:, :, x0 // PACK : x0 // PACK + count]
            nc.vector.tensor_copy(dst, raw.rearrange("p j (m u v) -> p u m j v", u=2, v=2))

        def deal_pair(grouped, raw, u):
            dst = grouped[:].rearrange("p (u v m j) -> p u m j v", u=2, v=2, j=PACK)[:, u]
            nc.vector.tensor_copy(dst, raw.rearrange("p j (m u v) -> p u m j v", u=2, v=2)[:, u])

        def deal_gpsimd(grouped, raw, x0):
            count = raw.shape[2] // PACK
            dst = grouped[:].rearrange("p (t m j) -> p m t j", t=PACK, j=PACK)[:, x0 // PACK : x0 // PACK + count]
            nc.gpsimd.tensor_scalar(dst, raw.rearrange("p j (m t) -> p m t j", t=PACK), 1.0, 0.0, ALU.mult, ALU.add)

        def group_gpsimd(raw, name, on=None, skip=0):
            grouped = tile([P, PACK * raw.shape[2]], BF16, name, on, skip)
            dst = grouped[:].rearrange("p (c j) -> p c j", j=PACK)
            nc.gpsimd.tensor_scalar(dst, raw.rearrange("p j c -> p c j"), 1.0, 0.0, ALU.mult, ALU.add)
            return grouped

        def group(engine, grouped, raw, x0, x1):
            dst, src = grouped[:, PACK * x0 : PACK * x1], raw[:, :, x0:x1]
            if engine is nc.vector:
                nc.vector.tensor_copy(dst.rearrange("p (c i j) -> p c j i", i=LINE, j=PACK), src.rearrange("p j (c i) -> p c j i", i=LINE))
            else:
                nc.gpsimd.tensor_scalar(dst.rearrange("p (c j) -> p c j", j=PACK), src.rearrange("p j c -> p c j"), 1.0, 0.0, ALU.mult, ALU.add)

        def product(dst, lhs, lhs_fmt, block, codes, scales, rhs_fmt):
            cols = slice(block * P, (block + 1) * P)
            nc.tensor.matmul_mx(
                out=dst,
                lhsT=lhs[0][:, cols].bitcast(lhs_fmt),
                lhsT_scale=lhs[1][:, cols],
                rhs=codes.bitcast(rhs_fmt),
                rhs_scale=scales,
                start=True,
                stop=True,
            )

        def slope_tile(name, on=None):
            return tile([P, HALF // LINE, PACK, LINE], F32, name, on)

        def squares(b, h, q_mx, first_bank):
            w = slope_tile(f"w{b}{h}")
            cols = slice(b * N + h * HALF, b * N + (h + 1) * HALF)
            for pair in range(2):
                scores = bank(first_bank + pair, f"a{b}{h}{pair}")
                for u in range(2):
                    product(scores[:, u * HALF : (u + 1) * HALF], q_mx, E4M3, 2 * pair + u, keys[:, cols], k_bytes[:, cols], E4M3)
                lines = scores[:].rearrange("p (t c i) -> p c t i", t=2, i=LINE)
                nc.scalar.activation(w[:, :, 2 * pair : 2 * pair + 2, :], lines, ACT.Sigmoid, scale=2.0)
            for pair in range(2):
                part = w[:, :, 2 * pair : 2 * pair + 2, :]
                nc.scalar.activation(part, part, ACT.Square, bias=-0.5)
            return w

        def gate(engine, b, w, dst=None):
            dst = w if dst is None else dst
            for t in range(PACK):
                col = slice(b * PACK + t, b * PACK + t + 1)
                if engine is nc.scalar:
                    nc.scalar.activation(dst[:, :, t, :], w[:, :, t, :], ACT.Identity, scale=four_gates[:, col], bias=gates[:, col])
                else:
                    engine.tensor_scalar(dst[:, :, t, :], w[:, :, t, :], four_gates[:, col], gates[:, col], ALU.mult, ALU.add)
            return dst

        def dp_quarters(b, h, do_mx, v_codes, first_bank):
            banks = [bank(first_bank + u, f"dp{b}{h}{u}") for u in range(2)]
            for u in range(2):
                cols = slice(u * QUARTER, (u + 1) * QUARTER)
                x0 = b * N + h * HALF + u * QUARTER
                for t in range(PACK):
                    product(banks[u][:, t * QUARTER : (t + 1) * QUARTER], do_mx, E5M2, t, v_codes[:, cols], v_bytes[:, x0 : x0 + QUARTER], E4M3)
            return banks

        def form_ds(b, h, w, banks, room=0, on=None):
            ds = tile([P, HALF * PACK], BF16, f"ds{b}{h}", on, room=room)
            for u in range(2):
                nc.vector.tensor_tensor(
                    ds[:, u * N : (u + 1) * N].rearrange("p (c i t) -> p c t i", i=LINE, t=PACK),
                    w[:, u * QUARTER // LINE : (u + 1) * QUARTER // LINE],
                    banks[u][:].rearrange("p (t c i) -> p c t i", t=PACK, i=LINE),
                    ALU.mult,
                )
            for u in range(2):
                quantize(ds_mx[b], h * HALF + u * QUARTER, ds[:, u * N : (u + 1) * N], E5M2)

        def form_only(b, h, w, banks, on=None, skip=0):
            ds = tile([P, HALF * PACK], BF16, f"ds{b}{h}", on, skip)
            for u in range(2):
                nc.vector.tensor_tensor(
                    ds[:, u * N : (u + 1) * N].rearrange("p (c i t) -> p c t i", i=LINE, t=PACK),
                    w[:, u * QUARTER // LINE : (u + 1) * QUARTER // LINE],
                    banks[u][:].rearrange("p (t c i) -> p c t i", t=PACK, i=LINE),
                    ALU.mult,
                )
            return ds

        def dk_pair(index, u, b, h):
            dst = bank(index, f"dk{u}{b}{h}")
            cols = slice(h * HALF, (h + 1) * HALF)
            for c in range(2):
                product(dst[:, c * HALF : (c + 1) * HALF], qm_mx[b, u], E4M3, c, ds_mx[b][0][:, cols], ds_mx[b][1][:, cols], E5M2)
            return dst

        def dk_whole(index, c, b):
            dst = bank(index, f"dk{c}{b}")
            product(dst[:], qm_mx[b, c // 2], E4M3, c % 2, ds_mx[b][0][:], ds_mx[b][1][:], E5M2)
            return dst

        def leave(engine, dst, part):
            if engine is nc.scalar:
                nc.scalar.copy(dst, part)
            else:
                nc.vector.tensor_copy(dst, part)

        def stage(engine, part, name, on=None, skip=0):
            staged = tile([P, part.shape[1]], F32, name, on, skip)
            leave(engine, staged[:], part)
            return staged

        def scatter(engine, c, first, staged):
            if engine is nc.scalar:
                nc.scalar.activation(windows[c][:].indirect(listed(first, staged.shape[1])), staged, ACT.Copy, scale=ones[:])
            else:
                nc.vector.tensor_copy(windows[c][:].indirect(listed(first, staged.shape[1])), staged)

        def store(c):
            nc.sync.dma_start(out[c * P : (c + 1) * P, :], windows[c][:])

        offsets = keep.tile([P, B * N // GROUP], U16, name="offsets")
        nc.sync.dma_start(offsets[:], offs)
        k_plane = zero_plane(nc.vector, "k_plane")
        v_plane = zero_plane(nc.vector, "v_plane")
        k_pool = load_words(k_words, "k_pool")
        region("late_windows", 2 * T * 4)
        rw_wide = tile([P, 2 * ALIGN // 4], F32, "rw_raw", on="late_windows", skip=T * 4 - ALIGN)
        rw_raw = rw_wide[:, : B * PACK]
        nc.sync.dma_start(rw_raw.rearrange("p (b t) -> p b t", b=B), rw.rearrange("b (p t) o -> p b (t o)", t=PACK))
        load_scales(k_plane, k_scales)
        q_raw = [load_rows(qT[0][:, h * HALF : (h + 1) * HALF], f"q0{h}") for h in range(2)]
        do_raw = load_rows(doT[0], "do0")
        load_scales(v_plane, v_scales)
        v_pool = load_words(v_words, "v_pool")
        qm_raw = [load_rows(qm[0][:, :HALF], "qm00")]
        q_next_raw = load_rows(qT[1], "q1")
        do_next_raw = load_rows(doT[1], "do1")
        qm_raw.append(load_rows(qm[0][:, HALF:], "qm01"))
        qm_next_raw = load_rows(qm[1], "qm1")
        windows = {c: zero_window(nc.vector, c) for c in range(2)}
        four_gates = tile([P, B * PACK], F32, "four_gates")
        nc.gpsimd.tensor_scalar(four_gates[:], rw_raw, -4.0, 0.0, ALU.mult, ALU.add)
        gates = tile([P, B * PACK], F32, "gates")
        nc.gpsimd.tensor_scalar(gates[:], rw_raw, 1.0, 0.0, ALU.mult, ALU.add)
        ones = tile([P, 1], F32, "ones")
        nc.gpsimd.memset(ones[:], 1.0)
        for c in (2, 3):
            windows[c] = zero_window(nc.gpsimd, c, on="late_windows", skip=(c - 2) * T * 4)
        qm_mx = {}
        qm_mx[0, 0] = mx_tiles("qm00", HALF)
        ds_mx = {0: mx_tiles("ds0", N)}

        keys = gather(k_pool, U32, 0, B * N, "keys")
        k_bytes = gather(k_plane, U8, 0, B * N, "k_bytes")

        grouped = tile([P, PACK * R], BF16, "q0g")
        for h in range(2):
            deal_scalar(grouped, q_raw[h][:], h * HALF)
        q_mx = mx_tiles("q0", R)
        quantize(q_mx, 0, grouped[:], E4M3)
        grouped = tile([P, PACK * R], BF16, "do0g")
        deal_scalar(grouped, do_raw[:, :, :HALF], 0)
        deal_vector(grouped, do_raw[:, :, HALF:], HALF)
        v_bytes = gather(v_plane, U8, 0, B * N, "v_bytes")
        do_mx = mx_tiles("do0", R)
        quantize(do_mx, 0, grouped[:], E5M2)
        values = [gather(v_pool, U32, 0, HALF, "vw00")]
        squared = squares(0, 0, q_mx, 0)
        blocks = [tile([P, PACK * P], BF16, "qm00g0")]
        group(nc.vector, blocks[0], qm_raw[0], 0, P)
        w = [gate(nc.vector, 0, squared, slope_tile("g00"))]
        quantize(qm_mx[0, 0], 0, blocks[0][:], E4M3)
        blocks.append(tile([P, PACK * P], BF16, "qm00g1", on="w00"))
        group(nc.gpsimd, blocks[1], qm_raw[0][:, :, P:], 0, P)
        w.append(gate(nc.scalar, 0, squares(0, 1, q_mx, 2)))
        form_ds(0, 0, w[0], dp_quarters(0, 0, do_mx, values[0], 4))
        quantize(qm_mx[0, 0], P, blocks[1][:], E4M3)
        low = [dk_pair(0, 0, 0, 0)]

        grouped = tile([P, PACK * R], BF16, "q1g")
        deal_scalar(grouped, q_next_raw[:, :, :HALF], 0)
        deal_vector(grouped, q_next_raw[:, :, HALF:], HALF)
        scatter(nc.scalar, 0, 0, stage(nc.scalar, low[0][:, :HALF], "s00", on="q1", skip=6 * KIB)[:])
        values.append(gather(v_pool, U32, HALF, HALF, "vw01", on="g00"))
        banks = dp_quarters(0, 1, do_mx, values[1], 6)
        q_mx = mx_tiles("q1", R)
        quantize(q_mx, 0, grouped[:], E4M3)
        grouped = tile([P, PACK * R], BF16, "do1g", on="q1", skip=2 * KIB)
        for u in range(2):
            deal_pair(grouped, do_next_raw[:], u)
        do_mx = mx_tiles("do1", R)
        for u in range(2):
            quantize(do_mx, u * HALF, grouped[:, u * PACK * HALF : (u + 1) * PACK * HALF], E5M2)
        ds = form_only(0, 1, w[1], banks, on="do1", skip=2 * KIB)
        values = gather(v_pool, U32, N, N, "vw1", on="do1")
        grouped = tile([P, PACK * HALF], BF16, "qm01g", on="q1", skip=3 * KIB)
        group(nc.gpsimd, grouped, qm_raw[1], 0, HALF)
        qm_mx[0, 1] = mx_tiles("qm01", HALF)
        quantize(ds_mx[0], HALF, ds[:], E5M2)
        first = stage(nc.vector, low[0][:, HALF:], "s10", on="qm01")
        quantize(qm_mx[0, 1], 0, grouped[:], E4M3)
        scatter(nc.vector, 1, 0, first[:])
        low.append(dk_pair(1, 0, 0, 1))
        w = [gate(nc.gpsimd, 1, squares(1, 0, q_mx, 2), slope_tile("g10", on="q1"))]
        w.append(gate(nc.gpsimd, 1, squares(1, 1, q_mx, 4), slope_tile("g11")))
        grouped = tile([P, PACK * HALF], BF16, "qm10g", on="w11")
        group(nc.gpsimd, grouped, qm_next_raw, 0, HALF)
        high = [dk_whole(4 + c, 2 + c, 0) for c in range(2)]
        second = stage(nc.scalar, low[1][:], "s01", on="q1_codes")
        staged = {2: stage(nc.scalar, high[0][:], "s20")}
        late = tile([P, B * N], F32, "late")
        leave(nc.scalar, late[:, :N], high[1][:])
        scatter(nc.vector, 0, HALF, second[:, :HALF])
        scatter(nc.scalar, 1, HALF, second[:, HALF:])
        scatter(nc.scalar, 2, 0, staged[2][:])
        scatter(nc.scalar, 3, 0, late[:, :256])
        banks = [dp_quarters(1, h, do_mx, values[:, h * HALF : (h + 1) * HALF], 6 - 4 * h) for h in range(2)]
        ds = [form_only(1, h, w[h], banks[h]) for h in range(2)]
        ds_mx[1] = (tile([P, N], U32, "ds1_codes", on="w11", skip=2 * KIB), tile([P, N], U8, "ds1_scales"))
        qm_mx[1, 0] = mx_tiles("qm10", HALF)
        quantize(ds_mx[1], 0, ds[0][:], E5M2)
        quantize(qm_mx[1, 0], 0, grouped[:], E4M3)
        quantize(ds_mx[1], HALF, ds[1][:], E5M2)
        grouped = tile([P, PACK * HALF], BF16, "qm11g", on="g11")
        group(nc.vector, grouped, qm_next_raw[:, :, HALF:], 0, HALF)
        last = {c: dk_whole(6 + i, c, 1) for i, c in enumerate((1, 0))}
        staged[1] = stage(nc.vector, last[1][:], "s11x")
        qm_mx[1, 1] = (tile([P, HALF], U32, "qm11_codes", on="qm10_codes"), tile([P, HALF], U8, "qm11_scales"))
        quantize(qm_mx[1, 1], 0, grouped[:], E4M3)
        for i, c in enumerate((3, 2)):
            last[c] = dk_whole(i, c, 1)
        staged[0] = stage(nc.scalar, last[0][:], "s01x")
        for c, engine in ((0, nc.scalar), (1, nc.vector)):
            scatter(engine, c, N, staged[c][:])
            store(c)
        leave(nc.vector, late[:, N:], last[3][:])
        scatter(nc.scalar, 2, N, stage(nc.scalar, last[2][:], "s21x")[:])
        store(2)
        scatter(nc.vector, 3, 256, late[:, 256:])
        store(3)
